import numpy as np, ml_dtypes
CORES = [2,3,42,43,82,83,122,123]
N = 8
BF = ml_dtypes.bfloat16
def gentries(a):
    return np.ascontiguousarray(a.reshape(8, 16, -1).transpose(0, 2, 1)).reshape(8, -1)
def gtable(e):
    e = np.asarray(e); return np.ascontiguousarray(e.reshape(8, -1, 16).transpose(0, 2, 1)).reshape(128, -1).astype(np.int32)
A, W0, B, STEPS, W = 1024, 2048, 192, 6, 2624
def tidy(x):
    return np.asarray(x, np.float32).astype(BF).astype(np.float32)
def sign(rng, m, *shape):
    return (m * (2 * rng.integers(0, 2, shape) - 1)).astype(np.float32)
def num(rng, m, *shape):
    return tidy((np.float32(0.25) + np.float32(0.75) * rng.random(shape, dtype=np.float32)) * sign(rng, m, *shape))
def brink(rng, lo, hi, share, *shape):
    e = np.where(rng.random(shape) < 0.5, lo, hi)
    return np.where(rng.random(shape) < share, e, rng.integers(lo, hi + 1, shape))
def parts(rng):
    d = {"ut": num(rng, 0.5, N, 128, W0), "vt": num(rng, 0.5, N, 128, W0), "bs": num(rng, 1.0, N, 128, A)}
    d["zs"] = num(rng, 1.0, N, 128, B); d["cs"] = num(rng, 0.5, N, 128, B); d["tg"] = num(rng, 1.0, N, 128, B)
    d["ui"] = rng.integers(0, W0, (N, 8, 16, A)); d["vo"] = rng.integers(0, W0, (N, 8, 16, A))
    d["ad"] = rng.integers(0, A, (N, 8, B)); d["nx"] = rng.integers(0, A, (N, 8, 2, A))
    hot = np.argsort(rng.random((N, 8, 16)), axis=2)[..., :2]
    for name in ("sl", "tr"):
        w = np.take_along_axis(hot, rng.integers(0, 2, (N, 8, STEPS * B)), 2)
        d[name] = np.where(rng.random(w.shape) < 0.75, w, rng.integers(0, 16, w.shape)).reshape(N, 8, STEPS, B)
    d["hv"] = rng.integers(6, 12, (N, 8, STEPS, B))
    return d
def pack(d):
    out = {}
    for k in ("ut", "vt"): out[k] = d[k].astype(BF)
    for k in ("ui", "vo"): out[k] = np.ascontiguousarray(d[k].reshape(N, 128, A)).astype(np.int32)
    for k in ("bs", "zs", "cs", "tg"): out[k] = d[k].astype(BF)
    out["ad"] = np.stack([gtable(a) for a in d["ad"]])
    for k in ("nx", "sl", "tr", "hv"): out[k] = np.ascontiguousarray(d[k].reshape(N, 8, -1)).astype(np.int32)
    return out
def setup_inputs(rng):
    return pack(parts(rng))
def setup_inputs_spread(rng):
    d = parts(rng)
    for k in ("ut", "vt", "bs", "zs", "cs", "tg"):
        n = d[k].shape[2]
        d[k] = tidy(d[k] * np.repeat(np.exp2(-rng.integers(0, 3, (N, 8, n)).astype(np.float32)), 16, axis=1))
    lo = (W0 * rng.random((N, 8, 16, A)) ** 2).astype(np.int64); hi = W0 - 1 - (W0 * rng.random((N, 8, 16, A)) ** 2).astype(np.int64)
    m = rng.random((N, 8, 1, A)) < rng.random((N, 8, 1, 1))
    d["ui"] = np.where(m, lo, hi); d["vo"] = np.where(m, hi, lo)
    w = rng.random((N, 8, 16, A)) < 0.4
    d["ui"], d["vo"] = np.where(w, d["vo"], d["ui"]), np.where(w, d["ui"], d["vo"])
    d["ad"] = (A * rng.random((N, 8, B)) ** 2).astype(np.int64); d["nx"] = (A * rng.random((N, 8, 2, A)) ** 1.5).astype(np.int64)
    d["sl"] = (16 * rng.random((N, 8, STEPS, B)) ** 2).astype(np.int64); d["tr"] = (16 * rng.random((N, 8, STEPS, B)) ** 2).astype(np.int64)
    d["hv"] = rng.integers(1, 17, (N, 8, STEPS, B))
    return pack(d)
def setup_inputs_ends(rng):
    d = {"ut": sign(rng, 0.5, N, 128, W0), "vt": sign(rng, 0.5, N, 128, W0), "bs": sign(rng, 1.0, N, 128, A)}
    d["zs"] = sign(rng, 1.0, N, 128, B); d["cs"] = sign(rng, 0.5, N, 128, B); d["tg"] = sign(rng, 1.0, N, 128, B)
    d["ui"] = brink(rng, 0, W0 - 1, 0.7, N, 8, 16, A); d["vo"] = brink(rng, 0, W0 - 1, 0.7, N, 8, 16, A)
    for a in (A - 1, 2): d["ui"][..., a] = W0 - 1; d["vo"][..., a] = 0
    for a in (0, A - 3): d["ui"][..., a] = 0; d["vo"][..., a] = W0 - 1
    d["ui"][..., 1] = W0 - 1; d["vo"][..., 1] = W0 - 1
    d["ad"] = brink(rng, 0, A - 1, 0.65, N, 8, B); d["nx"] = brink(rng, 0, A - 1, 0.65, N, 8, 2, A)
    d["ad"][..., B - 1] = A - 1; d["ad"][..., B - 2] = 2; d["ad"][..., 3] = 1; d["ad"][..., 4] = 0; d["ad"][..., 5] = A - 3
    d["sl"] = 15 * rng.integers(0, 2, (N, 8, STEPS, B)); d["tr"] = 15 * rng.integers(0, 2, (N, 8, STEPS, B))
    d["hv"] = brink(rng, 1, 16, 0.8, N, 8, STEPS, B)
    d["hv"][:, :, 0, B - 1] = 16; d["hv"][:, :, 0, B - 2] = 16; d["hv"][:, :, 0, 3:6] = 1
    for p, s in ((127, 1.0), (126, -1.0), (15, 1.0), (14, -1.0)):
        d["ut"][:, p, W0 - 1] = 0.5; d["vt"][:, p, 0] = 0.5 * s; d["zs"][:, p, B - 2:] = 1.0; d["bs"][:, p, A - 1] = s; d["bs"][:, p, 2] = s
    return pack(d)
def setup_inputs_corners(rng):
    d = parts(rng); q = (0, 1, 2, 3, 8, 14, 15, 16); own = np.arange(A)
    for g in range(8):
        same_ad = rng.permutation(np.arange(1, A - 1))[:B]; same_ad[0] = A - 1; same_ad[B - 1] = 0
        k0, k1 = rng.permutation(16)[:2]; kind = g % 4
        for r in range(N):
            n = q[(g + 3 * r) % 8]
            yes = np.argsort(rng.random((16, A)), axis=0) < n
            lo = rng.integers(0, W0 - 1, (16, A)); hi = lo + 1 + (rng.random((16, A)) * (W0 - 1 - lo)).astype(np.int64)
            hi = np.where(rng.random((16, A)) < 0.3, lo + 1, hi); far = rng.random((16, A)) < 0.1
            lo = np.where(far, 0, lo); hi = np.where(far, W0 - 1, hi); tie = rng.random((16, A)) < 0.3
            d["ui"][r, g] = np.where(yes, hi, lo); d["vo"][r, g] = np.where(yes, lo, np.where(tie, lo, hi))
            d["hv"][r, g] = np.clip(n + rng.integers(0, 2, (STEPS, B)), 1, 16)
            if kind == 0:
                d["nx"][r, g, 0] = rng.permutation(A); d["nx"][r, g, 1] = rng.permutation(A)
                d["sl"][r, g] = 15 * rng.integers(0, 2, (STEPS, B)); d["tr"][r, g] = 15 * rng.integers(0, 2, (STEPS, B))
            elif kind == 2:
                d["nx"][r, g] = np.where(rng.random((2, A)) < 0.6, own[None, :], (A - 1) * rng.integers(0, 2, (2, A)))
            else:
                d["ad"][r, g] = same_ad; d["nx"][r, g, 0] = own; d["nx"][r, g, 1] = own if kind == 1 else own[::-1]
                d["sl"][r, g, :2] = k0; d["sl"][r, g, 2:] = k1; d["tr"][r, g] = k0
    return pack(d)
def setup_inputs_crowd(rng):
    d = parts(rng); own = np.arange(A)
    for g in range(8):
        kind = g % 4; p, w = [int(x) for x in rng.permutation(A)[:2]]; k0, k1 = [int(x) for x in rng.permutation(16)[:2]]; ring = rng.permutation(A)[:B]
        if g == 0: p, w = A - 1, 0
        if g == 1: p, w = 0, A - 1
        for r in range(N):
            if kind < 2:
                d["ad"][r, g] = p; d["nx"][r, g] = own[None, :]
                if kind == 1:
                    d["ad"][r, g, B - 1 if g == 1 else 0] = w
                    d["nx"][r, g, 1, p] = w; d["nx"][r, g, 1, w] = p
                d["sl"][r, g] = k0; d["tr"][r, g] = np.where(rng.random((STEPS, B)) < 0.5, k0, k1); d["tr"][r, g, 2] = k0
                if g == 1:
                    yes = (((np.arange(16) - k0) % 16) >= 1) & (((np.arange(16) - k0) % 16) <= 7)
                    for a in (p, w):
                        lo = rng.integers(0, W0 // 2, 16); hi = rng.integers(W0 // 2, W0, 16)
                        d["ui"][r, g, :, a] = np.where(yes, hi, lo); d["vo"][r, g, :, a] = np.where(yes, lo, hi)
                    d["hv"][r, g, :2] = 16; d["hv"][r, g, 0, B - 2] = 1; d["hv"][r, g, 2, B - 2:] = 8
            elif g == 6:
                lo = rng.integers(0, W0 // 2, (16, A)); hi = lo + rng.integers(1, W0 // 2, (16, A)); yes = ((np.arange(16) - k0) % 16)[:, None] < 8
                d["ui"][r, g] = np.where(yes, hi, lo); d["vo"][r, g] = np.where(yes, lo, hi)
                d["ad"][r, g] = ring; d["nx"][r, g, 0] = own; d["nx"][r, g, 0, ring] = np.roll(ring, -1); d["nx"][r, g, 1] = own[::-1]
                d["sl"][r, g] = k0; d["hv"][r, g, :4] = 16; d["hv"][r, g, 4:] = 8
            elif kind == 2:
                d["ad"][r, g] = np.where(rng.random(B) < 0.5, p, w); d["nx"][r, g, 0] = p; d["nx"][r, g, 1] = w
                for a in (p, w):
                    d["ui"][r, g, :8, a] = W0 - 1; d["vo"][r, g, :8, a] = 0; d["ui"][r, g, 8:, a] = 0; d["vo"][r, g, 8:, a] = W0 - 1
                d["hv"][r, g] = 8 + rng.integers(0, 2, (STEPS, B)); d["sl"][r, g] = rng.choice(np.array([0, 8, 15]), (STEPS, B)); d["tr"][r, g] = rng.choice(np.array([0, 8, 15]), (STEPS, B))
            else:
                m0, n0 = [int(x) for x in np.sort(rng.permutation(W0)[:2])]
                if r == 0: m0, n0 = 0, W0 - 1
                if (r + g // 4) % 2: m0, n0 = n0, m0
                d["ui"][r, g] = n0; d["vo"][r, g] = m0
                o = rng.permutation(A)[:B]; d["ad"][r, g] = o; d["nx"][r, g, 0] = rng.permutation(A); d["nx"][r, g, 1] = rng.permutation(A)
                if g == 7: d["ui"][r, g, :, o[0]] = m0; d["vo"][r, g, :, o[0]] = n0
                d["hv"][r, g] = (15 if n0 > m0 else 1) + rng.integers(0, 2, (STEPS, B))
    return pack(d)
def setup_inputs_brim(rng):
    d = parts(rng); one = int(rng.integers(0, 8))
    for r in range(N):
        for g in range(8):
            full = (g == one) == (r % 2 == 0)
            if full and r % 4 < 2:
                d["ad"][r, g] = int(rng.integers(0, A)); continue
            k = int(rng.integers(0, 16)); m = int(rng.integers(0, W0))
            o = d["vo"][r, g]; o[o == m] = (m + 1) % W0; o[k] = m
            d["ad"][r, g] = rng.permutation(A)[:B]
            w = (k + rng.integers(1, 16, B)) % 16
            if full: w[:] = k
            w[B - 1] = k
            d["tr"][r, g, 0] = w
            if not full:
                nm = rng.permutation(W0); nm = nm[nm != m][:B - 1]
                if g == (one + 4) % 8: nm[1] = nm[0]
                o[w[:B - 1], d["ad"][r, g, :B - 1]] = nm
    return pack(d)
def check_ranges(d):
    bad = []
    for k, lo, hi in (("ui", 0, W0 - 1), ("vo", 0, W0 - 1), ("ad", 0, A - 1), ("nx", 0, A - 1), ("sl", 0, 15), ("tr", 0, 15), ("hv", 1, 16)):
        if np.min(d[k]) < lo or np.max(d[k]) > hi: bad.append("range of " + k)
    for k, lo, hi in (("ut", 2.0 ** -5, 0.5), ("vt", 2.0 ** -5, 0.5), ("cs", 2.0 ** -5, 0.5), ("bs", 2.0 ** -4, 1.0), ("zs", 2.0 ** -4, 1.0), ("tg", 2.0 ** -4, 1.0)):
        v = np.abs(np.asarray(d[k]).astype(np.float64))
        if not np.all((v >= lo) & (v <= hi)): bad.append("range of " + k)
    return bad
def first(key, ok):
    w = np.where(ok, key, -1 - np.arange(B)[None, :]); o = np.argsort(w, axis=1, kind="stable"); s = np.take_along_axis(w, o, 1)
    f = np.ones(s.shape, bool); f[:, 1:] = s[:, 1:] != s[:, :-1]
    m = np.zeros(s.shape, bool); np.put_along_axis(m, o, f, 1)
    return m & ok
def name_at(x, k):
    return np.take_along_axis(x, k[:, None, :], 1)[:, 0]
def vector_at(x, k):
    return np.take_along_axis(x, k[:, None, None, :], 2)[:, :, 0]
def moved(x):
    h = B // 2; w = np.roll(x, 1, axis=0); w[..., h:] = np.roll(x, -1, axis=0)[..., h:]
    return w
def reference(ut, vt, ui, vo, bs, zs, cs, tg, ad, nx, sl, tr, hv):
    U = np.zeros((N, 8, 16, W)); V = np.zeros((N, 8, 16, W))
    U[..., :W0] = ut.astype(np.float64).reshape(N, 8, 16, W0); V[..., :W0] = vt.astype(np.float64).reshape(N, 8, 16, W0)
    I = ui.astype(np.int64).reshape(N, 8, 16, A); O = vo.astype(np.int64).reshape(N, 8, 16, A)
    b = bs.astype(np.float64).reshape(N, 8, 16, A); goal = tg.astype(np.float64).reshape(N, 8, 16, B)
    z = zs.astype(np.float64).reshape(N, 8, 16, B); c = cs.astype(np.float64).reshape(N, 8, 16, B)
    a = np.stack([gentries(x) for x in ad]).astype(np.int64); nxt = nx.astype(np.int64)
    sw, tn, hn = [x.astype(np.int64).reshape(N, 8, STEPS, B) for x in (sl, tr, hv)]
    ys = np.zeros((N, 8, 16, STEPS + 1, B))
    for t in range(STEPS + 1):
        zn, cn, an = np.zeros_like(z), np.zeros_like(c), np.zeros_like(a)
        for r in range(N):
            ai = a[r][:, None, :]
            In = np.take_along_axis(I[r], ai, 2); On = np.take_along_axis(O[r], ai, 2)
            pu = np.take_along_axis(U[r], In.reshape(8, 1, 16 * B), 2).reshape(8, 16, 16, B)
            pv = np.take_along_axis(V[r], On.reshape(8, 1, 16 * B), 2).reshape(8, 16, 16, B)
            y = np.take_along_axis(b[r], ai, 2) + 0.0625 * np.add.reduce(pu * pv, axis=2) * z[r]
            ys[r, :, :, t] = y
            if t == STEPS: continue
            e = y - goal[r]
            votes = np.add.reduce((In > On).astype(np.int64), axis=1)
            an[r] = np.take_along_axis(nxt[r], np.where(votes >= hn[r, :, t], A, 0) + a[r], 1)
            zn[r] = np.clip(y, -1.0, 1.0)
            act = first(a[r], np.ones((8, B), bool))
            if t % 2 == 0: X, Y, P, px, py, Pn, Qn = U, V, I, pu, pv, In, On
            else: X, Y, P, px, py, Pn, Qn = V, U, O, pv, pu, On, In
            k, j = sw[r, :, t], tn[r, :, t]
            xk, yk, xj = vector_at(px, k), vector_at(py, k), vector_at(px, j)
            pj, qj = name_at(Pn, j), name_at(Qn, j)
            go = act
            if t >= 2: go = act & (pj < W0 + B * (t // 2 - 1))
            go = first(qj, go)
            n = W0 + B * (t // 2) + np.arange(B)
            cn[r] = np.where(act[:, None, :], xk, c[r])
            more = 0.0625 * (xk - c[r]) * yk; less = 0.0625 * e * xj * z[r]
            for g in range(8):
                s = np.nonzero(act[g])[0]
                X[r, g][:, n[s]] = c[r, g][:, s]
                P[r, g][k[g, s], a[r, g, s]] = n[s]
                b[r, g][:, a[r, g, s]] += more[g][:, s]
                s = np.nonzero(go[g])[0]
                Y[r, g][:, qj[g, s]] -= less[g][:, s]
        if t < STEPS: z, c, a = moved(zn), moved(cn), moved(an)
    return {"ys": ys.reshape(N, 128, (STEPS + 1) * B).astype(np.float32), "fb": b.reshape(N, 128, A).astype(np.float32), "fc": c.reshape(N, 128, B).astype(np.float32)}

def check_inputs(d):
    bad = list(check_ranges(d))
    if not bad:
        for name, y in reference(**d).items():
            for q in range(N):
                v = np.abs(np.asarray(y[q], np.float64)); s = np.sqrt(np.mean(v * v))
                if v.max() > 3 * s or s < 2.0 ** -4: bad.append('%s of rank %d is uneven or too small' % (name, q))
    return bad

@@ -1,0 +1,662 @@
+import numpy as np
+from concourse.bass import DstId, RemoteDMATransfer
+from concourse.mybir import AluOpType as Op, ActivationFunctionType as Fn
+
+A, W0, B, STEPS = 1024, 2048, 192, 6
+H = B // 2
+CEN = 1408
+NCH, CS = 3, 64
+TW = B + W0 + 3 * B
+EOFF = [sum(B - 16 * q for q in range(m)) for m in range(13)]
+F32, BF, I32, U16, F16 = "float32", "bfloat16", "int32", "uint16", "float16"
+
+
+def _s(n, d):
+    return ("sbuf", [128, n], d)
+
+
+SCRATCH = {
+    "U": _s(TW, F32), "V": _s(TW, F32), "BS": _s(A + B, F32), "IT": _s(A + B, F32), "OT": _s(A + B, F32),
+    "UI": _s(A, I32), "VO": _s(A, I32), "ADI": _s(16, I32), "ADF": _s(16, F32),
+    "RI": _s(216, I32), "RB": _s(360, BF), "R": _s(6 * B, BF),
+    "NXI": _s(128, I32), "NXH": _s(128, BF), "NXL": _s(128, BF), "NXT": _s(A, BF),
+    "ZS": _s(B, BF), "CS": _s(B, BF), "TG": _s(B, BF), "D0": _s(B, F16),
+    "IJ": _s(256, I32), "PI": _s(2, I32), "LI": _s(2, I32), "COL": _s(16, F32), "JL": _s(256, I32), "JH": _s(256, F32),
+    "DG": _s(B, F32), "BO": _s(128, BF), "BOH": _s(128, F16), "WP": _s(144, BF), "WH": _s(144, F16), "WR2": _s(B, BF),
+    "ID": _s(128, F32), "IDN": _s(128, F32), "IN": _s(128, BF), "IB": _s(128, BF), "JN": _s(128, BF),
+    "JP": _s(128, BF), "BOW": _s(12 * 128, BF), "EF": _s(2 * 1248, BF), "RST": _s(16 * CS, BF), "SS": _s(16 * B, F32),
+    "IW": _s(12, F32), "ML": _s(12, U16), "DC": _s(72, F32), "DUM": _s(12, F32), "IW16": _s(144, F32), "IW17": _s(144, F32),
+    "W3": _s(288, BF), "QQ": _s(256, BF), "QI": _s(256, BF), "IR": _s(B, BF), "WROW": _s(B, BF), "THR": _s(B, BF),
+    "WCOL": _s(12, F32), "CHALF": _s(B, BF), "CZERO": _s(B, BF), "C88": _s(B, BF), "CONE": _s(288, BF), "CCEN": _s(36, BF),
+    "LKF": _s(144, F32), "LKJ": _s(144, U16), "NXA": _s(128, I32), "SGN": _s(128, BF), "SGM": _s(128, BF),
+    "BOS": _s(128, F16), "QH": _s(128, BF), "CD": _s(B, BF), "SV": _s(B, BF),
+    "AD": _s(6 * B, BF), "AG": _s(6 * B, BF), "AU": _s(7 * 204, U16), "WF": _s(7 * 48, F32), "NC": _s(2 * 2 * B, F32),
+    "OFFS": _s(7 * 2 * B, U16), "MX": _s(2 * 4 * B, F16), "SG": _s(6 * 36, BF), "LQ": _s(6 * 216, U16),
+    "EA": _s(2 * 1248, BF), "EG": _s(2 * 1248, BF), "SA": _s(3 * B, BF), "SO": _s(3 * B, BF), "KC": _s(2 * B, F32),
+    "LT": _s(48, F32), "L2": _s(6 * 24, U16), "TL": _s(6 * 12, U16),
+    "PY": _s(2 * 16 * B, F32), "PR": _s(16 * B, F32), "YS": _s(7 * B, F32), "ZL": _s(6 * B, F32), "ZC": _s(2 * B, F32),
+    "ZT": _s(B, F32), "CN": _s(6 * B, F32), "FC": _s(B, F32), "BG": _s(2 * B, F32), "XJ": _s(2 * B, F32),
+    "YK": _s(2 * B, F32), "YJ": _s(2 * B, F32), "M1": _s(B, F32), "M2": _s(B, F32), "T1": _s(B, F32), "EE": _s(B, F32),
+}
+for _b in range(8):
+    SCRATCH["P%d" % _b] = ("psum", [128, 512], F32)
+NDMA = 30
+SEMAPHORES = (["ev", "es", "et", "eg", "sent", "outs"] + ["d%d" % i for i in range(NDMA)]
+              + ["m%s%d" % (k, t) for k in "acz" for t in range(1, STEPS + 1)])
+
+T_DMA = 2200.0
+MODEL = (1.04, 0.52, 140.0, 1.56, 3.8, 3500.0)
+OPT = {
+    "MA": 12, "MG": 7,
+    "SCAN": [([64, 64, 64], [])] * 5 + [([64, 64], [64])] * 2,
+    "PEY": False,
+    "PED": False,
+    "CLIP": True,
+    "NA": 6, "NV": 3,
+    "CMP": True,
+    "SPL": False,
+}
+SEED = 0
+ORDER = "ahaiajagafacadaeaoanapabaaaqatbRaraDazakaxaBaAaEaJaCasawaFbSbKaTaUamblalbkbhaVaWaZbcaLcaaHbybMayaGaIbLcbbwbTbBbAbCbzbDbEbFcdccbObmbnbHbGbQbYbZbPbNceaRbVbxcgcfbocochbWbjbiaKbUcIcFbXavbsaPaOcpaNbrctcjckcscucvcDcNcKaQcicJaScLaMcOcHbIcMcGcEcPbqclcwaYeScxcyeJcrcqbubgczbvcQbfbpaXcCeIcRaubJcmcScTcAcUcBdydzcncWdBeLeKeOdsdrePeGeHcVdteQdwducXeXdidfdjdveTeMeRdDdhdAeWdEfidIdHdJdgebdWdTdFdXeaeYdGedeNdxeUdYdVdUdedZdaecdSdKdOeedkbtgDdCdLgHefdRcZdbddeVfjeZdcfkfafecYfbfldMffdldNegfcdmgCgGdnfgdPeheldoftfueidQejdpfdembebbbagEfweweydqekfhesgMfnfmgFeveufvfogNgIfqfrfygPfpexfCfzfxgQgOezfDgJgVfEgRgSgWfFfGgXbdhheqenfYfVgKepeofAfOfWgLfsfUfHgTfXfZgUfRerfQfSetfIfPhifBfTgYiBiDeAeBgafJfKgbiEhjgZhehdhfhkhaeCgchbeDfLeEgdhceFhlhmhthsfMgehvhggfhniJiNiFfNghiGiKggiOhohqiLgiiChpgthuhxhBgqhOgphyhNiHiMiPgriRgugsiViQiUhwgvhCiSiIhDiWjgiThzhQhVgmhrhShPhWgjkFkCjhhYgognjiglhEhFgkhUgwiXhThRhXiYjjhGjchZgxjdhHiZgyhAjagzhIgAjbgBhJkEjejsjrjuiaibjfhKkKkBhMhLkDigicjljkihilidkIkLkAitjnkNjviejmkGifjNjWjTjQimijjMjRjOjtipkOkTkMkPkVjAkUjpiskQjoiqirlfkJkHkRjqjXkSikjVjwjxjPjUjSjBiumCjCinioiikWjzjYjDmzjEjZjFkXlgkYjylclbldlhkZliivjIjHiwmAjGixlaiylrlqjJiziAleltmEmDmBjKjLlsmTkamFmJkbkflkljmSmLmUkgkcllmGmKlulmmMmNmOkdmHmImPkskqnekenfkkknkhlTkmlolnlvlPlMlNlpkjnglRkllWlQkimQmRkrkokplzktlVlwnhkumVlymWnqkvlAlBnpnonnnbnanclSlLmXlUkwkxmYlxkymZkzlOlCndlXnvlHlGlDnslElFlYnrnzlIntlZnwlKlJmamenunAnHnBnInCnxmfnGnimqmhmjmkmbnymmmimlmgmcnKnJnjmnmomrmpmsmdnLmtnQnPnDnlmunkmvnMnmnEnTnRmwnNmxnOmynUnFnZoanSnVofobocnYoeodohogomonojnWnXoloooiokopoqoros"
+ABC = "abcdefghijklmnopqrstuvwxyzABCDEFGHIJKLMNOPQRSTUVWXYZ"
+
+
+def cost(c, m):
+    return c[0] + m[0] * (c[1] + m[3] * c[2] + m[4] * c[3]) + m[1] * c[4]
+
+
+def v(name, a=0, b=None, st=1, p=(0, 128, 1)):
+    if b is None:
+        b = SCRATCH[name][1][1]
+    return ("v", name, a, b, st, p if len(p) == 3 else p + (1,))
+
+
+def ind(win, off):
+    return ("i", win, off)
+
+
+def ext(name, *ix):
+    return ("x", name, ix)
+
+
+def ncol(x):
+    if x[0] == "i":
+        return 16 * ncol(x[2])
+    return (x[3] - x[2] + x[4] - 1) // x[4]
+
+
+def isview(x):
+    return isinstance(x, tuple) and len(x) > 0 and x[0] in ("v", "i", "x")
+
+
+def inps(x):
+    return x[0] == "v" and SCRATCH[x[1]][0] == "psum"
+
+
+def two(x):
+    return x[0] == "v" and SCRATCH[x[1]][2] in (BF, U16, F16)
+
+
+def build(opt):
+    MA, MG, SCAN, PEY, PED, CLIP = [opt[k] for k in ("MA", "MG", "SCAN", "PEY", "PED", "CLIP")]
+    ops = []
+
+    def add(eng, instrs, c, lat=0.0, kind="c", extra_w=(), tag=None, after=()):
+        rd, wr = [], list(extra_w)
+        for (m, a, k) in instrs:
+            vs = [x for x in list(a) + list(k.values()) if isview(x)]
+            for n, x in enumerate(vs):
+                if x[0] == "x":
+                    continue
+                if x[0] == "i":
+                    (wr if n == 0 else rd).append(x[1])
+                    rd.append(x[2])
+                else:
+                    (wr if n == 0 else rd).append(x)
+        if not isinstance(c, tuple):
+            c = (c, 0, 0, 0, 0)
+        ops.append({"e": eng, "i": instrs, "cc": c, "lat": lat, "k": kind, "r": rd, "w": wr, "tag": tag,
+                    "after": list(after), "n": len(ops)})
+        return len(ops) - 1
+
+    def vcost(m, a):
+        o = a[0]
+        if o[0] == "i":
+            return (50, 0, 0, ncol(o), 0)
+        if len(a) > 1 and isview(a[1]) and a[1][0] == "i":
+            return (50, 0, ncol(o), 0, 0)
+        n = ncol(o)
+        if m == "tensor_tensor":
+            n = n if inps(a[1]) or inps(a[2]) else 2 * n
+        elif two(o) and (m == "memset" or two(a[1])):
+            n = n / 2
+        return (30, max(64, n), 0, 0, 0)
+
+    def vec(m, *a):
+        return add("v", [(m, a, {})], vcost(m, a))
+
+    def tt(o, x, y, op):
+        return vec("tensor_tensor", o, x, y, op)
+
+    def ts(o, x, s1, op0, s2=None, op1=None):
+        if op1 is None:
+            return vec("tensor_scalar", o, x, s1, None, op0)
+        return vec("tensor_scalar", o, x, s1, s2, op0, op1)
+
+    def cp(o, x):
+        return vec("tensor_copy", o, x)
+
+    def act(o, x, f=Fn.Identity, **k):
+        c = (70, 0, ncol(o), 0, 0) if x[0] == "i" else (30, max(64, ncol(o)), 0, 0, 0)
+        return add("s", [("activation", (o, x, f), k)], c)
+
+    def mm(lst):
+        c = 0
+        ins = []
+        for n, (o, l, r) in enumerate(lst):
+            c += max(64, ncol(r)) * (4 if SCRATCH[r[1]][2] == F32 else 1)
+            ins.append(("matmul", (o, l, r, n == 0, n == len(lst) - 1), {}))
+        return add("t", ins, (60, 0, 0, 0, c))
+
+    def pick(o, w, src, a, b, p=(0, 128), w0=0):
+        return [(o, v(w, w0 + 15 - l, w0 + 143 - l, p=p), v(src, a + l, b, 16, p=p)) for l in range(16)]
+
+    def dma(q, o, x, t=T_DMA, tag=None, out=False):
+        return add(q, [("dma_start", (o, x), {})], 1000.0 if q == "g" else 80.0, lat=t, kind="o" if out else "d", tag=tag)
+
+    def gp(m, *a, **k):
+        return add("g", [(m, a, k)], (200, 2 * ncol(a[0]), 0, 0, 0))
+
+    def send(kind, t, src, dst):
+        s = add("g", [("send", (("n",), src), {"d": (dst,), "sem": "m%s%d" % (kind, t)})], 900.0, kind="r")
+        ops[s]["r"], ops[s]["w"] = [src], []
+        add("x", [], 0.0, lat=-1.0, kind="a", extra_w=[dst], after=[s], tag="m%s%d" % (kind, t))
+
+    col = lambda j: v("COL", j, j + 1)
+    LANE, PF, GRP, L16, SQ, B1, HB = col(0), col(1), col(2), col(3), col(4), col(5), col(9)
+    P = lambda b, a, c: v("P%d" % b, a, c)
+    sub = lambda x, a, b: v(x[1], x[2] + a, x[2] + b)
+
+    gp("iota", v("PI"), [[0, 2]], 0, 1)
+    gp("iota", v("IJ"), [[1, 256]], 0, 0)
+    dma("y", v("ADI", 0, 12), ext("ad"))
+    dma("y", v("VO"), ext("vo"), 3000.0)
+    dma("y", v("UI"), ext("ui"), 3800.0)
+    dma("y", v("NXI", 0, 64), ext("nx", 0, A))
+    dma("y", v("NXI", 64, 128), ext("nx", A, 2 * A))
+    for n, nm in enumerate(("sl", "tr", "hv")):
+        dma("s", v("RI", 72 * n, 72 * n + 72), ext(nm))
+    dma("g", v("V", B, B + W0), ext("vt"), 4500.0)
+    dma("g", v("U", B, B + W0), ext("ut"), 5000.0)
+    dma("g", v("BS", 0, A), ext("bs"), 4500.0)
+    dma("y", v("CS"), ext("cs"), 4000.0)
+    dma("y", v("ZS"), ext("zs"), 4000.0)
+    dma("y", v("TG"), ext("tg"), 4000.0)
+    vec("memset", v("NXT"), 0.0)
+    vec("memset", v("CHALF"), 0.5)
+    vec("memset", v("CZERO"), 0.0)
+    vec("memset", v("CONE"), 1.0)
+    vec("memset", v("C88"), CEN / 16.0)
+    vec("memset", v("CCEN"), float(CEN))
+    vec("memset", v("WP"), 0.0)
+    vec("memset", v("QI", p=(32, 48)), -1.0)
+    vec("tensor_tensor_scan", v("WROW"), v("CHALF"), v("CZERO"), 2.0 ** 97, Op.mult, Op.add)
+    ts(v("LI"), v("PI"), 15, Op.bitwise_and)
+    cp(LANE, v("LI", 0, 1))
+    cp(PF, v("PI", 0, 1))
+    tt(GRP, PF, LANE, Op.subtract)
+    ts(v("JL", 0, B), v("IJ", 0, B), 15, Op.bitwise_and)
+    tt(v("JH", 0, 128), v("IJ", 0, 128), v("JL", 0, 128), Op.subtract)
+    ts(v("BO"), v("JH", 0, 128), GRP, Op.is_equal)
+    cp(v("BOH"), v("BO"))
+    cp(v("WP", 15, 128, 16), v("BO", 0, 128, 16))
+    cp(v("WH"), v("WP"))
+    ts(v("DG"), v("JL", 0, B), LANE, Op.is_equal)
+    ts(v("ID"), v("IJ", 0, 128), PF, Op.is_equal)
+    cp(v("ML"), v("IJ", 0, 12))
+    ts(v("IW"), v("IJ", 0, B, 16), LANE, Op.add)
+    act(v("IB"), v("ID"))
+    act(v("JN"), v("ID"), scale=-2048.0)
+    act(v("JP"), v("ID"), scale=2048.0)
+    if PEY:
+        act(v("IN"), v("ID"), scale=-1.0)
+    if PED:
+        act(v("IDN"), v("ID"), scale=-1.0)
+    ts(v("THR"), v("DG"), 2.0 ** 99, Op.mult, -2.0 ** 99, Op.add)
+    act(v("WR2"), v("WROW"), scale=-2.5)
+    tt(v("THR"), v("THR"), v("WR2"), Op.add)
+    act(L16, LANE, scale=16.0)
+    act(SQ, LANE, Fn.Square)
+    act(B1, SQ, scale=-1.0, bias=1.0)
+    for m in range(3):
+        act(col(6 + m), SQ, scale=-4096.0, bias=float(W0 + B * m - CEN))
+        act(v("DC", 24 * m, 24 * m + 12), v("IW"), bias=float(A + 14 * 2048))
+        act(v("DC", 24 * m + 12, 24 * m + 24), v("IW"), bias=float(W0 + B * m + 14 * 2048))
+    act(v("DUM"), v("IW"), bias=float(32768 - B))
+    ts(v("IR"), v("IJ", 0, B), 2.0 ** -16, Op.mult)
+    gp("iota", v("QI", p=(0, 32)), [[0, 16], [2, 16]], 0, 0, allow_small_or_imprecise_dtypes=True)
+    gp("affine_select", v("QQ", p=(0, 32)), v("QI", p=(0, 32)), [[-1, 16], [0, 16]], Op.is_equal, 0.0, 0, 1)
+    gp("affine_select", v("QQ", p=(32, 48)), v("QI", p=(32, 48)), [[-1, 16], [0, 16]], Op.is_equal, 0.0, 0, 1)
+    gp("affine_select", v("W3", p=(0, 32)), v("CONE", p=(0, 32)), [[128, 2], [1, 144]], Op.is_equal, 0.0, -15, -16)
+    gp("iota", v("IW16"), [[0, 12], [256, 12]], 0, 0, allow_small_or_imprecise_dtypes=True)
+    act(v("IW17"), v("IW16"), bias=L16)
+    mm(pick(P(7, 0, 12), "WP", "WROW", 0, B))
+    act(v("WCOL"), P(7, 0, 12), scale=0.0625)
+    for m in range(min(MA, MG), 12):
+        act(v("BOW", 128 * m, 128 * m + 128), v("BO"), scale=v("WCOL", m, m + 1))
+    rw = max([B] + [16 * w for x in SCAN for w in x[1]])
+    vec("memset", v("RST", 0, rw), 1.0)
+    vec("memset", v("RST", 0, rw, 16), 0.0)
+    ts(v("OT", 0, A), v("VO"), -float(CEN), Op.add)
+    ts(v("IT", 0, A), v("UI"), -float(CEN), Op.add)
+    cp(v("RB", 0, 216), v("RI"))
+    act(v("RB", 216, 360), v("RB", 0, 144), Fn.Square)
+    for n, q in enumerate((0, 1, 2, 2, 3, 4)):
+        dma("s" if n % 2 else "y", v("R", p=(8 * n, 8 * n + 8)), v("RB", 72 * q, 72 * q + 72))
+    for q in range(2):
+        mm(pick(P(6, 72 * q, 72 * q + 72), "W3", "R", 0, 6 * B, p=(0, 16), w0=144 * q))
+    tt(v("LKF"), P(6, 0, 144), v("IW17"), Op.add)
+    cp(v("LKJ"), v("LKF"))
+    ts(v("NXA"), v("NXI"), 31, Op.bitwise_and)
+    cp(v("NXL"), v("NXA"))
+    tt(v("NXH"), v("NXI"), v("NXA"), Op.subtract)
+    for n in range(4):
+        dma("s" if n % 2 else "y", v("NXT", p=(n, 128, 16)), v("NXL" if n % 2 else "NXH", 64 * (n // 2), 64 * (n // 2) + 64), tag="nx")
+    vec("memset", v("SGN"), -1.0)
+    vec("memset", v("SGN", 0, 128, 16), 1.0)
+    vec("memset", v("SGN", 1, 128, 16), 1.0)
+    tt(v("BOS"), v("BO"), v("SGN"), Op.mult)
+    act(v("SGM", p=(0, 32)), v("SGN", p=(0, 32)), scale=-1.0)
+    gp("affine_select", v("QH", p=(0, 32)), v("SGM", p=(0, 32)), [[-1, 8], [0, 16]], Op.is_equal, 0.0, -16, 1)
+    ts(HB, LANE, 2.0, Op.is_ge, 0.5, Op.subtract)
+    act(v("U", B + W0, 2 * B + W0), v("CS"))
+    if not PEY:
+        act(P(1, 0, B), v("TG"))
+    cp(v("ADF", 0, 12), v("ADI", 0, 12))
+    tt(v("D0"), ind(v("ADF", 0, 12), v("ML")), v("DG"), Op.mult)
+
+    def first(E, t, rep, prep, key, bank, sg, ms):
+        e0 = 1248 * (t % 2)
+        f0 = 1248 * (bank - 6)
+        for m in range(12):
+            kc = v("WF", key + m, key + m + 1)
+            if m < ms:
+                ts(v(E, e0 + EOFF[m], e0 + EOFF[m + 1]), v(rep[0], rep[1] + 16 * m, rep[1] + B), kc,
+                   Op.is_equal, v("WCOL", m, m + 1), Op.mult)
+            else:
+                act(v("EF", f0 + EOFF[m], f0 + EOFF[m + 1]), P(prep[0], prep[1] + 16 * m, prep[1] + B), Fn.Abs,
+                    scale=-1.0, bias=kc)
+        if ms < 12:
+            act(v(E, e0 + EOFF[ms], e0 + 1248), v("EF", f0 + EOFF[ms], f0 + 1248), Fn.Relu, scale=-1.0, bias=1.0)
+        mm([(P(bank, 0, B), v("IB"), v("THR"))]
+           + [(P(bank, 16 * m, B), v("BO") if m < ms else v("BOW", 128 * m, 128 * m + 128),
+               v(E, e0 + EOFF[m], e0 + EOFF[m + 1])) for m in range(12)])
+        act(v(sg, 0, B), P(bank, 0, B), Fn.Sign)
+        o = B + B * (t % 2)
+        vec("tensor_tensor_scan", v(sg, o, o + B), v("RST", 0, B), v(sg, 0, B), 0.0, Op.mult, Op.add)
+        return v(sg, o + 15, o + B, 16)
+
+    def ints(t):
+        last = t == STEPS
+        au, wf, nc, of = 204 * t, 48 * t, 2 * B * (t % 2), 2 * B * t
+        src, a0, bo, wp = ("D0", 0, "BOH", "WH") if t == 0 else ("AD", B * (t - 1), "BO", "WP")
+        mm(pick(P(4, B, B + 12), wp, src, a0, a0 + B))
+        if last:
+            cp(v("AU", au + B, au + 204), P(4, B, B + 12))
+        else:
+            if opt["SPL"]:
+                cp(v("AU", au + B, au + 204), P(4, B, B + 12))
+            mm([(P(4, 0, B), v(bo), v(src, a0, a0 + B))])
+            cp(v("AU", au, au + (B if opt["SPL"] else 204)), P(4, 0, B if opt["SPL"] else 204))
+            act(v("WF", wf, wf + 12), P(4, B, B + 12))
+        al = v("AU", au + B, au + 204)
+        PT, QT = ("IT", "OT") if t % 2 == 0 else ("OT", "IT")
+        pc, qc = v("NC", nc, nc + B), v("NC", nc + B, nc + 2 * B)
+        act(qc, ind(v(QT, 0, A), al))
+        act(pc, ind(v(PT, 0, A), al))
+        ts(v("OFFS", of, of + 2 * B), v("NC", nc, nc + 2 * B), float(CEN), Op.add)
+        if last:
+            return
+        mx, sg, lq = 4 * B * (t % 2), 36 * t, 216 * t
+        rt = v("R", B * t, B * t + B, p=(0, 48))
+        mm([(P(3, 0, B), v("QQ", 0, 128, p=(0, 48)), rt)])
+        mm([(P(3, B, 2 * B), v("QQ", 128, 256, p=(0, 48)), rt)])
+        act(P(3, 0, 2 * B), P(3, 0, 2 * B), Fn.Relu, bias=B1)
+        mm([(P(7, 216, 216 + B), v("QQ", 0, 128, p=(0, 48)), rt), (P(7, 216, 216 + B), v("BO"), v("IR"))])
+        kc = v("KC", B * (t % 2), B * (t % 2) + B)
+        act(kc, P(7, 216, 216 + B), scale=4096.0, bias=col(6 + t // 2))
+        if opt["CMP"]:
+            act(P(2, B, 2 * B), qc)
+        tt(v("MX", mx, mx + B), pc, P(2, B, 2 * B) if opt["CMP"] else qc, Op.is_gt if t % 2 == 0 else Op.is_lt)
+        tt(v("MX", mx + B, mx + 3 * B), v("NC", nc, nc + 2 * B), P(3, 0, 2 * B), Op.mult)
+        tt(v("MX", mx + 3 * B, mx + 4 * B), pc, P(3, B, 2 * B), Op.mult)
+        act(v("CD"), ind(v("NXT"), al))
+        mm([(P(5, 228, 228 + B), v("BOS"), v("MX", mx, mx + B)),
+            (P(5, 228, 228 + B), v("QH", p=(0, 24)), v("R", B * t, B * t + B, p=(0, 24)))])
+        act(v("SV"), P(5, 228, 228 + B), Fn.Sign, scale=-1.0, bias=HB)
+        mm([(P(4, 204, 204 + B), v("IB"), v("CD")), (P(4, 204, 204 + B), v("JP"), v("SV"))])
+        act(v("AG", B * t, B * t + B), P(4, 204, 204 + B), Fn.Relu, bias=-2048.0)
+        send("a", t + 1, v("AG", B * t, B * t + B), v("AD", B * t, B * t + B))
+        mm(pick(P(5, 0, 36), "WH", "MX", mx + B, mx + 4 * B) + [(P(5, 0, 36), v("IB"), v("CCEN"))])
+        mm([(P(5, 36, 36 + B), v("BOH"), v("MX", mx + 2 * B, mx + 3 * B)), (P(5, 36, 36 + B), v("BO"), v("C88"))])
+        cp(v("LQ", lq, lq + 204), P(5, 24, 228))
+        act(v("WF", wf + 12, wf + 36), P(5, 0, 24))
+        if t >= 2:
+            act(v("SG", sg + 12, sg + 24), P(5, 24, 36), Fn.Sign, bias=0.5 - (W0 + B * (t // 2 - 1)))
+        nb = first("EA", t, ("AU", au), (4, 0), wf, 6, "SA", MA)
+        dc = 24 * (t // 2)
+        mm([(P(6, 204, 228), v("ID"), v("DC", dc, dc + 24)), (P(6, 204, 216), v("JP"), nb), (P(6, 216, 228), v("JP"), nb)])
+        tt(v("LT", 0, 24), P(6, 204, 228), v("WF", wf, wf + 24), Op.max)
+        cp(v("L2", 24 * t, 24 * t + 24), v("LT", 0, 24))
+        tt(ind(v(PT), v("L2", 24 * t, 24 * t + 12)), pc, kc, Op.max)
+        lst = [(P(7, B, B + 12), v("ID"), v("WF", wf + 24, wf + 36)), (P(7, B, B + 12), v("JN"), nb)]
+        if t >= 2:
+            lst.append((P(7, B, B + 12), v("JN"), v("SG", sg + 12, sg + 24)))
+        mm(lst)
+        act(v("WF", wf + 36, wf + 48), P(7, B, B + 12), bias=-34816.0 if t >= 2 else -32768.0)
+        ng = first("EG", t, ("LQ", lq + 12), (5, 36), wf + 36, 7, "SO", MG)
+        mm([(P(7, 204, 216), v("ID"), v("WF", wf + 36, wf + 48)), (P(7, 204, 216), v("JN"), ng)])
+        tt(v("LT", 24, 36), P(7, 204, 216), v("DUM"), Op.max)
+        ts(v("TL", 12 * t, 12 * t + 12), v("LT", 24, 36), float(B - 32768), Op.add)
+
+    def floats(t):
+        last = t == STEPS
+        X, Y = ("U", "V") if t % 2 == 0 else ("V", "U")
+        ex = B + W0 + B * (t // 2)
+        ey = B + W0 + B * ((t + 1) // 2)
+        of, py, h2 = 2 * B * t, 16 * B * (t % 2), B * (t % 2)
+        al = v("AU", 204 * t + B, 204 * t + 204)
+        w = B // opt["NA"]
+        for c in range(0, B, w):
+            act(v("PY", py + 16 * c, py + 16 * (c + w)), ind(v(Y, B, ey), v("OFFS", of + B + c, of + B + c + w)), scale=0.0625)
+        d = 0
+        for w in SCAN[t][0] + SCAN[t][1]:
+            a, b = 16 * d, 16 * (d + w)
+            tt(v("PR", a, b), ind(v(X, B, ex), v("OFFS", of + d, of + d + w)), v("PY", py + a, py + b), Op.mult)
+            if d >= sum(SCAN[t][0]):
+                s0 = a - 16 * sum(SCAN[t][0])
+                vec("tensor_tensor_scan", v("SS", s0, s0 + 16 * w), v("RST", 0, 16 * w), v("PR", a, b), 0.0, Op.mult, Op.add)
+            else:
+                mm([(P(0, d, d + w), v("ID"), v("PR", a + k, b, 16)) for k in range(16)])
+            d += w
+        bg = v("BG", h2, h2 + B)
+        act(bg, ind(v("BS", 0, A), al))
+        if t == 0:
+            z = v("ZS")
+        else:
+            z = v("ZC", h2, h2 + B)
+            if CLIP:
+                act(v("ZT"), v("ZL", B * (t - 1), B * t), Fn.Relu, bias=1.0)
+                act(v("ZT"), v("ZT"), Fn.Relu, scale=-1.0, bias=2.0)
+                act(z, v("ZT"), scale=-1.0, bias=1.0)
+            else:
+                ts(z, v("ZL", B * (t - 1), B * t), -1.0, Op.max, 1.0, Op.min)
+        y, tmp = v("YS", B * t, B * t + B), P(1, B, 2 * B)
+        if not last:
+            xj, yk, yj = v("XJ", h2, h2 + B), v("YK", h2, h2 + B), v("YJ", h2, h2 + B)
+            cn = v("CN", B * t, B * t + B)
+            act(cn, ind(v(X, B, ex + B), v("L2", 24 * t + 12, 24 * t + 24)))
+            send("c", t + 1, cn, v("FC") if t + 1 == STEPS else v(Y, ey, ey + B))
+            act(xj, ind(v(X, B, ex), v("LQ", 216 * t, 216 * t + 12)), scale=0.0625)
+            pw = v("PY", py, py + 16 * B)
+            act(yj, ind(pw, v("LKJ", 72 + 12 * t, 84 + 12 * t)), scale=16.0)
+            act(yk, ind(pw, v("LKJ", 12 * t, 12 * t + 12)))
+        cut = sum(SCAN[t][0])
+        pey = PEY and not last
+        t1 = v("T1") if pey else tmp
+        if cut > 0:
+            tt(sub(t1, 0, cut), P(0, 0, cut), sub(z, 0, cut), Op.mult)
+        if cut < B:
+            tt(sub(t1, cut, B), v("SS", 15, 16 * (B - cut), 16), sub(z, cut, B), Op.mult)
+        if last:
+            tt(y, tmp, bg, Op.add)
+            dma("y", ext("ys", B * t, B * t + B), y, out=True)
+            return
+        if pey:
+            mm([(P(1, B, 2 * B), v("ID"), bg), (P(1, B, 2 * B), v("IN"), v("TG"))])
+            act(P(1, 0, B), xj)
+            tt(P(1, 0, B), P(1, 0, B), z, Op.mult)
+            tt(v("EE"), t1, P(1, B, 2 * B), Op.add)
+            tt(v("M1"), v("EE"), P(1, 0, B), Op.mult)
+            mm([(P(0, B, 2 * B), v("ID"), v("EE")), (P(0, B, 2 * B), v("IB"), v("TG"))])
+            act(y, P(0, B, 2 * B))
+        else:
+            tt(y, tmp, bg, Op.add)
+            tt(tmp, y, P(1, 0, B), Op.subtract)
+            tt(tmp, tmp, z, Op.mult)
+            tt(v("M1"), tmp, xj, Op.mult)
+        dma("y", ext("ys", B * t, B * t + B), y, out=True)
+        send("z", t + 1, y, v("ZL", B * t, B * t + B))
+        tt(ind(v(Y, 0, ey), v("TL", 12 * t, 12 * t + 12)), yj, v("M1"), Op.subtract)
+        if PED:
+            mm([(P(2, 0, B), v("ID"), cn), (P(2, 0, B), v("IDN"), v(X, ex, ex + B))])
+        else:
+            act(P(2, 0, B), cn)
+            tt(P(2, 0, B), P(2, 0, B), v(X, ex, ex + B), Op.subtract)
+        tt(v("M2"), P(2, 0, B), yk, Op.mult)
+        tt(ind(v("BS"), v("L2", 24 * t, 24 * t + 12)), bg, v("M2"), Op.add)
+        if t == STEPS - 1:
+            dma("y", ext("fb"), v("BS", 0, A), 3000.0, out=True)
+            dma("y", ext("fc"), v("FC"), out=True)
+
+    ints(0)
+    for t in range(STEPS + 1):
+        if t < STEPS:
+            ints(t + 1)
+        floats(t)
+    return ops
+
+
+def overlap(x, y):
+    return x[1] == y[1] and x[2] < y[3] and y[2] < x[3] and x[5][0] < y[5][1] and y[5][0] < x[5][1]
+
+
+def schedule(seed=SEED, opt=OPT, mod=MODEL, text=ORDER):
+    ops = build(opt)
+    n = len(ops)
+    fixed = [52 * ABC.index(text[i]) + ABC.index(text[i + 1]) for i in range(0, len(text), 2)]
+    assert len(fixed) in (0, n)
+    rng = np.random.RandomState(seed)
+    LAT = mod[2]
+    noise, look = (0.0, 100.0) if seed == 0 else (rng.choice([300.0, 1000.0, 3000.0]), rng.choice([50.0, 150.0, 300.0, 600.0]))
+    hist = {}
+    for o in ops:
+        o["c"] = cost(o["cc"], mod)
+        if o["k"] == "a":
+            o["lat"] = mod[5]
+        d = set(o["after"])
+        for x in o["r"]:
+            for (j, y, w) in hist.get(x[1], ()):
+                if w and overlap(x, y):
+                    d.add(j)
+        for x in o["w"]:
+            for (j, y, w) in hist.get(x[1], ()):
+                if overlap(x, y) and not (w and o["tag"] == "nx" and ops[j]["tag"] == "nx"):
+                    d.add(j)
+        d.discard(o["n"])
+        o["d"] = d
+        o["banks"] = set(x[1] for x in o["r"] + o["w"] if inps(x))
+        for x in o["r"]:
+            hist.setdefault(x[1], []).append((o["n"], x, False))
+        for x in o["w"]:
+            hist.setdefault(x[1], []).append((o["n"], x, True))
+    succ = [[] for _ in range(n)]
+    for o in ops:
+        for j in o["d"]:
+            succ[j].append(o["n"])
+    prio = [0.0] * n
+    for o in reversed(ops):
+        prio[o["n"]] = o["c"] + o["lat"] + LAT + max([prio[s] for s in succ[o["n"]]] + [0.0])
+    prio = [p + noise * rng.rand() for p in prio]
+    left = [len(o["d"]) for o in ops]
+    ready = {j: 0.0 for j in range(n) if left[j] == 0}
+    fin = [0.0] * n
+    free = {}
+    bank = {}
+    order = []
+    lastg = []
+    while ready:
+        est = {}
+        for j in ready:
+            o = ops[j]
+            s = max(free.get(o["e"], 0.0), ready[j])
+            for b in o["banks"]:
+                for e, i in bank.get(b, {}).items():
+                    if e != o["e"]:
+                        s = max(s, fin[i] + LAT)
+            est[j] = s
+        j0 = min(ready, key=lambda j: (est[j], -prio[j]))
+        e0 = ops[j0]["e"]
+        if fixed:
+            j = fixed[len(order)]
+        else:
+            j = max((j for j in ready if ops[j]["e"] == e0 and est[j] <= est[j0] + look), key=lambda j: (prio[j], -j))
+        o = ops[j]
+        for b in o["banks"]:
+            for e, i in bank.get(b, {}).items():
+                if e != o["e"]:
+                    o["d"].add(i)
+            bank.setdefault(b, {})[o["e"]] = j
+        if o["e"] == "g" and o["k"] == "c":
+            o["d"].update(lastg)
+            lastg[:] = [j]
+        o["t0"] = est[j]
+        if o["e"] != "x":
+            free[o["e"]] = est[j] + o["c"]
+        fin[j] = est[j] + o["c"] + o["lat"]
+        del ready[j]
+        order.append(j)
+        for s in succ[j]:
+            left[s] -= 1
+            if left[s] == 0:
+                ready[s] = max(fin[i] + LAT for i in ops[s]["d"])
+    cnt = {}
+    nd = 0
+    for j in order:
+        o = ops[j]
+        if o["k"] == "c":
+            s = "e" + o["e"]
+            cnt[s] = cnt.get(s, 0) + 1
+            o["sig"] = (s, cnt[s])
+        elif o["k"] == "d":
+            o["sig"] = ("d%d" % nd, 16)
+            nd += 1
+        elif o["k"] == "a":
+            o["sig"] = (o["tag"], -1)
+        else:
+            o["sig"] = None
+    pos = {j: i for i, j in enumerate(order)}
+    known = {}
+    for j in order:
+        o = ops[j]
+        if o["k"] == "a":
+            o["clock"] = {}
+            continue
+        kn = known.setdefault(o["e"], {})
+        o["waits"] = []
+        for i in sorted(o["d"], key=lambda i: -pos[i]):
+            s, c = ops[i]["sig"]
+            if s in kn and kn[s] >= c:
+                continue
+            o["waits"].append((s, c))
+            kn[s] = c
+            for s2, c2 in ops[i]["clock"].items():
+                if kn.get(s2, -2) < c2:
+                    kn[s2] = c2
+        o["clock"] = dict(kn)
+    need = {}
+    for j in order:
+        for (s, c) in ops[j].get("waits", ()):
+            if s[0] == "e":
+                need.setdefault(s, set()).add(c)
+    renum = {s: {c: i + 1 for i, c in enumerate(sorted(cs))} for s, cs in need.items()}
+    for j in order:
+        o = ops[j]
+        if o["k"] == "a":
+            continue
+        o["waits"] = [(s, renum[s][c]) if s[0] == "e" else (s, c) for (s, c) in o["waits"]]
+        if o["k"] == "c":
+            s, c = o["sig"]
+            o["inc"] = s if c in renum.get(s, {}) else None
+    return ops, order, max(fin)
+
+
+PLAN = []
+
+
+def masks(topo, core, nxt, prv):
+    a, b = topo.engines(core, nxt), topo.engines(core, prv)
+    k = min(len(a), len(b), len(set(a) | set(b)) // 2)
+    if len(a) <= len(b):
+        ea = a[:k]
+        eb = [e for e in reversed(b) if e not in ea][:k]
+    else:
+        eb = b[:k]
+        ea = [e for e in reversed(a) if e not in eb][:k]
+    return sum(1 << e for e in ea), sum(1 << e for e in eb), k
+
+
+def rank_program(g, core, T, topo):
+    rank = T.rank_of(core)
+    if rank is None:
+        return
+    if not PLAN:
+        PLAN.append(schedule())
+    ops, order, _ = PLAN[0]
+    cores = list(T.cores)
+    N = len(cores)
+    nxt, prv = cores[(rank + 1) % N], cores[(rank - 1) % N]
+    mn, mp, k = masks(topo, core, nxt, prv)
+    arrive = masks(topo, prv, core, cores[(rank - 2) % N])[2] + masks(topo, nxt, cores[(rank + 2) % N], core)[2]
+    idn, idp = [DstId(rid=topo.addr(c)[0], pnc=topo.addr(c)[1]) for c in (nxt, prv)]
+    Q = {"v": g.vector, "s": g.scalar, "t": g.tensor, "g": g, "y": g.sync}
+
+    def ap(x):
+        if not isview(x):
+            return x
+        if x[0] == "i":
+            return ap(x[1]).indirect(ap(x[2]))
+        if x[0] == "x":
+            return T[x[1]][:, x[2][0]:x[2][1]] if x[2] else T[x[1]][:]
+        p = x[5]
+        ps = slice(p[0], p[1]) if p[2] == 1 else slice(p[0], p[1], p[2])
+        return T[x[1]][ps, x[2]:x[3]] if x[4] == 1 else T[x[1]][ps, x[2]:x[3]:x[4]]
+
+    def half(x, h):
+        return ap(v(x[1], x[2] + h * H, x[2] + h * H + H))
+
+    calls = {
+        "matmul": lambda q: q.matmul, "activation": lambda q: q.activation, "dma_start": lambda q: q.dma_start,
+        "tensor_tensor": lambda q: q.tensor_tensor, "tensor_scalar": lambda q: q.tensor_scalar,
+        "tensor_copy": lambda q: q.tensor_copy, "memset": lambda q: q.memset, "iota": lambda q: q.iota,
+        "tensor_tensor_scan": lambda q: q.tensor_tensor_scan, "affine_select": lambda q: q.affine_select,
+    }
+    sent = outs = 0
+    for j in order:
+        o = ops[j]
+        if o["k"] == "a":
+            continue
+        q = Q[o["e"]]
+        for (s, c) in o["waits"]:
+            q.wait_ge(T.sem[s], arrive if c < 0 else c)
+        if o["k"] == "r":
+            _, a, kw = o["i"][0]
+            src, dst, sem = a[1], kw["d"][0], T.sem[kw["sem"]]
+            g.remote_dma_fused([
+                RemoteDMATransfer(dst_ids=[idn], dma_engine_mask=mn, remote_sem=sem, src=half(src, 0), dst=half(dst, 0)),
+                RemoteDMATransfer(dst_ids=[idp], dma_engine_mask=mp, remote_sem=sem, src=half(src, 1), dst=half(dst, 1)),
+            ], local_sem=T.sem.sent)
+            sent += 2 * k
+            continue
+        for (m, a, kw) in o["i"]:
+            ins = calls[m](q)(*[ap(x) for x in a], **{n: ap(x) for n, x in kw.items()})
+        if o["k"] == "c":
+            if o["inc"]:
+                ins.then_inc(T.sem[o["inc"]], 1)
+        elif o["k"] == "d":
+            ins.then_inc(T.sem[o["sig"][0]], 16)
+        else:
+            ins.then_inc(T.sem.outs, 16)
+            outs += 16
+    g.wait_ge(T.sem.sent, sent)
+    g.sync.wait_ge(T.sem.outs, outs)

@@ -1,13 +1,15 @@
 import numpy as np
 from concourse.bass import DstId, RemoteDMATransfer
-from concourse.mybir import AluOpType as Op, ActivationFunctionType as Fn
+from concourse.mybir import AluOpType as Op, ActivationFunctionType as Fn, AxisListType as Ax
 
 A, W0, B, STEPS = 1024, 2048, 192, 6
 H = B // 2
 CEN = 1408
-NCH, CS = 3, 64
+SUM0 = 16 * CEN
+BIG = 3072.0
 TW = B + W0 + 3 * B
 EOFF = [sum(B - 16 * q for q in range(m)) for m in range(13)]
+NE = EOFF[12]
 F32, BF, I32, U16, F16 = "float32", "bfloat16", "int32", "uint16", "float16"
 
 
@@ -17,52 +19,45 @@ def _s(n, d):
 
 SCRATCH = {
     "U": _s(TW, F32), "V": _s(TW, F32), "BS": _s(A + B, F32), "IT": _s(A + B, F32), "OT": _s(A + B, F32),
-    "UI": _s(A, I32), "VO": _s(A, I32), "ADI": _s(16, I32), "ADF": _s(16, F32),
-    "RI": _s(216, I32), "RB": _s(360, BF), "R": _s(6 * B, BF),
-    "NXI": _s(128, I32), "NXH": _s(128, BF), "NXL": _s(128, BF), "NXT": _s(A, BF),
-    "ZS": _s(B, BF), "CS": _s(B, BF), "TG": _s(B, BF), "D0": _s(B, F16),
-    "IJ": _s(256, I32), "PI": _s(2, I32), "LI": _s(2, I32), "COL": _s(16, F32), "JL": _s(256, I32), "JH": _s(256, F32),
-    "DG": _s(B, F32), "BO": _s(128, BF), "BOH": _s(128, F16), "WP": _s(144, BF), "WH": _s(144, F16), "WR2": _s(B, BF),
-    "ID": _s(128, F32), "IDN": _s(128, F32), "IN": _s(128, BF), "IB": _s(128, BF), "JN": _s(128, BF),
-    "JP": _s(128, BF), "BOW": _s(12 * 128, BF), "EF": _s(2 * 1248, BF), "RST": _s(16 * CS, BF), "SS": _s(16 * B, F32),
-    "IW": _s(12, F32), "ML": _s(12, U16), "DC": _s(72, F32), "DUM": _s(12, F32), "IW16": _s(144, F32), "IW17": _s(144, F32),
-    "W3": _s(288, BF), "QQ": _s(256, BF), "QI": _s(256, BF), "IR": _s(B, BF), "WROW": _s(B, BF), "THR": _s(B, BF),
-    "WCOL": _s(12, F32), "CHALF": _s(B, BF), "CZERO": _s(B, BF), "C88": _s(B, BF), "CONE": _s(288, BF), "CCEN": _s(36, BF),
-    "LKF": _s(144, F32), "LKJ": _s(144, U16), "NXA": _s(128, I32), "SGN": _s(128, BF), "SGM": _s(128, BF),
-    "BOS": _s(128, F16), "QH": _s(128, BF), "CD": _s(B, BF), "SV": _s(B, BF),
-    "AD": _s(6 * B, BF), "AG": _s(6 * B, BF), "AU": _s(7 * 204, U16), "WF": _s(7 * 48, F32), "NC": _s(2 * 2 * B, F32),
-    "OFFS": _s(7 * 2 * B, U16), "MX": _s(2 * 4 * B, F16), "SG": _s(6 * 36, BF), "LQ": _s(6 * 216, U16),
-    "EA": _s(2 * 1248, BF), "EG": _s(2 * 1248, BF), "SA": _s(3 * B, BF), "SO": _s(3 * B, BF), "KC": _s(2 * B, F32),
-    "LT": _s(48, F32), "L2": _s(6 * 24, U16), "TL": _s(6 * 12, U16),
+    "UB": _s(W0 + B, BF), "VB": _s(W0, BF), "BSB": _s(A, BF), "UI": _s(A, I32), "VO": _s(A, I32), "NX": _s(2 * A, I32),
+    "ADI": _s(16, I32), "RI": _s(6 * B, I32), "R": _s(6 * B, BF), "ZS": _s(B, BF), "TG": _s(B, BF), "D0": _s(B, F16),
+    "PI": _s(2, I32), "LI": _s(2, I32), "COL": _s(16, F32), "IJ": _s(B, BF), "JL": _s(256, BF), "JH": _s(128, BF),
+    "DG": _s(B, BF), "BO": _s(128, BF), "BOH": _s(128, F16), "WW": _s(288, F16),
+    "ID": _s(128, F32), "ID16": _s(128, F32), "IB": _s(128, BF), "JP": _s(128, BF), "JN": _s(128, BF),
+    "IH": _s(128, F16), "IN": _s(128, F16), "J5": _s(128, BF), "BOW": _s(12 * 128, BF),
+    "RST": _s(B, BF), "RS2": _s(1024, BF), "SS": _s(1024, F32), "ONE": _s(H, F32),
+    "IW": _s(12, F32), "ML": _s(12, U16), "DC": _s(108, F16), "IW16": _s(144, F32), "IW17": _s(144, F32),
+    "W3": _s(432, BF), "CONE": _s(432, BF), "QQ": _s(640, BF), "QI": _s(256, BF), "L2P": _s(256, BF),
+    "WROW": _s(B, BF), "OFFL": _s(B, BF), "THR": _s(B, BF), "CHALF": _s(B, BF), "WT": _s(16, F32), "WCOL": _s(12, F32),
+    "LKJ": _s(144, U16), "HL": _s(72, BF),
+    "AD": _s(7 * B, F16), "AG": _s(6 * B, F16), "LST": _s(7 * 48, U16), "WF": _s(6 * 24, F32), "OFFS": _s(7 * 2 * B, U16),
+    "NC": _s(2 * 2 * B, F16), "MX": _s(2 * 4 * B, F16), "RQ": _s(2 * B, U16), "SG": _s(6 * 24, BF), "VT": _s(12, F32),
+    "IX": _s(6 * 12, U16), "NM": _s(B, F32),
+    "EA": _s(2 * NE, BF), "EG": _s(2 * NE, BF), "EF": _s(2 * NE, BF), "SA": _s(3 * B, BF), "SO": _s(3 * B, BF),
+    "L2": _s(6 * 24, U16), "TL": _s(6 * 12, U16),
     "PY": _s(2 * 16 * B, F32), "PR": _s(16 * B, F32), "YS": _s(7 * B, F32), "ZL": _s(6 * B, F32), "ZC": _s(2 * B, F32),
-    "ZT": _s(B, F32), "CN": _s(6 * B, F32), "FC": _s(B, F32), "BG": _s(2 * B, F32), "XJ": _s(2 * B, F32),
-    "YK": _s(2 * B, F32), "YJ": _s(2 * B, F32), "M1": _s(B, F32), "M2": _s(B, F32), "T1": _s(B, F32), "EE": _s(B, F32),
+    "ZT": _s(B, F32), "DD": _s(6 * B, F32), "CL": _s(7 * B, F32), "BG": _s(2 * B, F32), "WJ": _s(2 * B, F32),
+    "YJ": _s(2 * B, F32), "M1": _s(B, F32), "M2": _s(B, F32), "BT": _s(64, F32),
+    "PW": ("psum", [128, 1024], F32),
 }
-for _b in range(8):
+for _b in (0, 1, 2, 5, 6, 7):
     SCRATCH["P%d" % _b] = ("psum", [128, 512], F32)
-NDMA = 30
-SEMAPHORES = (["ev", "es", "et", "eg", "sent", "outs"] + ["d%d" % i for i in range(NDMA)]
-              + ["m%s%d" % (k, t) for k in "acz" for t in range(1, STEPS + 1)])
+NDMA = 48
+SEMAPHORES = (["ev", "es", "et", "eg", "outs"] + ["d%d" % i for i in range(NDMA)]
+              + ["%s%s%d" % (w, k, t) for w in ("m", "lm") for k in "acz" for t in range(1, STEPS + 1)])
 
-T_DMA = 2200.0
-MODEL = (1.04, 0.52, 140.0, 1.56, 3.8, 3500.0)
 OPT = {
-    "MA": 12, "MG": 7,
-    "SCAN": [([64, 64, 64], [])] * 5 + [([64, 64], [64])] * 2,
-    "PEY": False,
-    "PED": False,
-    "CLIP": True,
-    "NA": 6, "NV": 3,
-    "CMP": True,
-    "SPL": False,
+    "MA": 8, "MG": 7,
+    "IDX": "v",
+    "CLIP": "s",
+    "CONV": "v",
+    "NA": 3,
+    "ST": True,
+    "SPLIT": True,
 }
-SEED = 0
-ORDER = "ahaiajagafacadaeaoanapabaaaqatbRaraDazakaxaBaAaEaJaCasawaFbSbKaTaUamblalbkbhaVaWaZbcaLcaaHbybMayaGaIbLcbbwbTbBbAbCbzbDbEbFcdccbObmbnbHbGbQbYbZbPbNceaRbVbxcgcfbocochbWbjbiaKbUcIcFbXavbsaPaOcpaNbrctcjckcscucvcDcNcKaQcicJaScLaMcOcHbIcMcGcEcPbqclcwaYeScxcyeJcrcqbubgczbvcQbfbpaXcCeIcRaubJcmcScTcAcUcBdydzcncWdBeLeKeOdsdrePeGeHcVdteQdwducXeXdidfdjdveTeMeRdDdhdAeWdEfidIdHdJdgebdWdTdFdXeaeYdGedeNdxeUdYdVdUdedZdaecdSdKdOeedkbtgDdCdLgHefdRcZdbddeVfjeZdcfkfafecYfbfldMffdldNegfcdmgCgGdnfgdPeheldoftfueidQejdpfdembebbbagEfweweydqekfhesgMfnfmgFeveufvfogNgIfqfrfygPfpexfCfzfxgQgOezfDgJgVfEgRgSgWfFfGgXbdhheqenfYfVgKepeofAfOfWgLfsfUfHgTfXfZgUfRerfQfSetfIfPhifBfTgYiBiDeAeBgafJfKgbiEhjgZhehdhfhkhaeCgchbeDfLeEgdhceFhlhmhthsfMgehvhggfhniJiNiFfNghiGiKggiOhohqiLgiiChpgthuhxhBgqhOgphyhNiHiMiPgriRgugsiViQiUhwgvhCiSiIhDiWjgiThzhQhVgmhrhShPhWgjkFkCjhhYgognjiglhEhFgkhUgwiXhThRhXiYjjhGjchZgxjdhHiZgyhAjagzhIgAjbgBhJkEjejsjrjuiaibjfhKkKkBhMhLkDigicjljkihilidkIkLkAitjnkNjviejmkGifjNjWjTjQimijjMjRjOjtipkOkTkMkPkVjAkUjpiskQjoiqirlfkJkHkRjqjXkSikjVjwjxjPjUjSjBiumCjCinioiikWjzjYjDmzjEjZjFkXlgkYjylclbldlhkZliivjIjHiwmAjGixlaiylrlqjJiziAleltmEmDmBjKjLlsmTkamFmJkbkflkljmSmLmUkgkcllmGmKlulmmMmNmOkdmHmImPkskqnekenfkkknkhlTkmlolnlvlPlMlNlpkjnglRkllWlQkimQmRkrkokplzktlVlwnhkumVlymWnqkvlAlBnpnonnnbnanclSlLmXlUkwkxmYlxkymZkzlOlCndlXnvlHlGlDnslElFlYnrnzlIntlZnwlKlJmamenunAnHnBnInCnxmfnGnimqmhmjmkmbnymmmimlmgmcnKnJnjmnmomrmpmsmdnLmtnQnPnDnlmunkmvnMnmnEnTnRmwnNmxnOmynUnFnZoanSnVofobocnYoeodohogomonojnWnXoloooiokopoqoros"
-ABC = "abcdefghijklmnopqrstuvwxyzABCDEFGHIJKLMNOPQRSTUVWXYZ"
-
-
-def cost(c, m):
-    return c[0] + m[0] * (c[1] + m[3] * c[2] + m[4] * c[3]) + m[1] * c[4]
+PRO = """lr3 fR lnx11 fQI fQQ JL PI lnx10 lad lr0 DG lr1 LI fH lr2 OFFL LANE PF WROW lvo BO GRP ML QI L2P lui fONE W96 pD lr4 fDC IB WCOL RS2a WT BOH IN lvt Ri ka.0 lnx5 D0 RS2b al.0 Ql Rk lnx2 qc.0 pK W3 lcs lzs ID EA7.0 EA1.0 lut ltg pH lnx9 Qq AD0 IW Qc1 IH nc.0 Rq PY0.0 pc.0 EA10.0 Qn0 lnx14 lnx4 lnx0 Qc2 EA11.0 WH lnx3 lnx6 Qc0 EA8.0 lnx1 ID16 WR2 EA4.0 IJ EA0.0 mx.0 pp.0 HL PR0.0 PY1.0 lnx15 DCn0 lnx13 sd.0 lnx8 vs.0 lnx7 lnx12 EA6.0 fWW JP ix.0 ag.0 IW17 JH cV pw.0 IW16 senda.0 Qk S0.0 pq.0 L16 DCa0 EAm.0 pd.0 EA9.0 EA3.0 RST THR JN EA5.0 EA2.0 Z0.0 W0 nm.0 PR1.0 Qn1 BOW7 ls.0 rq.0 tg BOW9 pl.0 LKJ PY2.0 EAs.0 z.0 EAc.0 bg.0 EG7.0 EG8.0 BOW8 EG9.0 EG2.0 EG0.0 EG4.0 l2.0 EG11.0 EG1.0 EG10.0 BOW10 lbs EG3.0 EG6.0 f1 EG5.0 kq.0 S1.0 PR2.0 wj.0 t0.0 y0.0 IT EGs.0 e0.0 EGr.0 EGm.0 dd.0 m2.0 bt.0 EGc.0 S2.0 BOW11 yj.0 sn.0 Z1.0 c0 EA6.1 m0.0 pa.1 al.1 EA9.1 ka.1 EA1.1 EA7.1 qc.1 sendc.0 EA2.1 pc.1 EA10.1 Qn2 EA8.1 Z2.0 y1.0 nc.1 tl.0 EA5.1 oy.0 cx.1 EA11.1 t1.0 cB sendz.0 PY0.1 DCa2 sd.1 e1.0 EA0.1 pd.1 sy0.0 pt.0 pw.1 m1.0 EAm.1 PY1.1 EAs.1 sy1.0 EA3.1 EA4.1 DCa1 OT pp.1 mx.1 pq.1 PR0.1 DCn1 DCn2 cx.0 S0.1 EAr.1 cU"""
+LOOP = """S0 PR0 pd vs EAs rs pl ix EAc ls ag PR1 l2 Z0 rq PY2 EG11 senda sb:-1 kq dd nm Z1 EA7 EG2 EG3 EG1 EG0 EG6 S1 EG4 EG9 EG5 zt EG10 EG8 EGr EGm pa:1 PR2 S2 sendc t0 sn z yj EG7 wj y0 bt EGs bg EGc EA3:1 e0 al:1 EA10:1 ka:1 EA9:1 m2 EA1:1 EA5:1 pt m0 Z2 tl pw:1 qc:1 EA11:1 PY0:1 EAr:1 cx:1 sy0 t1 nc:1 sd:1 EA8:1 EA2:1 EA4:1 PY1:1 e1 oy y1 EA6:1 pc:1 sendz m1 EAm:1 sy1 mx:1 pq:1 pp:1 EA0:1"""
+POST = """PR0.5 S0.5 vs.5 EAc.5 rs.5 ix.5 ag.5 senda.5 ls.5 rq.5 nm.5 PR1.5 PY2.5 pl.5 kq.5 l2.5 sb.4 EG11.5 yj.5 Z1.5 EG6.5 EG7.5 EG3.5 EGr.5 Z0.5 EG9.5 EG5.5 dd.5 EG4.5 cx.5 EG2.5 zt.5 EG8.5 EG0.5 sendc.5 z.5 EG1.5 EGm.5 PR2.5 m2.5 pa.6 S1.5 t0.5 wj.5 y0.5 bg.5 EGs.5 EG10.5 bt.5 Z2.5 EGc.5 S2.5 e0.5 sb.5 m0.5 t1.5 tl.5 e1.5 sy0.5 m1.5 oy.5 ob al.6 sn.5 sy1.5 sendz.5 oc qc.6 PY0.6 pc.6 pt.5 S0.6 S1.6 Z0.6 PR0.6 y1.5 PY1.6 PY2.6 PR2.6 PR1.6 bg.6 S2.6 zt.6 z.6 t1.6 t0.6 y1.6 oy1.6 Z1.6 y0.6 oy0.6"""
 
 
 def v(name, a=0, b=None, st=1, p=(0, 128, 1)):
@@ -98,10 +93,10 @@ def two(x):
 
 
 def build(opt):
-    MA, MG, SCAN, PEY, PED, CLIP = [opt[k] for k in ("MA", "MG", "SCAN", "PEY", "PED", "CLIP")]
+    MA, MG = opt["MA"], opt["MG"]
     ops = []
 
-    def add(eng, instrs, c, lat=0.0, kind="c", extra_w=(), tag=None, after=()):
+    def add(nm, eng, instrs, c, kind="c", extra_w=(), tag=None, after=(), nbytes=0):
         rd, wr = [], list(extra_w)
         for (m, a, k) in instrs:
             vs = [x for x in list(a) + list(k.values()) if isview(x)]
@@ -113,331 +108,341 @@ def build(opt):
                     rd.append(x[2])
                 else:
                     (wr if n == 0 else rd).append(x)
-        if not isinstance(c, tuple):
-            c = (c, 0, 0, 0, 0)
-        ops.append({"e": eng, "i": instrs, "cc": c, "lat": lat, "k": kind, "r": rd, "w": wr, "tag": tag,
-                    "after": list(after), "n": len(ops)})
+        ops.append({"nm": nm, "e": eng, "i": instrs, "cc": c, "k": kind, "r": rd, "w": wr, "tag": tag,
+                    "after": list(after), "n": len(ops), "nb": nbytes})
         return len(ops) - 1
 
     def vcost(m, a):
         o = a[0]
         if o[0] == "i":
-            return (50, 0, 0, ncol(o), 0)
+            return ("vi", 0, 0, ncol(o), 0)
         if len(a) > 1 and isview(a[1]) and a[1][0] == "i":
-            return (50, 0, ncol(o), 0, 0)
-        n = ncol(o)
+            return ("vi", 0, ncol(o), 0, 0)
+        n = ncol(a[1]) if m == "tensor_reduce" else ncol(o)
         if m == "tensor_tensor":
             n = n if inps(a[1]) or inps(a[2]) else 2 * n
         elif two(o) and (m == "memset" or two(a[1])):
             n = n / 2
-        return (30, max(64, n), 0, 0, 0)
+        return ("v", max(64, n), 0, 0, 0)
 
-    def vec(m, *a):
-        return add("v", [(m, a, {})], vcost(m, a))
+    def vec(nm, m, *a):
+        return add(nm, "v", [(m, a, {})], vcost(m, a))
 
-    def tt(o, x, y, op):
-        return vec("tensor_tensor", o, x, y, op)
+    def tt(nm, o, x, y, op):
+        return vec(nm, "tensor_tensor", o, x, y, op)
 
-    def ts(o, x, s1, op0, s2=None, op1=None):
+    def ts(nm, o, x, s1, op0, s2=None, op1=None):
         if op1 is None:
-            return vec("tensor_scalar", o, x, s1, None, op0)
-        return vec("tensor_scalar", o, x, s1, s2, op0, op1)
+            return vec(nm, "tensor_scalar", o, x, s1, None, op0)
+        return vec(nm, "tensor_scalar", o, x, s1, s2, op0, op1)
 
-    def cp(o, x):
-        return vec("tensor_copy", o, x)
+    def cp(nm, o, x):
+        return vec(nm, "tensor_copy", o, x)
 
-    def act(o, x, f=Fn.Identity, **k):
-        c = (70, 0, ncol(o), 0, 0) if x[0] == "i" else (30, max(64, ncol(o)), 0, 0, 0)
-        return add("s", [("activation", (o, x, f), k)], c)
+    def fill(nm, o, c):
+        return vec(nm, "memset", o, c)
 
-    def mm(lst):
+    def scan(nm, o, x, y, init, op0, op1):
+        return vec(nm, "tensor_tensor_scan", o, x, y, init, op0, op1)
+
+    def act(nm, o, x, f=Fn.Identity, **k):
+        if o[0] == "i":
+            c = ("si", 0, 0, ncol(o), 0)
+        elif x[0] == "i":
+            c = ("si", 0, ncol(o), 0, 0)
+        else:
+            c = ("v", max(64, ncol(o)), 0, 0, 0)
+        return add(nm, "s", [("activation", (o, x, f), k)], c)
+
+    sums = []
+
+    def mm(nm, *groups, start=True, stop=True, after=()):
         c = 0
         ins = []
-        for n, (o, l, r) in enumerate(lst):
-            c += max(64, ncol(r)) * (4 if SCRATCH[r[1]][2] == F32 else 1)
-            ins.append(("matmul", (o, l, r, n == 0, n == len(lst) - 1), {}))
-        return add("t", ins, (60, 0, 0, 0, c))
+        for lst in groups:
+            for n, (o, l, r) in enumerate(lst):
+                c += max(64, ncol(r)) * (4 if SCRATCH[r[1]][2] == F32 else 1)
+                ins.append(("matmul", (o, l, r, start and n == 0, stop and n == len(lst) - 1), {}))
+        j = add(nm, "t", ins, ("t", 0, 0, 0, c), after=after)
+        ops[j]["soft"] = set(after)
+        return j
 
     def pick(o, w, src, a, b, p=(0, 128), w0=0):
         return [(o, v(w, w0 + 15 - l, w0 + 143 - l, p=p), v(src, a + l, b, 16, p=p)) for l in range(16)]
 
-    def dma(q, o, x, t=T_DMA, tag=None, out=False):
-        return add(q, [("dma_start", (o, x), {})], 1000.0 if q == "g" else 80.0, lat=t, kind="o" if out else "d", tag=tag)
+    def dma(nm, q, o, x, nbytes, tag=None, out=False, after=()):
+        return add(nm, q, [("dma_start", (o, x), {})], ("dg" if q == "g" else "d", 0, 0, 0, 0),
+                   kind="o" if out else "d", tag=tag, nbytes=nbytes, after=after)
 
-    def gp(m, *a, **k):
-        return add("g", [(m, a, k)], (200, 2 * ncol(a[0]), 0, 0, 0))
+    def gp(nm, m, *a, **k):
+        return add(nm, "g", [(m, a, k)], ("g", 2 * ncol(a[0]), 0, 0, 0))
 
-    def send(kind, t, src, dst):
-        s = add("g", [("send", (("n",), src), {"d": (dst,), "sem": "m%s%d" % (kind, t)})], 900.0, kind="r")
-        ops[s]["r"], ops[s]["w"] = [src], []
-        add("x", [], 0.0, lat=-1.0, kind="a", extra_w=[dst], after=[s], tag="m%s%d" % (kind, t))
+    def iota(nm, o, pat, base=0, cm=0):
+        if SCRATCH[o[1]][2] == I32:
+            return gp(nm, "iota", o, pat, base, cm)
+        return gp(nm, "iota", o, pat, base, cm, allow_small_or_imprecise_dtypes=True)
 
-    col = lambda j: v("COL", j, j + 1)
-    LANE, PF, GRP, L16, SQ, B1, HB = col(0), col(1), col(2), col(3), col(4), col(5), col(9)
+    def send(kind, t, srcs, dst, alu=0, whole=()):
+        s = add("send%s.%d" % (kind, t - 1), "g", [("send", (), {"s": list(srcs), "w": list(whole), "d": [dst], "alu": alu,
+                                                              "sem": "m%s%d" % (kind, t)})], ("r", 0, 0, 0, 0), kind="r")
+        ops[s]["r"], ops[s]["w"] = list(srcs) + list(whole), []
+        add("land%s.%d" % (kind, t - 1), "x", [], ("x", 0, 0, 0, 0), kind="a", extra_w=[dst], after=[s], tag="m%s%d" % (kind, t))
+
+    col = lambda j, p=(0, 128): v("COL", j, j + 1, p=p)
+    LANE, PF, GRP, L16, W96 = col(0), col(1), col(2), col(3), col(4)
     P = lambda b, a, c: v("P%d" % b, a, c)
+    PW = lambda a, c: v("PW", a, c)
     sub = lambda x, a, b: v(x[1], x[2] + a, x[2] + b)
+    KB = 1024
 
-    gp("iota", v("PI"), [[0, 2]], 0, 1)
-    gp("iota", v("IJ"), [[1, 256]], 0, 0)
-    dma("y", v("ADI", 0, 12), ext("ad"))
-    dma("y", v("VO"), ext("vo"), 3000.0)
-    dma("y", v("UI"), ext("ui"), 3800.0)
-    dma("y", v("NXI", 0, 64), ext("nx", 0, A))
-    dma("y", v("NXI", 64, 128), ext("nx", A, 2 * A))
-    for n, nm in enumerate(("sl", "tr", "hv")):
-        dma("s", v("RI", 72 * n, 72 * n + 72), ext(nm))
-    dma("g", v("V", B, B + W0), ext("vt"), 4500.0)
-    dma("g", v("U", B, B + W0), ext("ut"), 5000.0)
-    dma("g", v("BS", 0, A), ext("bs"), 4500.0)
-    dma("y", v("CS"), ext("cs"), 4000.0)
-    dma("y", v("ZS"), ext("zs"), 4000.0)
-    dma("y", v("TG"), ext("tg"), 4000.0)
-    vec("memset", v("NXT"), 0.0)
-    vec("memset", v("CHALF"), 0.5)
-    vec("memset", v("CZERO"), 0.0)
-    vec("memset", v("CONE"), 1.0)
-    vec("memset", v("C88"), CEN / 16.0)
-    vec("memset", v("CCEN"), float(CEN))
-    vec("memset", v("WP"), 0.0)
-    vec("memset", v("QI", p=(32, 48)), -1.0)
-    vec("tensor_tensor_scan", v("WROW"), v("CHALF"), v("CZERO"), 2.0 ** 97, Op.mult, Op.add)
-    ts(v("LI"), v("PI"), 15, Op.bitwise_and)
-    cp(LANE, v("LI", 0, 1))
-    cp(PF, v("PI", 0, 1))
-    tt(GRP, PF, LANE, Op.subtract)
-    ts(v("JL", 0, B), v("IJ", 0, B), 15, Op.bitwise_and)
-    tt(v("JH", 0, 128), v("IJ", 0, 128), v("JL", 0, 128), Op.subtract)
-    ts(v("BO"), v("JH", 0, 128), GRP, Op.is_equal)
-    cp(v("BOH"), v("BO"))
-    cp(v("WP", 15, 128, 16), v("BO", 0, 128, 16))
-    cp(v("WH"), v("WP"))
-    ts(v("DG"), v("JL", 0, B), LANE, Op.is_equal)
-    ts(v("ID"), v("IJ", 0, 128), PF, Op.is_equal)
-    cp(v("ML"), v("IJ", 0, 12))
-    ts(v("IW"), v("IJ", 0, B, 16), LANE, Op.add)
-    act(v("IB"), v("ID"))
-    act(v("JN"), v("ID"), scale=-2048.0)
-    act(v("JP"), v("ID"), scale=2048.0)
-    if PEY:
-        act(v("IN"), v("ID"), scale=-1.0)
-    if PED:
-        act(v("IDN"), v("ID"), scale=-1.0)
-    ts(v("THR"), v("DG"), 2.0 ** 99, Op.mult, -2.0 ** 99, Op.add)
-    act(v("WR2"), v("WROW"), scale=-2.5)
-    tt(v("THR"), v("THR"), v("WR2"), Op.add)
-    act(L16, LANE, scale=16.0)
-    act(SQ, LANE, Fn.Square)
-    act(B1, SQ, scale=-1.0, bias=1.0)
-    for m in range(3):
-        act(col(6 + m), SQ, scale=-4096.0, bias=float(W0 + B * m - CEN))
-        act(v("DC", 24 * m, 24 * m + 12), v("IW"), bias=float(A + 14 * 2048))
-        act(v("DC", 24 * m + 12, 24 * m + 24), v("IW"), bias=float(W0 + B * m + 14 * 2048))
-    act(v("DUM"), v("IW"), bias=float(32768 - B))
-    ts(v("IR"), v("IJ", 0, B), 2.0 ** -16, Op.mult)
-    gp("iota", v("QI", p=(0, 32)), [[0, 16], [2, 16]], 0, 0, allow_small_or_imprecise_dtypes=True)
-    gp("affine_select", v("QQ", p=(0, 32)), v("QI", p=(0, 32)), [[-1, 16], [0, 16]], Op.is_equal, 0.0, 0, 1)
-    gp("affine_select", v("QQ", p=(32, 48)), v("QI", p=(32, 48)), [[-1, 16], [0, 16]], Op.is_equal, 0.0, 0, 1)
-    gp("affine_select", v("W3", p=(0, 32)), v("CONE", p=(0, 32)), [[128, 2], [1, 144]], Op.is_equal, 0.0, -15, -16)
-    gp("iota", v("IW16"), [[0, 12], [256, 12]], 0, 0, allow_small_or_imprecise_dtypes=True)
-    act(v("IW17"), v("IW16"), bias=L16)
-    mm(pick(P(7, 0, 12), "WP", "WROW", 0, B))
-    act(v("WCOL"), P(7, 0, 12), scale=0.0625)
+    dma("lad", "y", v("ADI", 0, 12), ext("ad"), 6 * KB)
+    for n, (nm, p0) in enumerate((("sl", 0), ("tr", 8), ("hv", 16), ("sl", 32), ("tr", 40))):
+        dma("lr%d" % n, "s" if n % 2 else "y", v("RI", p=(p0, p0 + 8)), ext(nm), 36 * KB)
+    dma("lvo", "y", v("VO"), ext("vo"), 512 * KB)
+    dma("lvt", "y", v("VB"), ext("vt"), 512 * KB)
+    dma("lui", "y", v("UI"), ext("ui"), 512 * KB)
+    lut = dma("lut", "y", v("UB", 0, W0), ext("ut"), 512 * KB)
+    dma("lcs", "y", v("UB", W0, W0 + B), ext("cs"), 48 * KB)
+    dma("lzs", "y", v("ZS"), ext("zs"), 48 * KB)
+    dma("ltg", "y", v("TG"), ext("tg"), 48 * KB)
+    for l in range(16):
+        dma("lnx%d" % l, "y", v("NX", p=(l, 128, 16)), ext("nx"), 64 * KB)
+    dma("lbs", "y", v("BSB"), ext("bs"), 256 * KB)
+    dma("cV", "g", v("V", B, B + W0), ext("vt"), 1024 * KB, after=[lut])
+    dma("cB", "g", v("BS", 0, A), ext("bs"), 512 * KB, after=[lut])
+    dma("cU", "g", v("U", B, B + W0), ext("ut"), 1024 * KB, after=[lut])
+    iota("PI", v("PI"), [[0, 2]], 0, 1)
+    iota("JL", v("JL"), [[0, 16], [1, 16]])
+    iota("IJ", v("IJ"), [[1, B]])
+    iota("JH", v("JH"), [[16, 8], [0, 16]])
+    iota("IW16", v("IW16"), [[0, 12], [256, 12]])
+    fill("fR", v("R", p=(0, 32)), -1.0)
+    fill("fQQ", v("QQ", 0, 256, p=(0, 32)), 0.0)
+    fill("fQI", v("QI", p=(32, 48)), -4096.0)
+    fill("fONE", v("CONE", p=(0, 32)), 1.0)
+    fill("fWW", v("WW"), 0.0)
+    fill("fDC", v("DC"), float(B))
+    fill("fH", v("CHALF"), 0.5)
+    fill("f1", v("ONE"), 1.0)
+    ts("LI", v("LI"), v("PI"), 15, Op.bitwise_and)
+    cp("LANE", LANE, v("LI", 0, 1))
+    cp("PF", PF, v("PI", 0, 1))
+    tt("GRP", GRP, PF, LANE, Op.subtract)
+    ts("BO", v("BO"), v("JH"), GRP, Op.is_equal)
+    cp("BOH", v("BOH"), v("BO"))
+    cp("WH", v("WW", 15, 128, 16), v("BO", 0, 128, 16))
+    ts("DG", v("DG"), v("JL", 0, B), LANE, Op.is_equal)
+    ts("RST", v("RST"), v("JL", 0, B), 0.5, Op.is_gt)
+    ts("IB", v("IB"), v("IJ", 0, 128), PF, Op.is_equal)
+    cp("W0", v("WW", 144 + 15, 144 + 128, 16), v("IB", 0, 128, 16))
+    act("ID", v("ID"), v("IB"))
+    act("ID16", v("ID16"), v("IB"), scale=16.0)
+    ts("JP", v("JP"), v("IB"), BIG, Op.mult)
+    ts("JN", v("JN"), v("IB"), -BIG, Op.mult)
+    cp("IH", v("IH"), v("IB"))
+    ts("IN", v("IN"), v("IB"), -1.0, Op.mult)
+    if opt["IDX"] == "s":
+        ts("J5", v("J5"), v("IB"), 512.0, Op.mult)
+    ts("OFFL", v("OFFL"), v("DG"), 2.0 ** 99, Op.mult, -2.0 ** 99, Op.add)
+    scan("WROW", v("WROW"), v("CHALF"), v("OFFL"), 2.0 ** 97, Op.mult, Op.max)
+    act("WR2", P(1, B, 2 * B), v("WROW"), scale=-2.5)
+    tt("THR", v("THR"), P(1, B, 2 * B), v("OFFL"), Op.add)
+    tt("WT", v("WT"), v("WROW", 96, 112), v("DG", 0, 16), Op.mult)
+    vec("W96", "tensor_reduce", W96, v("WT"), Ax.X, Op.add)
+    ts("WCOL", v("WCOL"), v("WROW", 0, B, 16), W96, Op.mult)
     for m in range(min(MA, MG), 12):
-        act(v("BOW", 128 * m, 128 * m + 128), v("BO"), scale=v("WCOL", m, m + 1))
-    rw = max([B] + [16 * w for x in SCAN for w in x[1]])
-    vec("memset", v("RST", 0, rw), 1.0)
-    vec("memset", v("RST", 0, rw, 16), 0.0)
-    ts(v("OT", 0, A), v("VO"), -float(CEN), Op.add)
-    ts(v("IT", 0, A), v("UI"), -float(CEN), Op.add)
-    cp(v("RB", 0, 216), v("RI"))
-    act(v("RB", 216, 360), v("RB", 0, 144), Fn.Square)
-    for n, q in enumerate((0, 1, 2, 2, 3, 4)):
-        dma("s" if n % 2 else "y", v("R", p=(8 * n, 8 * n + 8)), v("RB", 72 * q, 72 * q + 72))
-    for q in range(2):
-        mm(pick(P(6, 72 * q, 72 * q + 72), "W3", "R", 0, 6 * B, p=(0, 16), w0=144 * q))
-    tt(v("LKF"), P(6, 0, 144), v("IW17"), Op.add)
-    cp(v("LKJ"), v("LKF"))
-    ts(v("NXA"), v("NXI"), 31, Op.bitwise_and)
-    cp(v("NXL"), v("NXA"))
-    tt(v("NXH"), v("NXI"), v("NXA"), Op.subtract)
-    for n in range(4):
-        dma("s" if n % 2 else "y", v("NXT", p=(n, 128, 16)), v("NXL" if n % 2 else "NXH", 64 * (n // 2), 64 * (n // 2) + 64), tag="nx")
-    vec("memset", v("SGN"), -1.0)
-    vec("memset", v("SGN", 0, 128, 16), 1.0)
-    vec("memset", v("SGN", 1, 128, 16), 1.0)
-    tt(v("BOS"), v("BO"), v("SGN"), Op.mult)
-    act(v("SGM", p=(0, 32)), v("SGN", p=(0, 32)), scale=-1.0)
-    gp("affine_select", v("QH", p=(0, 32)), v("SGM", p=(0, 32)), [[-1, 8], [0, 16]], Op.is_equal, 0.0, -16, 1)
-    ts(HB, LANE, 2.0, Op.is_ge, 0.5, Op.subtract)
-    act(v("U", B + W0, 2 * B + W0), v("CS"))
-    if not PEY:
-        act(P(1, 0, B), v("TG"))
-    cp(v("ADF", 0, 12), v("ADI", 0, 12))
-    tt(v("D0"), ind(v("ADF", 0, 12), v("ML")), v("DG"), Op.mult)
+        act("BOW%d" % m, v("BOW", 128 * m, 128 * m + 128), v("BO"), scale=v("WCOL", m, m + 1))
+    cp("ML", v("ML"), v("IJ", 0, 12))
+    ts("IW", v("IW"), v("IJ", 0, B, 16), LANE, Op.add)
+    for m in range(3):
+        act("DCa%d" % m, v("DC", 36 * m, 36 * m + 12), v("IW"), bias=A - BIG)
+        act("DCn%d" % m, v("DC", 36 * m + 12, 36 * m + 24), v("IW"), bias=W0 + B * m - BIG)
+    act("L16", L16, LANE, scale=16.0)
+    act("IW17", v("IW17"), v("IW16"), bias=L16)
+    dma("Ri", "s", v("R", p=(25, 26)), v("IJ", p=(0, 6)), 3 * KB)
+    act("Rk", v("R", p=(0, 24)), v("RI", p=(0, 24)))
+    act("Rq", v("R", p=(32, 48)), v("RI", p=(32, 48)), Fn.Square)
+    act("L2P", v("L2P", p=(0, 1)), v("JL", p=(0, 1)), Fn.Square, scale=64.0)
+    dma("Ql", "s", v("QQ", 0, 256, p=(24, 25)), v("L2P", p=(0, 1)), KB)
+    act("QI", v("QI", p=(0, 16)), v("JL", p=(0, 16)), Fn.Silu, scale=8192.0)
+    gp("Qk", "affine_select", v("QQ", 0, 256, p=(0, 16)), v("QI", p=(0, 16)), [[-1, 16], [0, 16]], Op.is_equal, 0.0, 0, 1)
+    gp("Qq", "affine_select", v("QQ", 0, 256, p=(32, 48)), v("QI", p=(32, 48)), [[-1, 16], [0, 16]], Op.is_equal, 0.0, 0, 1)
+    for m in range(3):
+        ts("Qc%d" % m, col(5 + m), v("ID", 26, 27), -float(W0 + B * m), Op.mult, v("ID", 25, 26), Op.add)
+        ts("Qn%d" % m, v("QQ", 256 + 128 * m, 384 + 128 * m, p=(0, 48)), v("QQ", 0, 128, p=(0, 48)), col(5 + m, (0, 48)), Op.add)
+    gp("W3", "affine_select", v("W3", p=(0, 32)), v("CONE", p=(0, 32)), [[128, 3], [1, 144]], Op.is_equal, 0.0, -15, -16)
+    mm("pH", pick(P(2, 144, 216), "W3", "R", 0, 6 * B, p=(0, 24), w0=288))
+    act("HL", v("HL"), P(2, 144, 216), scale=-2.0)
+    mm("pK", *[pick(P(2, 72 * q, 72 * q + 72), "W3", "R", 0, 6 * B, p=(0, 24), w0=144 * q) for q in range(2)])
+    tt("LKJ", v("LKJ"), P(2, 0, 144), v("IW17"), Op.add)
+    gp("IT", "affine_select", v("IT", 0, A), v("UI"), [[0, A]], Op.is_ge, 0.0, 0, 0)
+    gp("OT", "affine_select", v("OT", 0, A), v("VO"), [[0, A]], Op.is_ge, 0.0, 0, 0)
+    act("c0", v("CL", 0, B), v("UB", W0, W0 + B))
+    act("tg", P(1, 0, B), v("TG"))
+    act("z.0", v("ZC", 0, B), v("ZS"), scale=0.0625)
+    tt("D0", v("D0"), ind(v("ADI", 0, 12), v("ML")), v("DG"), Op.mult)
+    mm("pD", [(P(5, 0, B), v("BOH"), v("D0"))])
+    act("AD0", v("AD", 0, B), P(5, 0, B))
+    fill("RS2a", v("RS2"), 1.0)
+    fill("RS2b", v("RS2", 0, 1024, 16), 0.0)
 
-    def first(E, t, rep, prep, key, bank, sg, ms):
-        e0 = 1248 * (t % 2)
-        f0 = 1248 * (bank - 6)
+    def first(E, t, rep, key, bank, sg, ms):
+        e0 = NE * (t % 2)
+        f0 = NE * (bank - 6)
         for m in range(12):
             kc = v("WF", key + m, key + m + 1)
             if m < ms:
-                ts(v(E, e0 + EOFF[m], e0 + EOFF[m + 1]), v(rep[0], rep[1] + 16 * m, rep[1] + B), kc,
+                ts("%s%d.%d" % (E, m, t), v(E, e0 + EOFF[m], e0 + EOFF[m + 1]), sub(rep, 16 * m, B), kc,
                    Op.is_equal, v("WCOL", m, m + 1), Op.mult)
             else:
-                act(v("EF", f0 + EOFF[m], f0 + EOFF[m + 1]), P(prep[0], prep[1] + 16 * m, prep[1] + B), Fn.Abs,
+                act("%s%d.%d" % (E, m, t), v("EF", f0 + EOFF[m], f0 + EOFF[m + 1]), sub(rep, 16 * m, B), Fn.Abs,
                     scale=-1.0, bias=kc)
         if ms < 12:
-            act(v(E, e0 + EOFF[ms], e0 + 1248), v("EF", f0 + EOFF[ms], f0 + 1248), Fn.Relu, scale=-1.0, bias=1.0)
-        mm([(P(bank, 0, B), v("IB"), v("THR"))]
+            act("%sr.%d" % (E, t), v(E, e0 + EOFF[ms], e0 + NE), v("EF", f0 + EOFF[ms], f0 + NE), Fn.Relu, scale=-1.0, bias=1.0)
+        mm("%sm.%d" % (E, t), [(P(bank, 0, B), v("IB"), v("THR"))]
            + [(P(bank, 16 * m, B), v("BO") if m < ms else v("BOW", 128 * m, 128 * m + 128),
                v(E, e0 + EOFF[m], e0 + EOFF[m + 1])) for m in range(12)])
-        act(v(sg, 0, B), P(bank, 0, B), Fn.Sign)
+        act("%ss.%d" % (E, t), v(sg, 0, B), P(bank, 0, B), Fn.Sign)
         o = B + B * (t % 2)
-        vec("tensor_tensor_scan", v(sg, o, o + B), v("RST", 0, B), v(sg, 0, B), 0.0, Op.mult, Op.add)
+        scan("%sc.%d" % (E, t), v(sg, o, o + B), v("RST"), v(sg, 0, B), 0.0, Op.mult, Op.max)
         return v(sg, o + 15, o + B, 16)
 
     def ints(t):
         last = t == STEPS
-        au, wf, nc, of = 204 * t, 48 * t, 2 * B * (t % 2), 2 * B * t
-        src, a0, bo, wp = ("D0", 0, "BOH", "WH") if t == 0 else ("AD", B * (t - 1), "BO", "WP")
-        mm(pick(P(4, B, B + 12), wp, src, a0, a0 + B))
-        if last:
-            cp(v("AU", au + B, au + 204), P(4, B, B + 12))
+        N = lambda s: "%s.%d" % (s, t)
+        ls, wf, nc, of = 48 * t, 24 * t, 2 * B * (t % 2), 2 * B * t
+        al, rep = v("LST", ls, ls + 12), v("AD", B * t, B * t + B)
+        if t == 0:
+            src = v("ADI", 0, 12)
         else:
-            if opt["SPL"]:
-                cp(v("AU", au + B, au + 204), P(4, B, B + 12))
-            mm([(P(4, 0, B), v(bo), v(src, a0, a0 + B))])
-            cp(v("AU", au, au + (B if opt["SPL"] else 204)), P(4, 0, B if opt["SPL"] else 204))
-            act(v("WF", wf, wf + 12), P(4, B, B + 12))
-        al = v("AU", au + B, au + 204)
+            src = P(5, 448, 460)
+            mm(N("pa"), pick(src, "WW", "AD", B * t, B * t + B, w0=144))
+        act(N("al"), al, src)
+        if not last:
+            act(N("ka"), v("WF", wf, wf + 12), src)
         PT, QT = ("IT", "OT") if t % 2 == 0 else ("OT", "IT")
-        pc, qc = v("NC", nc, nc + B), v("NC", nc + B, nc + 2 * B)
-        act(qc, ind(v(QT, 0, A), al))
-        act(pc, ind(v(PT, 0, A), al))
-        ts(v("OFFS", of, of + 2 * B), v("NC", nc, nc + 2 * B), float(CEN), Op.add)
+        pw = v({0: "UI", 1: "VO"}.get(t, PT), 0, A)
+        qw = v({0: "VO"}.get(t, QT), 0, A)
+        pc, qc = v("OFFS", of, of + B), v("OFFS", of + B, of + 2 * B)
+        act(N("qc"), qc, ind(qw, al), bias=0.3)
+        act(N("pc"), pc, ind(pw, al), bias=0.3)
         if last:
             return
-        mx, sg, lq = 4 * B * (t % 2), 36 * t, 216 * t
+        mx, sg = 4 * B * (t % 2), 24 * t
+        if opt["CONV"] == "v":
+            ts(N("nc"), v("NC", nc, nc + 2 * B), v("OFFS", of, of + 2 * B), -float(CEN), Op.add)
+        else:
+            act(N("nc"), v("NC", nc, nc + 2 * B), v("OFFS", of, of + 2 * B), bias=-float(CEN))
+        ph, qh = v("NC", nc, nc + B), v("NC", nc + B, nc + 2 * B)
         rt = v("R", B * t, B * t + B, p=(0, 48))
-        mm([(P(3, 0, B), v("QQ", 0, 128, p=(0, 48)), rt)])
-        mm([(P(3, B, 2 * B), v("QQ", 128, 256, p=(0, 48)), rt)])
-        act(P(3, 0, 2 * B), P(3, 0, 2 * B), Fn.Relu, bias=B1)
-        mm([(P(7, 216, 216 + B), v("QQ", 0, 128, p=(0, 48)), rt), (P(7, 216, 216 + B), v("BO"), v("IR"))])
-        kc = v("KC", B * (t % 2), B * (t % 2) + B)
-        act(kc, P(7, 216, 216 + B), scale=4096.0, bias=col(6 + t // 2))
-        if opt["CMP"]:
-            act(P(2, B, 2 * B), qc)
-        tt(v("MX", mx, mx + B), pc, P(2, B, 2 * B) if opt["CMP"] else qc, Op.is_gt if t % 2 == 0 else Op.is_lt)
-        tt(v("MX", mx + B, mx + 3 * B), v("NC", nc, nc + 2 * B), P(3, 0, 2 * B), Op.mult)
-        tt(v("MX", mx + 3 * B, mx + 4 * B), pc, P(3, B, 2 * B), Op.mult)
-        act(v("CD"), ind(v("NXT"), al))
-        mm([(P(5, 228, 228 + B), v("BOS"), v("MX", mx, mx + B)),
-            (P(5, 228, 228 + B), v("QH", p=(0, 24)), v("R", B * t, B * t + B, p=(0, 24)))])
-        act(v("SV"), P(5, 228, 228 + B), Fn.Sign, scale=-1.0, bias=HB)
-        mm([(P(4, 204, 204 + B), v("IB"), v("CD")), (P(4, 204, 204 + B), v("JP"), v("SV"))])
-        act(v("AG", B * t, B * t + B), P(4, 204, 204 + B), Fn.Relu, bias=-2048.0)
-        send("a", t + 1, v("AG", B * t, B * t + B), v("AD", B * t, B * t + B))
-        mm(pick(P(5, 0, 36), "WH", "MX", mx + B, mx + 4 * B) + [(P(5, 0, 36), v("IB"), v("CCEN"))])
-        mm([(P(5, 36, 36 + B), v("BOH"), v("MX", mx + 2 * B, mx + 3 * B)), (P(5, 36, 36 + B), v("BO"), v("C88"))])
-        cp(v("LQ", lq, lq + 204), P(5, 24, 228))
-        act(v("WF", wf + 12, wf + 36), P(5, 0, 24))
+        Q = lambda n: v("QQ", 128 * n, 128 * n + 128, p=(0, 48))
+        mm(N("pd"), [(P(5, 0, B), v("IH"), ph), (P(5, 0, B), v("IN"), qh)])
+        act(N("sd"), v("MX", mx + 3 * B, mx + 4 * B), P(5, 0, B), Fn.Sign, scale=1.0 if t % 2 == 0 else -1.0, bias=-0.5)
+        mm(N("pw"), *[[(PW(128 + B * n, 320 + B * n), v("IH"), x), (PW(128 + B * n, 320 + B * n), Q(q), rt)]
+                      for n, (x, q) in enumerate(((ph, 0), (qh, 1), (ph, 1)))], [(PW(704, 896), Q(2 + t // 2), rt)])
+        ts(N("mx"), v("MX", mx, mx + 3 * B), PW(128, 704), -float(CEN), Op.max)
+        tt(N("nm"), v("NM"), PW(704, 896), pc, Op.max)
+        mm(N("pp"), pick(P(5, B, B + 48), "WW", "MX", mx, mx + 4 * B)
+           + [(P(5, B + 36, B + 48), v("IB"), v("HL", 12 * t, 12 * t + 12))])
+        ix = v("IX", 12 * t, 12 * t + 12)
+        if opt["IDX"] == "s":
+            act(N("vs"), v("SG", sg, sg + 12), P(5, B + 36, B + 48), Fn.Sign, bias=16.5)
+            mm(N("pv"), [(P(5, 460, 472), v("ID"), v("WF", wf, wf + 12)), (P(5, 460, 472), v("J5"), v("SG", sg, sg + 12))])
+            act(N("ix"), ix, P(5, 460, 472), bias=512.0)
+        else:
+            ts(N("vs"), v("VT"), P(5, B + 36, B + 48), -16.5, Op.is_gt, float(A), Op.mult)
+            tt(N("ix"), ix, v("VT"), al, Op.add)
+        act(N("ag"), v("AG", B * t, B * t + B), ind(v("NX"), ix))
+        send("a", t + 1, [v("AG", B * t, B * t + B)], v("AD", B * t + B, B * t + 2 * B))
+        act(N("ls"), v("LST", ls + 12, ls + 48), P(5, B, B + 36), bias=float(SUM0))
         if t >= 2:
-            act(v("SG", sg + 12, sg + 24), P(5, 24, 36), Fn.Sign, bias=0.5 - (W0 + B * (t // 2 - 1)))
-        nb = first("EA", t, ("AU", au), (4, 0), wf, 6, "SA", MA)
-        dc = 24 * (t // 2)
-        mm([(P(6, 204, 228), v("ID"), v("DC", dc, dc + 24)), (P(6, 204, 216), v("JP"), nb), (P(6, 216, 228), v("JP"), nb)])
-        tt(v("LT", 0, 24), P(6, 204, 228), v("WF", wf, wf + 24), Op.max)
-        cp(v("L2", 24 * t, 24 * t + 24), v("LT", 0, 24))
-        tt(ind(v(PT), v("L2", 24 * t, 24 * t + 12)), pc, kc, Op.max)
-        lst = [(P(7, B, B + 12), v("ID"), v("WF", wf + 24, wf + 36)), (P(7, B, B + 12), v("JN"), nb)]
-        if t >= 2:
-            lst.append((P(7, B, B + 12), v("JN"), v("SG", sg + 12, sg + 24)))
-        mm(lst)
-        act(v("WF", wf + 36, wf + 48), P(7, B, B + 12), bias=-34816.0 if t >= 2 else -32768.0)
-        ng = first("EG", t, ("LQ", lq + 12), (5, 36), wf + 36, 7, "SO", MG)
-        mm([(P(7, 204, 216), v("ID"), v("WF", wf + 36, wf + 48)), (P(7, 204, 216), v("JN"), ng)])
-        tt(v("LT", 24, 36), P(7, 204, 216), v("DUM"), Op.max)
-        ts(v("TL", 12 * t, 12 * t + 12), v("LT", 24, 36), float(B - 32768), Op.add)
+            act(N("rs"), v("SG", sg + 12, sg + 24), P(5, B + 24, B + 36), Fn.Relu, bias=float(SUM0 + 1 - W0 - B * (t // 2 - 1)))
+        rq = v("RQ", B * (t % 2), B * (t % 2) + B)
+        mm(N("pq"), [(P(5, 240, 240 + B), v("BOH"), v("MX", mx + B, mx + 2 * B))])
+        act(N("rq"), rq, P(5, 240, 240 + B), bias=float(SUM0 + B))
+        nb = first("EA", t, rep, wf, 6, "SA", MA if t else 12)
+        dc = 36 * (t // 2)
+        mm(N("pl"), [(P(6, B, B + 36), v("IH"), v("DC", dc, dc + 36)), (P(6, B, B + 12), v("JP"), nb),
+                     (P(6, B + 12, B + 24), v("JP"), nb), (P(6, B + 24, B + 36), v("JN"), nb)]
+           + ([(P(6, B + 24, B + 36), v("JN"), v("SG", sg + 12, sg + 24))] if t >= 2 else []))
+        tt(N("l2"), v("L2", 24 * t, 24 * t + 24), P(6, B, B + 24), v("LST", ls, ls + 24), Op.max)
+        tt(N("kq"), v("WF", wf + 12, wf + 24), P(6, B + 24, B + 36), v("LST", ls + 24, ls + 36), Op.add)
+        act(N("sn"), ind(v(PT), v("L2", 24 * t, 24 * t + 12)), v("NM"), Fn.Silu)
+        ng = first("EG", t, rq, wf + 12, 7, "SO", MG)
+        mm(N("pt"), [(P(7, B, B + 12), v("ID"), v("WF", wf + 12, wf + 24)), (P(7, B, B + 12), v("JN"), ng)])
+        tt(N("tl"), v("TL", 12 * t, 12 * t + 12), P(7, B, B + 12), v("IW"), Op.max)
 
     def floats(t):
         last = t == STEPS
+        N = lambda s: "%s.%d" % (s, t)
         X, Y = ("U", "V") if t % 2 == 0 else ("V", "U")
         ex = B + W0 + B * (t // 2)
         ey = B + W0 + B * ((t + 1) // 2)
+        xw = v("UB", 0, W0) if t == 0 else v(X, B, ex)
+        xc = v("UB") if t == 0 else v(X, B, ex + B)
+        yw = {0: v("VB"), 1: v("UB")}.get(t, v(Y, B, ey))
         of, py, h2 = 2 * B * t, 16 * B * (t % 2), B * (t % 2)
-        al = v("AU", 204 * t + B, 204 * t + 204)
+        al = v("LST", 48 * t, 48 * t + 12)
         w = B // opt["NA"]
-        for c in range(0, B, w):
-            act(v("PY", py + 16 * c, py + 16 * (c + w)), ind(v(Y, B, ey), v("OFFS", of + B + c, of + B + c + w)), scale=0.0625)
-        d = 0
-        for w in SCAN[t][0] + SCAN[t][1]:
-            a, b = 16 * d, 16 * (d + w)
-            tt(v("PR", a, b), ind(v(X, B, ex), v("OFFS", of + d, of + d + w)), v("PY", py + a, py + b), Op.mult)
-            if d >= sum(SCAN[t][0]):
-                s0 = a - 16 * sum(SCAN[t][0])
-                vec("tensor_tensor_scan", v("SS", s0, s0 + 16 * w), v("RST", 0, 16 * w), v("PR", a, b), 0.0, Op.mult, Op.add)
+        for n, c in enumerate(range(0, B, w)):
+            act(N("PY%d" % n), v("PY", py + 16 * c, py + 16 * (c + w)), ind(yw, v("OFFS", of + B + c, of + B + c + w)),
+                scale=1.0 if last else 0.0625)
+        split = opt["SPLIT"] or last
+        for n in range(3):
+            d = 64 * n
+            a, b = 16 * d, 16 * (d + 64)
+            tt(N("PR%d" % n), v("PR", a, b), ind(xw, v("OFFS", of + d, of + d + 64)), v("PY", py + a, py + b), Op.mult)
+            if last and n == 2:
+                scan(N("S2"), v("SS"), v("RS2"), v("PR", a, b), 0.0, Op.mult, Op.add)
             else:
-                mm([(P(0, d, d + w), v("ID"), v("PR", a + k, b, 16)) for k in range(16)])
-            d += w
+                o = P(2, 0, 64) if split and n == 2 else P(0, d, d + 64)
+                lst = [(o, v("ID" if last else "ID16"), v("PR", a + k, b, 16)) for k in range(16)]
+                j = mm(N("S%d" % n), lst[:8], stop=False, after=sums[-1:])
+                sums[:] = [mm(N("Z%d" % n), lst[8:], start=False, after=[j])]
         bg = v("BG", h2, h2 + B)
-        act(bg, ind(v("BS", 0, A), al))
-        if t == 0:
-            z = v("ZS")
-        else:
-            z = v("ZC", h2, h2 + B)
-            if CLIP:
-                act(v("ZT"), v("ZL", B * (t - 1), B * t), Fn.Relu, bias=1.0)
-                act(v("ZT"), v("ZT"), Fn.Relu, scale=-1.0, bias=2.0)
-                act(z, v("ZT"), scale=-1.0, bias=1.0)
+        act(N("bg"), bg, ind(v("BSB") if t == 0 else v("BS", 0, A), al))
+        z = v("ZC", h2, h2 + B)
+        if t > 0:
+            zl = v("ZL", B * (t - 1), B * t)
+            if opt["CLIP"] == "s":
+                act(N("zt"), v("ZT"), zl, Fn.Relu, scale=0.0625, bias=0.0625)
+                act(N("z"), z, v("ZT"), bias=-0.0625)
             else:
-                ts(z, v("ZL", B * (t - 1), B * t), -1.0, Op.max, 1.0, Op.min)
+                ts(N("z"), z, zl, -1.0, Op.max, 0.0625, Op.mult)
         y, tmp = v("YS", B * t, B * t + B), P(1, B, 2 * B)
         if not last:
-            xj, yk, yj = v("XJ", h2, h2 + B), v("YK", h2, h2 + B), v("YJ", h2, h2 + B)
-            cn = v("CN", B * t, B * t + B)
-            act(cn, ind(v(X, B, ex + B), v("L2", 24 * t + 12, 24 * t + 24)))
-            send("c", t + 1, cn, v("FC") if t + 1 == STEPS else v(Y, ey, ey + B))
-            act(xj, ind(v(X, B, ex), v("LQ", 216 * t, 216 * t + 12)), scale=0.0625)
+            wj, yj, dd, c = v("WJ", h2, h2 + B), v("YJ", h2, h2 + B), v("DD", B * t, B * t + B), v("CL", B * t, B * t + B)
             pw = v("PY", py, py + 16 * B)
-            act(yj, ind(pw, v("LKJ", 72 + 12 * t, 84 + 12 * t)), scale=16.0)
-            act(yk, ind(pw, v("LKJ", 12 * t, 12 * t + 12)))
-        cut = sum(SCAN[t][0])
-        pey = PEY and not last
-        t1 = v("T1") if pey else tmp
-        if cut > 0:
-            tt(sub(t1, 0, cut), P(0, 0, cut), sub(z, 0, cut), Op.mult)
-        if cut < B:
-            tt(sub(t1, cut, B), v("SS", 15, 16 * (B - cut), 16), sub(z, cut, B), Op.mult)
+            dma(N("cx"), "y", v(X, ex, ex + B), c, 96 * KB)
+            tt(N("dd"), dd, ind(xc, v("L2", 24 * t + 12, 24 * t + 24)), c, Op.subtract)
+            send("c", t + 1, [dd, c], v("CL", B * t + B, B * t + 2 * B), 1)
+            tt(N("wj"), wj, ind(xw, v("LST", 48 * t + 36, 48 * t + 48)), z, Op.mult)
+            act(N("yj"), yj, ind(pw, v("LKJ", 72 + 12 * t, 84 + 12 * t)), scale=16.0)
+            tt(N("m2"), v("M2"), ind(pw, v("LKJ", 12 * t, 12 * t + 12)), dd, Op.mult)
+        for n, (a, b) in enumerate(((0, 128), (128, B)) if split else ((0, B),)):
+            s = P(0, a, b) if n == 0 else v("SS", 15, 1024, 16) if last else P(2, 0, 64)
+            tt(N("t%d" % n), sub(tmp, a, b), s, sub(z, a, b), Op.mult)
+            tt(N("y%d" % n), sub(y, a, b), sub(tmp, a, b), sub(bg, a, b), Op.add)
+            if n == 1 and opt["ST"] and not last:
+                tt(N("bt"), v("BT"), sub(bg, a, b), P(1, a, b), Op.subtract)
+                tt(N("e1"), P(1, 2 * B, 2 * B + 64), sub(tmp, a, b), v("BT"), Op.add)
+                tt(N("m1"), v("M1", a, b), P(1, 2 * B, 2 * B + 64), sub(wj, a, b), Op.mult)
+                continue
+            if last:
+                dma(N("oy%d" % n), "y", ext("ys", B * t + a, B * t + b), sub(y, a, b), 64 * KB, out=True)
+                continue
+            tt(N("e%d" % n), sub(tmp, a, b), sub(y, a, b), P(1, a, b), Op.subtract)
+            tt(N("m%d" % n), v("M1", a, b), sub(tmp, a, b), sub(wj, a, b), Op.mult)
         if last:
-            tt(y, tmp, bg, Op.add)
-            dma("y", ext("ys", B * t, B * t + B), y, out=True)
             return
-        if pey:
-            mm([(P(1, B, 2 * B), v("ID"), bg), (P(1, B, 2 * B), v("IN"), v("TG"))])
-            act(P(1, 0, B), xj)
-            tt(P(1, 0, B), P(1, 0, B), z, Op.mult)
-            tt(v("EE"), t1, P(1, B, 2 * B), Op.add)
-            tt(v("M1"), v("EE"), P(1, 0, B), Op.mult)
-            mm([(P(0, B, 2 * B), v("ID"), v("EE")), (P(0, B, 2 * B), v("IB"), v("TG"))])
-            act(y, P(0, B, 2 * B))
-        else:
-            tt(y, tmp, bg, Op.add)
-            tt(tmp, y, P(1, 0, B), Op.subtract)
-            tt(tmp, tmp, z, Op.mult)
-            tt(v("M1"), tmp, xj, Op.mult)
-        dma("y", ext("ys", B * t, B * t + B), y, out=True)
-        send("z", t + 1, y, v("ZL", B * t, B * t + B))
-        tt(ind(v(Y, 0, ey), v("TL", 12 * t, 12 * t + 12)), yj, v("M1"), Op.subtract)
-        if PED:
-            mm([(P(2, 0, B), v("ID"), cn), (P(2, 0, B), v("IDN"), v(X, ex, ex + B))])
-        else:
-            act(P(2, 0, B), cn)
-            tt(P(2, 0, B), P(2, 0, B), v(X, ex, ex + B), Op.subtract)
-        tt(v("M2"), P(2, 0, B), yk, Op.mult)
-        tt(ind(v("BS"), v("L2", 24 * t, 24 * t + 12)), bg, v("M2"), Op.add)
+        dma(N("oy"), "y", ext("ys", B * t, B * t + B), y, 96 * KB, out=True)
+        send("z", t + 1, [y], v("ZL", B * t, B * t + B), 3, [v("ONE")])
+        for n, (a, b) in enumerate(((0, 128), (128, B)) if split else ((0, B),)):
+            tt(N("sy%d" % n), ind(v(Y, 0, ey), v("TL", 12 * t + a // 16, 12 * t + b // 16)), sub(yj, a, b), v("M1", a, b), Op.subtract)
+        tt(N("sb"), ind(v("BS"), v("L2", 24 * t, 24 * t + 12)), bg, v("M2"), Op.add)
         if t == STEPS - 1:
-            dma("y", ext("fb"), v("BS", 0, A), 3000.0, out=True)
-            dma("y", ext("fc"), v("FC"), out=True)
+            dma("ob", "y", ext("fb"), v("BS", 0, A), 512 * KB, out=True)
+            dma("oc", "y", ext("fc"), v("CL", 6 * B, 7 * B), 96 * KB, out=True)
 
     ints(0)
     for t in range(STEPS + 1):
@@ -448,92 +453,67 @@ def build(opt):
 
 
 def overlap(x, y):
-    return x[1] == y[1] and x[2] < y[3] and y[2] < x[3] and x[5][0] < y[5][1] and y[5][0] < x[5][1]
+    if not (x[1] == y[1] and x[2] < y[3] and y[2] < x[3] and x[5][0] < y[5][1] and y[5][0] < x[5][1]):
+        return False
+    return x[5][2] == 1 or x[5][2] != y[5][2] or (x[5][0] - y[5][0]) % x[5][2] == 0
 
 
-def schedule(seed=SEED, opt=OPT, mod=MODEL, text=ORDER):
-    ops = build(opt)
-    n = len(ops)
-    fixed = [52 * ABC.index(text[i]) + ABC.index(text[i + 1]) for i in range(0, len(text), 2)]
-    assert len(fixed) in (0, n)
-    rng = np.random.RandomState(seed)
-    LAT = mod[2]
-    noise, look = (0.0, 100.0) if seed == 0 else (rng.choice([300.0, 1000.0, 3000.0]), rng.choice([50.0, 150.0, 300.0, 600.0]))
+def depend(ops):
     hist = {}
     for o in ops:
-        o["c"] = cost(o["cc"], mod)
-        if o["k"] == "a":
-            o["lat"] = mod[5]
         d = set(o["after"])
         for x in o["r"]:
-            for (j, y, w) in hist.get(x[1], ()):
-                if w and overlap(x, y):
-                    d.add(j)
+            d.update(j for (j, y, w) in hist.get(x[1], ()) if w and overlap(x, y))
         for x in o["w"]:
-            for (j, y, w) in hist.get(x[1], ()):
-                if overlap(x, y) and not (w and o["tag"] == "nx" and ops[j]["tag"] == "nx"):
-                    d.add(j)
+            d.update(j for (j, y, w) in hist.get(x[1], ()) if overlap(x, y))
         d.discard(o["n"])
         o["d"] = d
-        o["banks"] = set(x[1] for x in o["r"] + o["w"] if inps(x))
+        o["banks"] = sorted(set((x[1], b) for x in o["r"] + o["w"] if inps(x) for b in range(x[2] // 512, (x[3] - 1) // 512 + 1)))
         for x in o["r"]:
             hist.setdefault(x[1], []).append((o["n"], x, False))
         for x in o["w"]:
             hist.setdefault(x[1], []).append((o["n"], x, True))
-    succ = [[] for _ in range(n)]
-    for o in ops:
-        for j in o["d"]:
-            succ[j].append(o["n"])
-    prio = [0.0] * n
-    for o in reversed(ops):
-        prio[o["n"]] = o["c"] + o["lat"] + LAT + max([prio[s] for s in succ[o["n"]]] + [0.0])
-    prio = [p + noise * rng.rand() for p in prio]
-    left = [len(o["d"]) for o in ops]
-    ready = {j: 0.0 for j in range(n) if left[j] == 0}
-    fin = [0.0] * n
-    free = {}
-    bank = {}
-    order = []
-    lastg = []
-    while ready:
-        est = {}
-        for j in ready:
-            o = ops[j]
-            s = max(free.get(o["e"], 0.0), ready[j])
-            for b in o["banks"]:
-                for e, i in bank.get(b, {}).items():
-                    if e != o["e"]:
-                        s = max(s, fin[i] + LAT)
-            est[j] = s
-        j0 = min(ready, key=lambda j: (est[j], -prio[j]))
-        e0 = ops[j0]["e"]
-        if fixed:
-            j = fixed[len(order)]
-        else:
-            j = max((j for j in ready if ops[j]["e"] == e0 and est[j] <= est[j0] + look), key=lambda j: (prio[j], -j))
+
+
+def expand(ops, pro, loop, post):
+    at = {o["nm"]: o["n"] for o in ops}
+    names = pro.split()
+    for p in range(STEPS + 3):
+        for x in loop.split():
+            nm, dt = x.split(":") if ":" in x else (x, "0")
+            if "%s.%d" % (nm, p + int(dt)) not in post.split():
+                names.append("%s.%d" % (nm, p + int(dt)))
+    order, seen = [], set()
+
+    def emit(j):
+        if j not in seen:
+            seen.add(j)
+            for i in sorted(ops[j]["d"]):
+                emit(i)
+            order.append(j)
+
+    for x in names + post.split() + [o["nm"] for o in ops]:
+        if x in at:
+            emit(at[x])
+    return order
+
+
+def schedule(opt=OPT, pro=PRO, loop=LOOP, post=POST):
+    ops = build(opt)
+    depend(ops)
+    order = expand(ops, pro, loop, post)
+    assert sorted(order) == list(range(len(ops)))
+    pos = {j: i for i, j in enumerate(order)}
+    bank, lastg, cnt, nd = {}, [], {}, 0
+    for j in order:
         o = ops[j]
+        assert all(pos[i] < pos[j] for i in o["d"]), o["nm"]
         for b in o["banks"]:
-            for e, i in bank.get(b, {}).items():
-                if e != o["e"]:
-                    o["d"].add(i)
+            o["d"].update(i for e, i in bank.get(b, {}).items() if e != o["e"])
             bank.setdefault(b, {})[o["e"]] = j
         if o["e"] == "g" and o["k"] == "c":
             o["d"].update(lastg)
             lastg[:] = [j]
-        o["t0"] = est[j]
-        if o["e"] != "x":
-            free[o["e"]] = est[j] + o["c"]
-        fin[j] = est[j] + o["c"] + o["lat"]
-        del ready[j]
-        order.append(j)
-        for s in succ[j]:
-            left[s] -= 1
-            if left[s] == 0:
-                ready[s] = max(fin[i] + LAT for i in ops[s]["d"])
-    cnt = {}
-    nd = 0
-    for j in order:
-        o = ops[j]
         if o["k"] == "c":
             s = "e" + o["e"]
             cnt[s] = cnt.get(s, 0) + 1
@@ -543,9 +523,10 @@ def schedule(seed=SEED, opt=OPT, mod=MODEL, text=ORDER):
             nd += 1
         elif o["k"] == "a":
             o["sig"] = (o["tag"], -1)
+        elif o["k"] == "r":
+            o["sig"] = ("l" + o["i"][0][2]["sem"], -2)
         else:
             o["sig"] = None
-    pos = {j: i for i, j in enumerate(order)}
     known = {}
     for j in order:
         o = ops[j]
@@ -556,12 +537,12 @@ def schedule(seed=SEED, opt=OPT, mod=MODEL, text=ORDER):
         o["waits"] = []
         for i in sorted(o["d"], key=lambda i: -pos[i]):
             s, c = ops[i]["sig"]
-            if s in kn and kn[s] >= c:
+            if i in o.get("soft", ()) or (s in kn and kn[s] >= c):
                 continue
             o["waits"].append((s, c))
             kn[s] = c
             for s2, c2 in ops[i]["clock"].items():
-                if kn.get(s2, -2) < c2:
+                if kn.get(s2, -3) < c2:
                     kn[s2] = c2
         o["clock"] = dict(kn)
     need = {}
@@ -578,7 +559,7 @@ def schedule(seed=SEED, opt=OPT, mod=MODEL, text=ORDER):
         if o["k"] == "c":
             s, c = o["sig"]
             o["inc"] = s if c in renum.get(s, {}) else None
-    return ops, order, max(fin)
+    return ops, order
 
 
 PLAN = []
@@ -602,7 +583,7 @@ def rank_program(g, core, T, topo):
         return
     if not PLAN:
         PLAN.append(schedule())
-    ops, order, _ = PLAN[0]
+    ops, order = PLAN[0]
     cores = list(T.cores)
     N = len(cores)
     nxt, prv = cores[(rank + 1) % N], cores[(rank - 1) % N]
@@ -625,28 +606,32 @@ def rank_program(g, core, T, topo):
     def half(x, h):
         return ap(v(x[1], x[2] + h * H, x[2] + h * H + H))
 
+    def transfer(kw, h, to, mask):
+        srcs = [half(x, h) for x in kw["s"]] + [ap(x) for x in kw["w"]]
+        sem, dst = T.sem[kw["sem"]], half(kw["d"][0], h)
+        if kw["alu"]:
+            return RemoteDMATransfer(dst_ids=[to], dma_engine_mask=mask, remote_sem=sem, srcs=srcs, dsts=[dst], alu_op=kw["alu"])
+        return RemoteDMATransfer(dst_ids=[to], dma_engine_mask=mask, remote_sem=sem, src=srcs[0], dst=dst)
+
     calls = {
         "matmul": lambda q: q.matmul, "activation": lambda q: q.activation, "dma_start": lambda q: q.dma_start,
         "tensor_tensor": lambda q: q.tensor_tensor, "tensor_scalar": lambda q: q.tensor_scalar,
         "tensor_copy": lambda q: q.tensor_copy, "memset": lambda q: q.memset, "iota": lambda q: q.iota,
         "tensor_tensor_scan": lambda q: q.tensor_tensor_scan, "affine_select": lambda q: q.affine_select,
+        "tensor_reduce": lambda q: q.tensor_reduce,
     }
-    sent = outs = 0
+    sent, outs = [], 0
     for j in order:
         o = ops[j]
         if o["k"] == "a":
             continue
         q = Q[o["e"]]
         for (s, c) in o["waits"]:
-            q.wait_ge(T.sem[s], arrive if c < 0 else c)
+            q.wait_ge(T.sem[s], {-1: arrive, -2: 2 * k}.get(c, c))
         if o["k"] == "r":
-            _, a, kw = o["i"][0]
-            src, dst, sem = a[1], kw["d"][0], T.sem[kw["sem"]]
-            g.remote_dma_fused([
-                RemoteDMATransfer(dst_ids=[idn], dma_engine_mask=mn, remote_sem=sem, src=half(src, 0), dst=half(dst, 0)),
-                RemoteDMATransfer(dst_ids=[idp], dma_engine_mask=mp, remote_sem=sem, src=half(src, 1), dst=half(dst, 1)),
-            ], local_sem=T.sem.sent)
-            sent += 2 * k
+            kw = o["i"][0][2]
+            g.remote_dma_fused([transfer(kw, 0, idn, mn), transfer(kw, 1, idp, mp)], local_sem=T.sem[o["sig"][0]])
+            sent.append(o["sig"][0])
             continue
         for (m, a, kw) in o["i"]:
             ins = calls[m](q)(*[ap(x) for x in a], **{n: ap(x) for n, x in kw.items()})
@@ -658,5 +643,6 @@ def rank_program(g, core, T, topo):
         else:
             ins.then_inc(T.sem.outs, 16)
             outs += 16
-    g.wait_ge(T.sem.sent, sent)
+    for s in sent:
+        g.wait_ge(T.sem[s], 2 * k)
     g.sync.wait_ge(T.sem.outs, outs)

@@ -5,7 +5,7 @@ from concourse.mybir import AluOpType as Op, ActivationFunctionType as Fn, AxisL
 A, W0, B, STEPS = 1024, 2048, 192, 6
 H = B // 2
 CEN = 1408
-SUM0 = 16 * CEN
+SUM0 = CEN
 BIG = 3072.0
 TW = B + W0 + 3 * B
 EOFF = [sum(B - 16 * q for q in range(m)) for m in range(13)]
@@ -20,11 +20,11 @@ def _s(n, d):
 SCRATCH = {
     "U": _s(TW, F32), "V": _s(TW, F32), "BS": _s(A + B, F32), "IT": _s(A + B, F32), "OT": _s(A + B, F32),
     "UB": _s(W0 + B, BF), "VB": _s(W0, BF), "BSB": _s(A, BF), "UI": _s(A, I32), "VO": _s(A, I32), "NX": _s(2 * A, I32),
-    "ADI": _s(16, I32), "RI": _s(6 * B, I32), "R": _s(6 * B, BF), "ZS": _s(B, BF), "TG": _s(B, BF), "D0": _s(B, F16),
+    "ADI": _s(16, I32), "RI": _s(216, I32), "RB": _s(360, BF), "NEG": _s(72, BF), "ZU": _s(64, F32), "R": _s(6 * B, BF), "ZS": _s(B, BF), "TG": _s(B, BF), "D0": _s(B, F16),
     "PI": _s(2, I32), "LI": _s(2, I32), "COL": _s(16, F32), "IJ": _s(B, BF), "JL": _s(256, BF), "JH": _s(128, BF),
-    "DG": _s(B, BF), "BO": _s(128, BF), "BOH": _s(128, F16), "WW": _s(288, F16),
+    "DG": _s(B, BF), "BO": _s(128, BF), "WW": _s(288, BF),
     "ID": _s(128, F32), "ID16": _s(128, F32), "IB": _s(128, BF), "JP": _s(128, BF), "JN": _s(128, BF),
-    "IH": _s(128, F16), "IN": _s(128, F16), "J5": _s(128, BF), "BOW": _s(12 * 128, BF),
+    "IN": _s(128, BF), "J5": _s(128, BF), "BOW": _s(12 * 128, BF),
     "RST": _s(B, BF), "RS2": _s(1024, BF), "SS": _s(1024, F32), "ONE": _s(H, F32),
     "IW": _s(12, F32), "ML": _s(12, U16), "DC": _s(108, F16), "IW16": _s(144, F32), "IW17": _s(144, F32),
     "W3": _s(432, BF), "CONE": _s(432, BF), "QQ": _s(640, BF), "QI": _s(256, BF), "L2P": _s(256, BF),
@@ -42,22 +42,26 @@ SCRATCH = {
 }
 for _b in (0, 1, 2, 5, 6, 7):
     SCRATCH["P%d" % _b] = ("psum", [128, 512], F32)
-NDMA = 48
+NDMA = 52
 SEMAPHORES = (["ev", "es", "et", "eg", "outs"] + ["d%d" % i for i in range(NDMA)]
               + ["%s%s%d" % (w, k, t) for w in ("m", "lm") for k in "acz" for t in range(1, STEPS + 1)])
 
 OPT = {
-    "MA": 8, "MG": 7,
-    "IDX": "v",
+    "MA": 8, "MG": 7, "ML": 7,
+    "IDX": "s",
     "CLIP": "s",
     "CONV": "v",
-    "NA": 3,
+    "SEL": "m",
+    "HALF": "",
+    "SCAN": 5,
+    "VC": "ID ID16 JP JN L16 IW17 BOW7 BOW8 BOW9 BOW10 BOW11 z.0",
+    "NA": 6,
     "ST": True,
     "SPLIT": True,
 }
-PRO = """lr3 fR lnx11 fQI fQQ JL PI lnx10 lad lr0 DG lr1 LI fH lr2 OFFL LANE PF WROW lvo BO GRP ML QI L2P lui fONE W96 pD lr4 fDC IB WCOL RS2a WT BOH IN lvt Ri ka.0 lnx5 D0 RS2b al.0 Ql Rk lnx2 qc.0 pK W3 lcs lzs ID EA7.0 EA1.0 lut ltg pH lnx9 Qq AD0 IW Qc1 IH nc.0 Rq PY0.0 pc.0 EA10.0 Qn0 lnx14 lnx4 lnx0 Qc2 EA11.0 WH lnx3 lnx6 Qc0 EA8.0 lnx1 ID16 WR2 EA4.0 IJ EA0.0 mx.0 pp.0 HL PR0.0 PY1.0 lnx15 DCn0 lnx13 sd.0 lnx8 vs.0 lnx7 lnx12 EA6.0 fWW JP ix.0 ag.0 IW17 JH cV pw.0 IW16 senda.0 Qk S0.0 pq.0 L16 DCa0 EAm.0 pd.0 EA9.0 EA3.0 RST THR JN EA5.0 EA2.0 Z0.0 W0 nm.0 PR1.0 Qn1 BOW7 ls.0 rq.0 tg BOW9 pl.0 LKJ PY2.0 EAs.0 z.0 EAc.0 bg.0 EG7.0 EG8.0 BOW8 EG9.0 EG2.0 EG0.0 EG4.0 l2.0 EG11.0 EG1.0 EG10.0 BOW10 lbs EG3.0 EG6.0 f1 EG5.0 kq.0 S1.0 PR2.0 wj.0 t0.0 y0.0 IT EGs.0 e0.0 EGr.0 EGm.0 dd.0 m2.0 bt.0 EGc.0 S2.0 BOW11 yj.0 sn.0 Z1.0 c0 EA6.1 m0.0 pa.1 al.1 EA9.1 ka.1 EA1.1 EA7.1 qc.1 sendc.0 EA2.1 pc.1 EA10.1 Qn2 EA8.1 Z2.0 y1.0 nc.1 tl.0 EA5.1 oy.0 cx.1 EA11.1 t1.0 cB sendz.0 PY0.1 DCa2 sd.1 e1.0 EA0.1 pd.1 sy0.0 pt.0 pw.1 m1.0 EAm.1 PY1.1 EAs.1 sy1.0 EA3.1 EA4.1 DCa1 OT pp.1 mx.1 pq.1 PR0.1 DCn1 DCn2 cx.0 S0.1 EAr.1 cU"""
-LOOP = """S0 PR0 pd vs EAs rs pl ix EAc ls ag PR1 l2 Z0 rq PY2 EG11 senda sb:-1 kq dd nm Z1 EA7 EG2 EG3 EG1 EG0 EG6 S1 EG4 EG9 EG5 zt EG10 EG8 EGr EGm pa:1 PR2 S2 sendc t0 sn z yj EG7 wj y0 bt EGs bg EGc EA3:1 e0 al:1 EA10:1 ka:1 EA9:1 m2 EA1:1 EA5:1 pt m0 Z2 tl pw:1 qc:1 EA11:1 PY0:1 EAr:1 cx:1 sy0 t1 nc:1 sd:1 EA8:1 EA2:1 EA4:1 PY1:1 e1 oy y1 EA6:1 pc:1 sendz m1 EAm:1 sy1 mx:1 pq:1 pp:1 EA0:1"""
-POST = """PR0.5 S0.5 vs.5 EAc.5 rs.5 ix.5 ag.5 senda.5 ls.5 rq.5 nm.5 PR1.5 PY2.5 pl.5 kq.5 l2.5 sb.4 EG11.5 yj.5 Z1.5 EG6.5 EG7.5 EG3.5 EGr.5 Z0.5 EG9.5 EG5.5 dd.5 EG4.5 cx.5 EG2.5 zt.5 EG8.5 EG0.5 sendc.5 z.5 EG1.5 EGm.5 PR2.5 m2.5 pa.6 S1.5 t0.5 wj.5 y0.5 bg.5 EGs.5 EG10.5 bt.5 Z2.5 EGc.5 S2.5 e0.5 sb.5 m0.5 t1.5 tl.5 e1.5 sy0.5 m1.5 oy.5 ob al.6 sn.5 sy1.5 sendz.5 oc qc.6 PY0.6 pc.6 pt.5 S0.6 S1.6 Z0.6 PR0.6 y1.5 PY1.6 PY2.6 PR2.6 PR1.6 bg.6 S2.6 zt.6 z.6 t1.6 t0.6 y1.6 oy1.6 Z1.6 y0.6 oy0.6"""
+PRO = """JL lr2 fH fONE fQQ lr1 PI fQI fR IJ LI LANE lad lr0 lui lvo QI JH Ri Rq lvt Rn1 Rn0 PF GRP IB ML lnx15 fWW DG Rk Rd3 Rd4 Rd2 Rd0 L2P Rd1 Ql lut lnx9 lnx6 lnx0 lnx11 IW lnx3 lzs lbs lnx5 lnx12 lnx2 OFFL WROW lnx4 lnx13 lnx10 lnx8 lnx14 lnx1 lnx7 ltg lcs al.0 pc.0 qc.0 D0 Qq W3 Qk WT BO pD AD0 W96 IN nc.0 ka.0 IT RST fDC IW16 pd.0 J5 WCOL EA10.0 EA4.0 JP EA0.0 cV EA7.0 W0 EA5.0 EA1.0 PY0.0 EA6.0 WH pw.0 mk.0 mx.0 my.0 sd.0 EA8.0 ID pH HL WR2 pp.0 EA9.0 EA2.0 PY1.0 BOW8 pw.1 DCn0 THR BOW11 EA3.0 ID16 z.0 EA11.0 vs.0 pv.0 L16 DCa0 PR0.0 ix.0 EAm.0 ls.0 ag.0 pq.0 PY2.0 JN EAs.0 BOW7 BOW9 PY3.0 pK S0.0 tg senda.0 PY4.0 wj.0 EAc.0 IW17 LKJ pl.0 Qc0 rq.0 Qn0 PY5.0 Z0.0 PR1.0 BOW10 pk.0 kq.0 S1.0 Z1.0 mk.1 l2.0 EG10.0 EG11.0 EG9.0 EG2.0 EG7.0 EG8.0 EGr.0 Qc1 yj.0 bg.0 EG0.0 nm.0 EG3.0 EG4.0 EG5.0 EG6.0 sn.0 EG1.0 EGm.0 c0 PR2.0 pa.1 t0.0 EGs.0 al.1 RS2 y0.0 RS3 ka.1 S2.0 OT dd.0 e0.0 EGc.0 pt.0 qc.1 EA10.1 EA11.1 pc.1 PY1.1 bt.0 m0.0 EA1.1 EA7.1 EA6.1 m2.0 EA3.1 tl.0 nc.1 sy0.0 Z2.0 mx.1 t1.0 EA2.1 EA0.1 EA5.1 EA9.1 PY0.1 pd.1 pk.1 EA8.1 e1.0 my.1 m1.0 EA4.1 sd.1 DCa1 EAr.1 Qc2 PY2.1 sy1.0 pp.1 vs.1 y1.0 EAm.1 PY3.1 EAs.1 DCn2 cB cU f1 RS1 sendc.0 pq.1 pv.1 ix.1 Qn1 oy.0 Qn2 ag.1 cx.0 sendz.0 cx.1 RS0 DCa2 DCn1"""
+LOOP = """PR0 vs PY3 pk EAm EAs nm EAc pv ix ag pw:1 ls rs rq PY4 PY5 sendz:-1 oy:-1 S0 PR1 pl kq EG7 Z0 S1 Z1 EG10 EG8 sb:-1 EG11 zt EG9 mk:1 EG5 EG0 EGr cx z l2 EG4 bg sn yj EG3 EG6 EG1 EG2 PR2 EGm EGs t0 senda dd sendc y0 wj pa:1 al:1 m2 e0 EGc bt ka:1 m0 EA0:1 qc:1 S2 EA1:1 pc:1 PY1:1 pt PY0:1 EA8:1 nc:1 Z2 tl EA6:1 mx:1 sy0 t1 my:1 e1 pd:1 pq:1 y1 EA2:1 EA9:1 EA11:1 EA10:1 sd:1 pp:1 EAr:1 PY2:1 m1 EA3:1 EA4:1 sy1 EA5:1 EA7:1"""
+POST = """PR0.5 oy.4 S0.5 rq.5 PY5.5 nm.5 EAc.5 PY4.5 PR1.5 pl.5 kq.5 sb.4 EG8.5 EG9.5 EG11.5 zt.5 EG7.5 z.5 EG2.5 EG10.5 bg.5 EG0.5 Z0.5 EG3.5 S1.5 l2.5 Z1.5 EG4.5 EG6.5 EG5.5 EGr.5 EG1.5 yj.5 sn.5 PR2.5 t0.5 bt.5 EGm.5 S2.5 EGs.5 zu.5 pa.6 EGc.5 pt.5 y0.5 wj.5 e0.5 t1.5 tl.5 m0.5 e1.5 y1.5 sy0.5 m1.5 dd.5 sy1.5 m2.5 al.6 qc.6 sendc.5 pc.6 PY0.6 PY1.6 PY3.6 PY2.6 PR0.6 PY5.6 PY4.6 PR1.6 sendz.5 oy.5 PR2.6 S0.6 sb.5 S2.6 oc ob Z0.6 zt.6 S1.6 z.6 Z1.6 bg.6 t0.6 t1.6 y0.6 oy0.6 y1.6 oy1.6"""
 
 
 def v(name, a=0, b=None, st=1, p=(0, 128, 1)):
@@ -146,6 +150,8 @@ def build(opt):
         return vec(nm, "tensor_tensor_scan", o, x, y, init, op0, op1)
 
     def act(nm, o, x, f=Fn.Identity, **k):
+        if nm in opt["VC"].split():
+            return ts(nm, o, x, k.get("scale", 1.0), Op.mult, k.get("bias", 0.0), Op.add)
         if o[0] == "i":
             c = ("si", 0, 0, ncol(o), 0)
         elif x[0] == "i":
@@ -196,8 +202,8 @@ def build(opt):
     KB = 1024
 
     dma("lad", "y", v("ADI", 0, 12), ext("ad"), 6 * KB)
-    for n, (nm, p0) in enumerate((("sl", 0), ("tr", 8), ("hv", 16), ("sl", 32), ("tr", 40))):
-        dma("lr%d" % n, "s" if n % 2 else "y", v("RI", p=(p0, p0 + 8)), ext(nm), 36 * KB)
+    for n, nm in enumerate(("sl", "tr", "hv")):
+        dma("lr%d" % n, "s", v("RI", 72 * n, 72 * n + 72), ext(nm), 36 * KB)
     dma("lvo", "y", v("VO"), ext("vo"), 512 * KB)
     dma("lvt", "y", v("VB"), ext("vt"), 512 * KB)
     dma("lui", "y", v("UI"), ext("ui"), 512 * KB)
@@ -216,30 +222,28 @@ def build(opt):
     iota("IJ", v("IJ"), [[1, B]])
     iota("JH", v("JH"), [[16, 8], [0, 16]])
     iota("IW16", v("IW16"), [[0, 12], [256, 12]])
-    fill("fR", v("R", p=(0, 32)), -1.0)
+    fill("fR", v("NEG"), -1.0)
     fill("fQQ", v("QQ", 0, 256, p=(0, 32)), 0.0)
     fill("fQI", v("QI", p=(32, 48)), -4096.0)
-    fill("fONE", v("CONE", p=(0, 32)), 1.0)
+    fill("fONE", v("CONE"), 1.0)
     fill("fWW", v("WW"), 0.0)
-    fill("fDC", v("DC"), float(B))
+    iota("fDC", v("DC"), [[0, 108]], B)
     fill("fH", v("CHALF"), 0.5)
-    fill("f1", v("ONE"), 1.0)
+    iota("f1", v("ONE"), [[0, H]], 1)
     ts("LI", v("LI"), v("PI"), 15, Op.bitwise_and)
     cp("LANE", LANE, v("LI", 0, 1))
     cp("PF", PF, v("PI", 0, 1))
     tt("GRP", GRP, PF, LANE, Op.subtract)
     ts("BO", v("BO"), v("JH"), GRP, Op.is_equal)
-    cp("BOH", v("BOH"), v("BO"))
     cp("WH", v("WW", 15, 128, 16), v("BO", 0, 128, 16))
     ts("DG", v("DG"), v("JL", 0, B), LANE, Op.is_equal)
-    ts("RST", v("RST"), v("JL", 0, B), 0.5, Op.is_gt)
+    gp("RST", "affine_select", v("RST", 0, B), v("CONE", 0, B), [[0, 12], [1, 16]], Op.not_equal, 0.0, 0, 0)
     ts("IB", v("IB"), v("IJ", 0, 128), PF, Op.is_equal)
     cp("W0", v("WW", 144 + 15, 144 + 128, 16), v("IB", 0, 128, 16))
     act("ID", v("ID"), v("IB"))
     act("ID16", v("ID16"), v("IB"), scale=16.0)
-    ts("JP", v("JP"), v("IB"), BIG, Op.mult)
-    ts("JN", v("JN"), v("IB"), -BIG, Op.mult)
-    cp("IH", v("IH"), v("IB"))
+    act("JP", v("JP"), v("IB"), scale=BIG)
+    act("JN", v("JN"), v("IB"), scale=-BIG)
     ts("IN", v("IN"), v("IB"), -1.0, Op.mult)
     if opt["IDX"] == "s":
         ts("J5", v("J5"), v("IB"), 512.0, Op.mult)
@@ -250,7 +254,7 @@ def build(opt):
     tt("WT", v("WT"), v("WROW", 96, 112), v("DG", 0, 16), Op.mult)
     vec("W96", "tensor_reduce", W96, v("WT"), Ax.X, Op.add)
     ts("WCOL", v("WCOL"), v("WROW", 0, B, 16), W96, Op.mult)
-    for m in range(min(MA, MG), 12):
+    for m in range(min(MA, MG, opt["ML"]), 12):
         act("BOW%d" % m, v("BOW", 128 * m, 128 * m + 128), v("BO"), scale=v("WCOL", m, m + 1))
     cp("ML", v("ML"), v("IJ", 0, 12))
     ts("IW", v("IW"), v("IJ", 0, B, 16), LANE, Op.add)
@@ -259,17 +263,21 @@ def build(opt):
         act("DCn%d" % m, v("DC", 36 * m + 12, 36 * m + 24), v("IW"), bias=W0 + B * m - BIG)
     act("L16", L16, LANE, scale=16.0)
     act("IW17", v("IW17"), v("IW16"), bias=L16)
-    dma("Ri", "s", v("R", p=(25, 26)), v("IJ", p=(0, 6)), 3 * KB)
-    act("Rk", v("R", p=(0, 24)), v("RI", p=(0, 24)))
-    act("Rq", v("R", p=(32, 48)), v("RI", p=(32, 48)), Fn.Square)
+    dma("Ri", "y", v("R", p=(25, 26)), v("IJ", p=(0, 6)), 3 * KB)
+    dma("Rn0", "y", v("R", p=(24, 25)), v("NEG", p=(0, 16)), 3 * KB)
+    dma("Rn1", "y", v("R", p=(26, 32)), v("NEG", p=(0, 96)), 14 * KB)
+    cp("Rk", v("RB", 0, 216), v("RI"))
+    act("Rq", v("RB", 216, 360), v("RI", 0, 144), Fn.Square)
+    for n, p0 in enumerate((0, 8, 16, 32, 40)):
+        dma("Rd%d" % n, "y", v("R", p=(p0, p0 + 8)), v("RB", 72 * n, 72 * n + 72), 18 * KB)
     act("L2P", v("L2P", p=(0, 1)), v("JL", p=(0, 1)), Fn.Square, scale=64.0)
     dma("Ql", "s", v("QQ", 0, 256, p=(24, 25)), v("L2P", p=(0, 1)), KB)
     act("QI", v("QI", p=(0, 16)), v("JL", p=(0, 16)), Fn.Silu, scale=8192.0)
     gp("Qk", "affine_select", v("QQ", 0, 256, p=(0, 16)), v("QI", p=(0, 16)), [[-1, 16], [0, 16]], Op.is_equal, 0.0, 0, 1)
     gp("Qq", "affine_select", v("QQ", 0, 256, p=(32, 48)), v("QI", p=(32, 48)), [[-1, 16], [0, 16]], Op.is_equal, 0.0, 0, 1)
     for m in range(3):
-        ts("Qc%d" % m, col(5 + m), v("ID", 26, 27), -float(W0 + B * m), Op.mult, v("ID", 25, 26), Op.add)
-        ts("Qn%d" % m, v("QQ", 256 + 128 * m, 384 + 128 * m, p=(0, 48)), v("QQ", 0, 128, p=(0, 48)), col(5 + m, (0, 48)), Op.add)
+        act("Qc%d" % m, col(5 + m), v("ID", 26, 27), scale=-float(W0 + B * m), bias=v("ID", 25, 26))
+        act("Qn%d" % m, v("QQ", 256 + 128 * m, 384 + 128 * m, p=(0, 48)), v("QQ", 0, 128, p=(0, 48)), bias=col(5 + m, (0, 48)))
     gp("W3", "affine_select", v("W3", p=(0, 32)), v("CONE", p=(0, 32)), [[128, 3], [1, 144]], Op.is_equal, 0.0, -15, -16)
     mm("pH", pick(P(2, 144, 216), "W3", "R", 0, 6 * B, p=(0, 24), w0=288))
     act("HL", v("HL"), P(2, 144, 216), scale=-2.0)
@@ -277,14 +285,15 @@ def build(opt):
     tt("LKJ", v("LKJ"), P(2, 0, 144), v("IW17"), Op.add)
     gp("IT", "affine_select", v("IT", 0, A), v("UI"), [[0, A]], Op.is_ge, 0.0, 0, 0)
     gp("OT", "affine_select", v("OT", 0, A), v("VO"), [[0, A]], Op.is_ge, 0.0, 0, 0)
-    act("c0", v("CL", 0, B), v("UB", W0, W0 + B))
-    act("tg", P(1, 0, B), v("TG"))
+    dma("c0", "g", v("CL", 0, B), ext("cs"), 96 * KB)
+    mm("tg", [(P(1, 0, B), v("IB"), v("TG"))])
     act("z.0", v("ZC", 0, B), v("ZS"), scale=0.0625)
     tt("D0", v("D0"), ind(v("ADI", 0, 12), v("ML")), v("DG"), Op.mult)
-    mm("pD", [(P(5, 0, B), v("BOH"), v("D0"))])
+    mm("pD", [(P(5, 0, B), v("BO"), v("D0"))])
     act("AD0", v("AD", 0, B), P(5, 0, B))
-    fill("RS2a", v("RS2"), 1.0)
-    fill("RS2b", v("RS2", 0, 1024, 16), 0.0)
+    for n in range(4):
+        gp("RS%d" % n, "affine_select", v("RS2", 256 * n, 256 * n + 256), v("CONE", 0, 256), [[0, 16], [1, 16]],
+           Op.not_equal, 0.0, 0, 0)
 
     def first(E, t, rep, key, bank, sg, ms):
         e0 = NE * (t % 2)
@@ -336,11 +345,21 @@ def build(opt):
         ph, qh = v("NC", nc, nc + B), v("NC", nc + B, nc + 2 * B)
         rt = v("R", B * t, B * t + B, p=(0, 48))
         Q = lambda n: v("QQ", 128 * n, 128 * n + 128, p=(0, 48))
-        mm(N("pd"), [(P(5, 0, B), v("IH"), ph), (P(5, 0, B), v("IN"), qh)])
+        mm(N("pd"), [(P(5, 0, B), v("IB"), ph), (P(5, 0, B), v("IN"), qh)])
         act(N("sd"), v("MX", mx + 3 * B, mx + 4 * B), P(5, 0, B), Fn.Sign, scale=1.0 if t % 2 == 0 else -1.0, bias=-0.5)
-        mm(N("pw"), *[[(PW(128 + B * n, 320 + B * n), v("IH"), x), (PW(128 + B * n, 320 + B * n), Q(q), rt)]
-                      for n, (x, q) in enumerate(((ph, 0), (qh, 1), (ph, 1)))], [(PW(704, 896), Q(2 + t // 2), rt)])
-        ts(N("mx"), v("MX", mx, mx + 3 * B), PW(128, 704), -float(CEN), Op.max)
+        if opt["SEL"] == "m":
+            SUM0 = CEN
+            mm(N("pw"), [(PW(0, B), Q(0), rt)], [(PW(B, 2 * B), Q(1), rt)])
+            act(N("mk"), PW(0, 2 * B), PW(0, 2 * B), Fn.Relu, scale=2.0 ** -12, bias=1.0)
+            mm(N("pk"), [(PW(704, 896), Q(2 + t // 2), rt)])
+            tt(N("mx"), v("MX", mx, mx + 2 * B), v("NC", nc, nc + 2 * B), PW(0, 2 * B), Op.mult)
+            tt(N("my"), v("MX", mx + 2 * B, mx + 3 * B), ph, PW(B, 2 * B), Op.mult)
+        else:
+            SUM0 = 16 * CEN
+            mm(N("pw"), *[[(PW(128 + B * n, 320 + B * n), v("IB"), x), (PW(128 + B * n, 320 + B * n), Q(q), rt)]
+                          for n, (x, q) in enumerate(((ph, 0), (qh, 1), (ph, 1)))])
+            mm(N("pk"), [(PW(704, 896), Q(2 + t // 2), rt)])
+            ts(N("mx"), v("MX", mx, mx + 3 * B), PW(128, 704), -float(CEN), Op.max)
         tt(N("nm"), v("NM"), PW(704, 896), pc, Op.max)
         mm(N("pp"), pick(P(5, B, B + 48), "WW", "MX", mx, mx + 4 * B)
            + [(P(5, B + 36, B + 48), v("IB"), v("HL", 12 * t, 12 * t + 12))])
@@ -358,17 +377,17 @@ def build(opt):
         if t >= 2:
             act(N("rs"), v("SG", sg + 12, sg + 24), P(5, B + 24, B + 36), Fn.Relu, bias=float(SUM0 + 1 - W0 - B * (t // 2 - 1)))
         rq = v("RQ", B * (t % 2), B * (t % 2) + B)
-        mm(N("pq"), [(P(5, 240, 240 + B), v("BOH"), v("MX", mx + B, mx + 2 * B))])
+        mm(N("pq"), [(P(5, 240, 240 + B), v("BO"), v("MX", mx + B, mx + 2 * B))])
         act(N("rq"), rq, P(5, 240, 240 + B), bias=float(SUM0 + B))
         nb = first("EA", t, rep, wf, 6, "SA", MA if t else 12)
         dc = 36 * (t // 2)
-        mm(N("pl"), [(P(6, B, B + 36), v("IH"), v("DC", dc, dc + 36)), (P(6, B, B + 12), v("JP"), nb),
+        mm(N("pl"), [(P(6, B, B + 36), v("IB"), v("DC", dc, dc + 36)), (P(6, B, B + 12), v("JP"), nb),
                      (P(6, B + 12, B + 24), v("JP"), nb), (P(6, B + 24, B + 36), v("JN"), nb)]
            + ([(P(6, B + 24, B + 36), v("JN"), v("SG", sg + 12, sg + 24))] if t >= 2 else []))
         tt(N("l2"), v("L2", 24 * t, 24 * t + 24), P(6, B, B + 24), v("LST", ls, ls + 24), Op.max)
         tt(N("kq"), v("WF", wf + 12, wf + 24), P(6, B + 24, B + 36), v("LST", ls + 24, ls + 36), Op.add)
         act(N("sn"), ind(v(PT), v("L2", 24 * t, 24 * t + 12)), v("NM"), Fn.Silu)
-        ng = first("EG", t, rq, wf + 12, 7, "SO", MG)
+        ng = first("EG", t, rq, wf + 12, 7, "SO", MG if t < STEPS - 1 else opt["ML"])
         mm(N("pt"), [(P(7, B, B + 12), v("ID"), v("WF", wf + 12, wf + 24)), (P(7, B, B + 12), v("JN"), ng)])
         tt(N("tl"), v("TL", 12 * t, 12 * t + 12), P(7, B, B + 12), v("IW"), Op.max)
 
@@ -391,8 +410,11 @@ def build(opt):
         for n in range(3):
             d = 64 * n
             a, b = 16 * d, 16 * (d + 64)
-            tt(N("PR%d" % n), v("PR", a, b), ind(xw, v("OFFS", of + d, of + d + 64)), v("PY", py + a, py + b), Op.mult)
-            if last and n == 2:
+            w = 32 if N("PR%d" % n) in opt["HALF"].split() else 64
+            for c in range(d, d + 64, w):
+                tt(N(("PR%d" if c == d else "PQ%d") % n), v("PR", 16 * c, 16 * (c + w)), ind(xw, v("OFFS", of + c, of + c + w)),
+                   v("PY", py + 16 * c, py + 16 * (c + w)), Op.mult)
+            if t >= opt["SCAN"] and n == 2:
                 scan(N("S2"), v("SS"), v("RS2"), v("PR", a, b), 0.0, Op.mult, Op.add)
             else:
                 o = P(2, 0, 64) if split and n == 2 else P(0, d, d + 64)
@@ -420,8 +442,12 @@ def build(opt):
             act(N("yj"), yj, ind(pw, v("LKJ", 72 + 12 * t, 84 + 12 * t)), scale=16.0)
             tt(N("m2"), v("M2"), ind(pw, v("LKJ", 12 * t, 12 * t + 12)), dd, Op.mult)
         for n, (a, b) in enumerate(((0, 128), (128, B)) if split else ((0, B),)):
-            s = P(0, a, b) if n == 0 else v("SS", 15, 1024, 16) if last else P(2, 0, 64)
-            tt(N("t%d" % n), sub(tmp, a, b), s, sub(z, a, b), Op.mult)
+            s = P(0, a, b) if n == 0 else v("SS", 15, 1024, 16) if t >= opt["SCAN"] else P(2, 0, 64)
+            zz = sub(z, a, b)
+            if n == 1 and opt["SCAN"] <= t < STEPS:
+                act(N("zu"), v("ZU"), zz, scale=16.0)
+                zz = v("ZU")
+            tt(N("t%d" % n), sub(tmp, a, b), s, zz, Op.mult)
             tt(N("y%d" % n), sub(y, a, b), sub(tmp, a, b), sub(bg, a, b), Op.add)
             if n == 1 and opt["ST"] and not last:
                 tt(N("bt"), v("BT"), sub(bg, a, b), P(1, a, b), Op.subtract)

@@ -1,15 +1,13 @@
-import numpy as np
 from concourse.bass import DstId, RemoteDMATransfer
 from concourse.mybir import AluOpType as Op, ActivationFunctionType as Fn, AxisListType as Ax
 
 A, W0, B, STEPS = 1024, 2048, 192, 6
 H = B // 2
+RUN = 64
 CEN = 1408
-SUM0 = CEN
 BIG = 3072.0
 TW = B + W0 + 3 * B
-EOFF = [sum(B - 16 * q for q in range(m)) for m in range(13)]
-NE = EOFF[12]
+NE = sum(B - 16 * m for m in range(12))
 F32, BF, I32, U16, F16 = "float32", "bfloat16", "int32", "uint16", "float16"
 
 
@@ -20,48 +18,62 @@ def _s(n, d):
 SCRATCH = {
     "U": _s(TW, F32), "V": _s(TW, F32), "BS": _s(A + B, F32), "IT": _s(A + B, F32), "OT": _s(A + B, F32),
     "UB": _s(W0 + B, BF), "VB": _s(W0, BF), "BSB": _s(A, BF), "UI": _s(A, I32), "VO": _s(A, I32), "NX": _s(2 * A, I32),
-    "ADI": _s(16, I32), "RI": _s(216, I32), "RB": _s(360, BF), "NEG": _s(72, BF), "ZU": _s(64, F32), "R": _s(6 * B, BF), "ZS": _s(B, BF), "TG": _s(B, BF), "D0": _s(B, F16),
+    "ADI": _s(16, I32), "RI": _s(216, I32), "RB": _s(360, BF), "NEG": _s(72, BF), "R": _s(6 * B, BF),
+    "ZS": _s(B, BF), "TG": _s(B, BF), "D0": _s(B, F16), "RH": _s(B, I32), "RG": _s(B, BF),
+    "NN": _s(128, I32), "G8": _s(128, BF), "L8": _s(2, I32), "LO": _s(12, I32), "LU": _s(12, U16), "G0": _s(B, F16),
+    "AB": _s(B, BF), "SV": _s(B, BF),
     "PI": _s(2, I32), "LI": _s(2, I32), "COL": _s(16, F32), "IJ": _s(B, BF), "JL": _s(256, BF), "JH": _s(128, BF),
-    "DG": _s(B, BF), "BO": _s(128, BF), "WW": _s(288, BF),
-    "ID": _s(128, F32), "ID16": _s(128, F32), "IB": _s(128, BF), "JP": _s(128, BF), "JN": _s(128, BF),
-    "IN": _s(128, BF), "J5": _s(128, BF), "BOW": _s(12 * 128, BF),
-    "RST": _s(B, BF), "RS2": _s(1024, BF), "SS": _s(1024, F32), "ONE": _s(H, F32),
+    "DG": _s(B, BF), "BO": _s(128, BF), "WW": _s(288, BF), "ID": _s(128, F32), "ID16": _s(128, F32), "IB": _s(128, BF),
+    "JP": _s(128, BF), "JN": _s(128, BF), "IN": _s(128, BF), "J5": _s(128, BF), "BOW": _s(12 * 128, BF),
+    "RST": _s(B, BF), "RS2": _s(16 * RUN, BF), "SS": _s(16 * RUN, F32), "ONE": _s(H, F32),
     "IW": _s(12, F32), "ML": _s(12, U16), "DC": _s(108, F16), "IW16": _s(144, F32), "IW17": _s(144, F32),
     "W3": _s(432, BF), "CONE": _s(432, BF), "QQ": _s(640, BF), "QI": _s(256, BF), "L2P": _s(256, BF),
     "WROW": _s(B, BF), "OFFL": _s(B, BF), "THR": _s(B, BF), "CHALF": _s(B, BF), "WT": _s(16, F32), "WCOL": _s(12, F32),
     "LKJ": _s(144, U16), "HL": _s(72, BF),
     "AD": _s(7 * B, F16), "AG": _s(6 * B, F16), "LST": _s(7 * 48, U16), "WF": _s(6 * 24, F32), "OFFS": _s(7 * 2 * B, U16),
-    "NC": _s(2 * 2 * B, F16), "MX": _s(2 * 4 * B, F16), "RQ": _s(2 * B, U16), "SG": _s(6 * 24, BF), "VT": _s(12, F32),
+    "NC": _s(2 * 2 * B, F16), "MX": _s(2 * 4 * B, F16), "RQ": _s(2 * B, U16), "SG": _s(6 * 24, BF),
     "IX": _s(6 * 12, U16), "NM": _s(B, F32),
     "EA": _s(2 * NE, BF), "EG": _s(2 * NE, BF), "EF": _s(2 * NE, BF), "SA": _s(3 * B, BF), "SO": _s(3 * B, BF),
     "L2": _s(6 * 24, U16), "TL": _s(6 * 12, U16),
     "PY": _s(2 * 16 * B, F32), "PR": _s(16 * B, F32), "YS": _s(7 * B, F32), "ZL": _s(6 * B, F32), "ZC": _s(2 * B, F32),
-    "ZT": _s(B, F32), "DD": _s(6 * B, F32), "CL": _s(7 * B, F32), "BG": _s(2 * B, F32), "WJ": _s(2 * B, F32),
-    "YJ": _s(2 * B, F32), "M1": _s(B, F32), "M2": _s(B, F32), "BT": _s(64, F32),
+    "ZT": _s(B, F32), "ZU": _s(RUN, F32), "DD": _s(6 * B, F32), "CL": _s(7 * B, F32), "BG": _s(2 * B, F32),
+    "WJ": _s(2 * B, F32), "YJ": _s(2 * B, F32), "M1": _s(B, F32), "M2": _s(B, F32), "BT": _s(RUN, F32),
     "PW": ("psum", [128, 1024], F32),
 }
 for _b in (0, 1, 2, 5, 6, 7):
     SCRATCH["P%d" % _b] = ("psum", [128, 512], F32)
-NDMA = 52
+NDMA = 54
 SEMAPHORES = (["ev", "es", "et", "eg", "outs"] + ["d%d" % i for i in range(NDMA)]
               + ["%s%s%d" % (w, k, t) for w in ("m", "lm") for k in "acz" for t in range(1, STEPS + 1)])
 
 OPT = {
-    "MA": 8, "MG": 7, "ML": 7,
-    "IDX": "s",
-    "CLIP": "s",
-    "CONV": "v",
-    "SEL": "m",
-    "HALF": "",
-    "SCAN": 5,
-    "VC": "ID ID16 JP JN L16 IW17 BOW7 BOW8 BOW9 BOW10 BOW11 z.0",
-    "NA": 6,
-    "ST": True,
-    "SPLIT": True,
+    "MA": 8,
+    "MG": 5,
+    "ML": 0,
+    "SCAN": (5, 6),
 }
-PRO = """JL lr2 fH fONE fQQ lr1 PI fQI fR IJ LI LANE lad lr0 lui lvo QI JH Ri Rq lvt Rn1 Rn0 PF GRP IB ML lnx15 fWW DG Rk Rd3 Rd4 Rd2 Rd0 L2P Rd1 Ql lut lnx9 lnx6 lnx0 lnx11 IW lnx3 lzs lbs lnx5 lnx12 lnx2 OFFL WROW lnx4 lnx13 lnx10 lnx8 lnx14 lnx1 lnx7 ltg lcs al.0 pc.0 qc.0 D0 Qq W3 Qk WT BO pD AD0 W96 IN nc.0 ka.0 IT RST fDC IW16 pd.0 J5 WCOL EA10.0 EA4.0 JP EA0.0 cV EA7.0 W0 EA5.0 EA1.0 PY0.0 EA6.0 WH pw.0 mk.0 mx.0 my.0 sd.0 EA8.0 ID pH HL WR2 pp.0 EA9.0 EA2.0 PY1.0 BOW8 pw.1 DCn0 THR BOW11 EA3.0 ID16 z.0 EA11.0 vs.0 pv.0 L16 DCa0 PR0.0 ix.0 EAm.0 ls.0 ag.0 pq.0 PY2.0 JN EAs.0 BOW7 BOW9 PY3.0 pK S0.0 tg senda.0 PY4.0 wj.0 EAc.0 IW17 LKJ pl.0 Qc0 rq.0 Qn0 PY5.0 Z0.0 PR1.0 BOW10 pk.0 kq.0 S1.0 Z1.0 mk.1 l2.0 EG10.0 EG11.0 EG9.0 EG2.0 EG7.0 EG8.0 EGr.0 Qc1 yj.0 bg.0 EG0.0 nm.0 EG3.0 EG4.0 EG5.0 EG6.0 sn.0 EG1.0 EGm.0 c0 PR2.0 pa.1 t0.0 EGs.0 al.1 RS2 y0.0 RS3 ka.1 S2.0 OT dd.0 e0.0 EGc.0 pt.0 qc.1 EA10.1 EA11.1 pc.1 PY1.1 bt.0 m0.0 EA1.1 EA7.1 EA6.1 m2.0 EA3.1 tl.0 nc.1 sy0.0 Z2.0 mx.1 t1.0 EA2.1 EA0.1 EA5.1 EA9.1 PY0.1 pd.1 pk.1 EA8.1 e1.0 my.1 m1.0 EA4.1 sd.1 DCa1 EAr.1 Qc2 PY2.1 sy1.0 pp.1 vs.1 y1.0 EAm.1 PY3.1 EAs.1 DCn2 cB cU f1 RS1 sendc.0 pq.1 pv.1 ix.1 Qn1 oy.0 Qn2 ag.1 cx.0 sendz.0 cx.1 RS0 DCa2 DCn1"""
-LOOP = """PR0 vs PY3 pk EAm EAs nm EAc pv ix ag pw:1 ls rs rq PY4 PY5 sendz:-1 oy:-1 S0 PR1 pl kq EG7 Z0 S1 Z1 EG10 EG8 sb:-1 EG11 zt EG9 mk:1 EG5 EG0 EGr cx z l2 EG4 bg sn yj EG3 EG6 EG1 EG2 PR2 EGm EGs t0 senda dd sendc y0 wj pa:1 al:1 m2 e0 EGc bt ka:1 m0 EA0:1 qc:1 S2 EA1:1 pc:1 PY1:1 pt PY0:1 EA8:1 nc:1 Z2 tl EA6:1 mx:1 sy0 t1 my:1 e1 pd:1 pq:1 y1 EA2:1 EA9:1 EA11:1 EA10:1 sd:1 pp:1 EAr:1 PY2:1 m1 EA3:1 EA4:1 sy1 EA5:1 EA7:1"""
-POST = """PR0.5 oy.4 S0.5 rq.5 PY5.5 nm.5 EAc.5 PY4.5 PR1.5 pl.5 kq.5 sb.4 EG8.5 EG9.5 EG11.5 zt.5 EG7.5 z.5 EG2.5 EG10.5 bg.5 EG0.5 Z0.5 EG3.5 S1.5 l2.5 Z1.5 EG4.5 EG6.5 EG5.5 EGr.5 EG1.5 yj.5 sn.5 PR2.5 t0.5 bt.5 EGm.5 S2.5 EGs.5 zu.5 pa.6 EGc.5 pt.5 y0.5 wj.5 e0.5 t1.5 tl.5 m0.5 e1.5 y1.5 sy0.5 m1.5 dd.5 sy1.5 m2.5 al.6 qc.6 sendc.5 pc.6 PY0.6 PY1.6 PY3.6 PY2.6 PR0.6 PY5.6 PY4.6 PR1.6 sendz.5 oy.5 PR2.6 S0.6 sb.5 S2.6 oc ob Z0.6 zt.6 S1.6 z.6 Z1.6 bg.6 t0.6 t1.6 y0.6 oy0.6 y1.6 oy1.6"""
+PRO = """
+fWW JL lnn lad fQI lr1 lr0 lr2 PI lvo fQQ LI fONE lh LANE PF DG fR GRP IJ JH QI L2P L8 lui lvt IW ML lo fH D0 BO OFFL Rk
+PM C8 Rq Rd3 Rn1 lut al.0 PH Rd0 lu Ql ka.0 Rd4 Rd1 pD Rn0 IW16 RST Qq Ri lnx5 Rd2 lzs W3 G8 lnx14 ltg lnx10 lnx7 Qk fDC
+lnx12 lnx3 lnx15 lnx4 cV lbs lnx9 lnx8 WROW lcs lnx11 lnx13 qc.0 WR2 AD0 ab WT L16 IB W96 WCOL WH THR pc.0 ar G0 Rh EA7.0
+sd.0 lnx2 lnx6 EA1.0 lnx0 lnx1 EA11.0 EA6.0 BOW10 EA9.0 ID16 JN JP EA2.0 EA8.0 EA4.0 W0 EA3.0 IN EA5.0 PY0.0 pu.0 vs.0
+pv.0 BOW8 EA0.0 EA10.0 pw.0 PY1.0 ID ix.0 tg px.0 nc.0 mk.0 Qc0 EAm.0 pK ag.0 PY3.0 DCa0 PR0.0 EAs.0 PY2.0 mx.0 pq.0 rq.0
+BOW9 my.0 IW17 z.0 EAc.0 RS0 senda.0 PY5.0 S0.0 BOW11 Qn0 DCn0 IT pw.1 pp.0 pl.0 mk.1 ls.0 Qc1 PR1.0 PY4.0 pk.0 l2.0 c0
+DCa2 kq.0 EG4.0 Z0.0 S1.0 Z1.0 LKJ EG0.0 EG7.0 EG5.0 J5 EG8.0 EG6.0 EG10.0 nm.0 EG2.0 DCn1 EG1.0 dd.0 EG11.0 EG9.0 EG3.0
+PR2.0 t0.0 bg.0 wj.0 y0.0 e0.0 m0.0 yj.0 EGr.0 EGm.0 sn.0 EGs.0 pa.1 Qn1 DCn2 al.1 S2.0 Z2.0 ka.1 EA5.1 OT m2.0 EA2.1
+DCa1 qc.1 EA11.1 f1 pc.1 PY1.1 EA10.1 EA8.1 PY0.1 EGc.0 bt.0 EA7.1 nc.1 pt.0 EA1.1 EA6.1 mx.1 t1.0 pd.1 EA4.1 tl.0 pH RS1
+my.1 cB sy0.0 e1.0 y1.0 sendc.0 RS3 sy1.0 sd.1 EA9.1 m1.0 Qc2 HL pw.2 pq.1 EA0.1 pk.1 pp.1 sendz.0 EAr.1 PY2.1 Qn2 cx.0
+oy.0 RS2 sy2.0 EA3.1 cx.1 vs.1 EAm.1 cU"""
+LOOP = """
+PR0 vs PY3 nm EAm EAs pv ix ls rs ag mk:1 PY4 rq S0 PY5 EAc pl Z0 PR1 S1 sendc:-1 cx kq EG9 EG8 EG7 Z1 sb:-1 sendz:-1 zt
+EG0 EG1 EG3 l2 EG5 oy:-1 EG6 EG11 EG10 EG4 bg EGr EG2 z yj sn PR2 dd t0 EGm EGs wj y0 m2 senda pa:1 al:1 ka:1 EGc e0 S2
+qc:1 EA0:1 EA1:1 EA6:1 bt pc:1 PY0:1 EA11:1 PY1:1 m0 pt tl EA8:1 nc:1 Z2 sy0 mx:1 sy1 t1 my:1 e1 pd:1 EA9:1 pq:1 EA10:1
+sd:1 EAr:1 PY2:1 EA2:1 y1 m1 pw:2 pk:1 EA4:1 EA3:1 pp:1 sy2 EA7:1 EA5:1"""
+POST = """
+PR0.5 EAc.5 PR1.5 S0.5 pl.5 kq.5 l2.5 sb.4 Z0.5 EG7.5 EG8.5 zt.5 S1.5 Z1.5 EG6.5 PR2.5 nm.5 EG4.5 EG3.5 EG2.5 EG11.5 EG0.5
+EG1.5 EG5.5 EG10.5 S2.5 EG9.5 yj.5 EGr.5 bg.5 z.5 t0.5 bt.5 wj.5 sn.5 y0.5 EGm.5 EGs.5 EGc.5 pa.6 e0.5 al.6 pt.5 zu.5 t1.5
+m0.5 tl.5 y1.5 e1.5 sy0.5 m1.5 sy1.5 dd.5 sendz.5 sendc.5 qc.6 pc.6 PY1.6 PY0.6 PY3.6 PY2.6 PY5.6 PY4.6 sy2.5 m2.5 PR0.6
+S0.6 Z0.6 PR1.6 S1.6 Z1.6 PR2.6 sb.5 ob zt.6 oc oy.5 S2.6 bg.6 z.6 t0.6 t1.6 y0.6 oy0.6 y1.6 oy1.6"""
 
 
 def v(name, a=0, b=None, st=1, p=(0, 128, 1)):
@@ -78,12 +90,6 @@ def ext(name, *ix):
     return ("x", name, ix)
 
 
-def ncol(x):
-    if x[0] == "i":
-        return 16 * ncol(x[2])
-    return (x[3] - x[2] + x[4] - 1) // x[4]
-
-
 def isview(x):
     return isinstance(x, tuple) and len(x) > 0 and x[0] in ("v", "i", "x")
 
@@ -92,15 +98,10 @@ def inps(x):
     return x[0] == "v" and SCRATCH[x[1]][0] == "psum"
 
 
-def two(x):
-    return x[0] == "v" and SCRATCH[x[1]][2] in (BF, U16, F16)
-
-
 def build(opt):
-    MA, MG = opt["MA"], opt["MG"]
     ops = []
 
-    def add(nm, eng, instrs, c, kind="c", extra_w=(), tag=None, after=(), nbytes=0):
+    def add(nm, eng, instrs, kind="c", extra_w=(), tag=None, after=()):
         rd, wr = [], list(extra_w)
         for (m, a, k) in instrs:
             vs = [x for x in list(a) + list(k.values()) if isview(x)]
@@ -112,25 +113,12 @@ def build(opt):
                     rd.append(x[2])
                 else:
                     (wr if n == 0 else rd).append(x)
-        ops.append({"nm": nm, "e": eng, "i": instrs, "cc": c, "k": kind, "r": rd, "w": wr, "tag": tag,
-                    "after": list(after), "n": len(ops), "nb": nbytes})
+        ops.append({"nm": nm, "e": eng, "i": instrs, "k": kind, "r": rd, "w": wr, "tag": tag, "after": list(after),
+                    "n": len(ops)})
         return len(ops) - 1
 
-    def vcost(m, a):
-        o = a[0]
-        if o[0] == "i":
-            return ("vi", 0, 0, ncol(o), 0)
-        if len(a) > 1 and isview(a[1]) and a[1][0] == "i":
-            return ("vi", 0, ncol(o), 0, 0)
-        n = ncol(a[1]) if m == "tensor_reduce" else ncol(o)
-        if m == "tensor_tensor":
-            n = n if inps(a[1]) or inps(a[2]) else 2 * n
-        elif two(o) and (m == "memset" or two(a[1])):
-            n = n / 2
-        return ("v", max(64, n), 0, 0, 0)
-
     def vec(nm, m, *a):
-        return add(nm, "v", [(m, a, {})], vcost(m, a))
+        return add(nm, "v", [(m, a, {})])
 
     def tt(nm, o, x, y, op):
         return vec(nm, "tensor_tensor", o, x, y, op)
@@ -150,73 +138,61 @@ def build(opt):
         return vec(nm, "tensor_tensor_scan", o, x, y, init, op0, op1)
 
     def act(nm, o, x, f=Fn.Identity, **k):
-        if nm in opt["VC"].split():
-            return ts(nm, o, x, k.get("scale", 1.0), Op.mult, k.get("bias", 0.0), Op.add)
-        if o[0] == "i":
-            c = ("si", 0, 0, ncol(o), 0)
-        elif x[0] == "i":
-            c = ("si", 0, ncol(o), 0, 0)
-        else:
-            c = ("v", max(64, ncol(o)), 0, 0, 0)
-        return add(nm, "s", [("activation", (o, x, f), k)], c)
-
-    sums = []
+        return add(nm, "s", [("activation", (o, x, f), k)])
 
     def mm(nm, *groups, start=True, stop=True, after=()):
-        c = 0
-        ins = []
-        for lst in groups:
-            for n, (o, l, r) in enumerate(lst):
-                c += max(64, ncol(r)) * (4 if SCRATCH[r[1]][2] == F32 else 1)
-                ins.append(("matmul", (o, l, r, start and n == 0, stop and n == len(lst) - 1), {}))
-        j = add(nm, "t", ins, ("t", 0, 0, 0, c), after=after)
+        ins = [("matmul", (o, l, r, start and n == 0, stop and n == len(lst) - 1), {})
+               for lst in groups for n, (o, l, r) in enumerate(lst)]
+        j = add(nm, "t", ins, after=after)
         ops[j]["soft"] = set(after)
         return j
 
     def pick(o, w, src, a, b, p=(0, 128), w0=0):
         return [(o, v(w, w0 + 15 - l, w0 + 143 - l, p=p), v(src, a + l, b, 16, p=p)) for l in range(16)]
 
-    def dma(nm, q, o, x, nbytes, tag=None, out=False, after=()):
-        return add(nm, q, [("dma_start", (o, x), {})], ("dg" if q == "g" else "d", 0, 0, 0, 0),
-                   kind="o" if out else "d", tag=tag, nbytes=nbytes, after=after)
+    def dma(nm, q, o, x, out=False, after=()):
+        return add(nm, q, [("dma_start", (o, x), {})], kind="o" if out else "d", after=after)
 
     def gp(nm, m, *a, **k):
-        return add(nm, "g", [(m, a, k)], ("g", 2 * ncol(a[0]), 0, 0, 0))
+        return add(nm, "g", [(m, a, k)])
 
     def iota(nm, o, pat, base=0, cm=0):
         if SCRATCH[o[1]][2] == I32:
             return gp(nm, "iota", o, pat, base, cm)
         return gp(nm, "iota", o, pat, base, cm, allow_small_or_imprecise_dtypes=True)
 
+    def select(nm, o, x, pat, op, base, cm):
+        return gp(nm, "affine_select", o, x, pat, op, 0.0, base, cm)
+
     def send(kind, t, srcs, dst, alu=0, whole=()):
-        s = add("send%s.%d" % (kind, t - 1), "g", [("send", (), {"s": list(srcs), "w": list(whole), "d": [dst], "alu": alu,
-                                                              "sem": "m%s%d" % (kind, t)})], ("r", 0, 0, 0, 0), kind="r")
-        ops[s]["r"], ops[s]["w"] = list(srcs) + list(whole), []
-        add("land%s.%d" % (kind, t - 1), "x", [], ("x", 0, 0, 0, 0), kind="a", extra_w=[dst], after=[s], tag="m%s%d" % (kind, t))
+        sem = "m%s%d" % (kind, t + 1)
+        kw = {"s": list(srcs), "w": list(whole), "d": [dst], "alu": alu, "sem": sem}
+        s = add("send%s.%d" % (kind, t), "g", [("send", (), kw)], kind="r")
+        ops[s]["r"] = list(srcs) + list(whole)
+        add("land%s.%d" % (kind, t), "x", [], kind="a", extra_w=[dst], after=[s], tag=sem)
 
     col = lambda j, p=(0, 128): v("COL", j, j + 1, p=p)
-    LANE, PF, GRP, L16, W96 = col(0), col(1), col(2), col(3), col(4)
+    LANE, PF, GRP, L16, W96, C8, PM, PH = col(0), col(1), col(2), col(3), col(4), col(8), col(9), col(10)
     P = lambda b, a, c: v("P%d" % b, a, c)
     PW = lambda a, c: v("PW", a, c)
     sub = lambda x, a, b: v(x[1], x[2] + a, x[2] + b)
-    KB = 1024
 
-    dma("lad", "y", v("ADI", 0, 12), ext("ad"), 6 * KB)
+    dma("lad", "y", v("ADI", 0, 12), ext("ad"))
     for n, nm in enumerate(("sl", "tr", "hv")):
-        dma("lr%d" % n, "s", v("RI", 72 * n, 72 * n + 72), ext(nm), 36 * KB)
-    dma("lvo", "y", v("VO"), ext("vo"), 512 * KB)
-    dma("lvt", "y", v("VB"), ext("vt"), 512 * KB)
-    dma("lui", "y", v("UI"), ext("ui"), 512 * KB)
-    lut = dma("lut", "y", v("UB", 0, W0), ext("ut"), 512 * KB)
-    dma("lcs", "y", v("UB", W0, W0 + B), ext("cs"), 48 * KB)
-    dma("lzs", "y", v("ZS"), ext("zs"), 48 * KB)
-    dma("ltg", "y", v("TG"), ext("tg"), 48 * KB)
+        dma("lr%d" % n, "s", v("RI", 72 * n, 72 * n + 72), ext(nm))
+    dma("lvo", "y", v("VO"), ext("vo"))
+    dma("lvt", "y", v("VB"), ext("vt"))
+    lui = dma("lui", "y", v("UI"), ext("ui"))
+    lut = dma("lut", "y", v("UB", 0, W0), ext("ut"))
+    dma("lcs", "y", v("UB", W0, W0 + B), ext("cs"))
+    dma("lzs", "y", v("ZS"), ext("zs"))
+    dma("ltg", "y", v("TG"), ext("tg"))
     for l in range(16):
-        dma("lnx%d" % l, "y", v("NX", p=(l, 128, 16)), ext("nx"), 64 * KB)
-    dma("lbs", "y", v("BSB"), ext("bs"), 256 * KB)
-    dma("cV", "g", v("V", B, B + W0), ext("vt"), 1024 * KB, after=[lut])
-    dma("cB", "g", v("BS", 0, A), ext("bs"), 512 * KB, after=[lut])
-    dma("cU", "g", v("U", B, B + W0), ext("ut"), 1024 * KB, after=[lut])
+        dma("lnx%d" % l, "y", v("NX", p=(l, 128, 16)), ext("nx"))
+    dma("lbs", "y", v("BSB"), ext("bs"))
+    dma("cV", "g", v("V", B, B + W0), ext("vt"), after=[lui])
+    dma("cB", "g", v("BS", 0, A), ext("bs"), after=[lut])
+    dma("cU", "g", v("U", B, B + W0), ext("ut"), after=[lut])
     iota("PI", v("PI"), [[0, 2]], 0, 1)
     iota("JL", v("JL"), [[0, 16], [1, 16]])
     iota("IJ", v("IJ"), [[1, B]])
@@ -237,16 +213,11 @@ def build(opt):
     ts("BO", v("BO"), v("JH"), GRP, Op.is_equal)
     cp("WH", v("WW", 15, 128, 16), v("BO", 0, 128, 16))
     ts("DG", v("DG"), v("JL", 0, B), LANE, Op.is_equal)
-    gp("RST", "affine_select", v("RST", 0, B), v("CONE", 0, B), [[0, 12], [1, 16]], Op.not_equal, 0.0, 0, 0)
+    select("RST", v("RST", 0, B), v("CONE", 0, B), [[0, 12], [1, 16]], Op.not_equal, 0, 0)
     ts("IB", v("IB"), v("IJ", 0, 128), PF, Op.is_equal)
     cp("W0", v("WW", 144 + 15, 144 + 128, 16), v("IB", 0, 128, 16))
-    act("ID", v("ID"), v("IB"))
-    act("ID16", v("ID16"), v("IB"), scale=16.0)
-    act("JP", v("JP"), v("IB"), scale=BIG)
-    act("JN", v("JN"), v("IB"), scale=-BIG)
-    ts("IN", v("IN"), v("IB"), -1.0, Op.mult)
-    if opt["IDX"] == "s":
-        ts("J5", v("J5"), v("IB"), 512.0, Op.mult)
+    for nm, c in (("ID", 1.0), ("ID16", 16.0), ("JP", BIG), ("JN", -BIG), ("IN", -1.0), ("J5", 512.0)):
+        ts(nm, v(nm), v("IB"), c, Op.mult)
     ts("OFFL", v("OFFL"), v("DG"), 2.0 ** 99, Op.mult, -2.0 ** 99, Op.add)
     scan("WROW", v("WROW"), v("CHALF"), v("OFFL"), 2.0 ** 97, Op.mult, Op.max)
     act("WR2", P(1, B, 2 * B), v("WROW"), scale=-2.5)
@@ -254,70 +225,85 @@ def build(opt):
     tt("WT", v("WT"), v("WROW", 96, 112), v("DG", 0, 16), Op.mult)
     vec("W96", "tensor_reduce", W96, v("WT"), Ax.X, Op.add)
     ts("WCOL", v("WCOL"), v("WROW", 0, B, 16), W96, Op.mult)
-    for m in range(min(MA, MG, opt["ML"]), 12):
-        act("BOW%d" % m, v("BOW", 128 * m, 128 * m + 128), v("BO"), scale=v("WCOL", m, m + 1))
+    for m in range(min(opt["MA"], 8), 12):
+        ts("BOW%d" % m, v("BOW", 128 * m, 128 * m + 128), v("BO"), v("WCOL", m, m + 1), Op.mult)
     cp("ML", v("ML"), v("IJ", 0, 12))
     ts("IW", v("IW"), v("IJ", 0, B, 16), LANE, Op.add)
     for m in range(3):
         act("DCa%d" % m, v("DC", 36 * m, 36 * m + 12), v("IW"), bias=A - BIG)
         act("DCn%d" % m, v("DC", 36 * m + 12, 36 * m + 24), v("IW"), bias=W0 + B * m - BIG)
-    act("L16", L16, LANE, scale=16.0)
-    act("IW17", v("IW17"), v("IW16"), bias=L16)
-    dma("Ri", "y", v("R", p=(25, 26)), v("IJ", p=(0, 6)), 3 * KB)
-    dma("Rn0", "y", v("R", p=(24, 25)), v("NEG", p=(0, 16)), 3 * KB)
-    dma("Rn1", "y", v("R", p=(26, 32)), v("NEG", p=(0, 96)), 14 * KB)
+    ts("L16", L16, LANE, 16.0, Op.mult)
+    ts("IW17", v("IW17"), v("IW16"), L16, Op.add)
+    dma("Ri", "y", v("R", p=(25, 26)), v("IJ", p=(0, 6)))
+    dma("Rn0", "y", v("R", p=(24, 25)), v("NEG", p=(0, 16)))
+    dma("Rn1", "y", v("R", p=(26, 32)), v("NEG", p=(0, 96)))
     cp("Rk", v("RB", 0, 216), v("RI"))
     act("Rq", v("RB", 216, 360), v("RI", 0, 144), Fn.Square)
     for n, p0 in enumerate((0, 8, 16, 32, 40)):
-        dma("Rd%d" % n, "y", v("R", p=(p0, p0 + 8)), v("RB", 72 * n, 72 * n + 72), 18 * KB)
+        dma("Rd%d" % n, "y", v("R", p=(p0, p0 + 8)), v("RB", 72 * n, 72 * n + 72))
     act("L2P", v("L2P", p=(0, 1)), v("JL", p=(0, 1)), Fn.Square, scale=64.0)
-    dma("Ql", "s", v("QQ", 0, 256, p=(24, 25)), v("L2P", p=(0, 1)), KB)
+    dma("Ql", "s", v("QQ", 0, 256, p=(24, 25)), v("L2P", p=(0, 1)))
     act("QI", v("QI", p=(0, 16)), v("JL", p=(0, 16)), Fn.Silu, scale=8192.0)
-    gp("Qk", "affine_select", v("QQ", 0, 256, p=(0, 16)), v("QI", p=(0, 16)), [[-1, 16], [0, 16]], Op.is_equal, 0.0, 0, 1)
-    gp("Qq", "affine_select", v("QQ", 0, 256, p=(32, 48)), v("QI", p=(32, 48)), [[-1, 16], [0, 16]], Op.is_equal, 0.0, 0, 1)
+    select("Qk", v("QQ", 0, 256, p=(0, 16)), v("QI", p=(0, 16)), [[-1, 16], [0, 16]], Op.is_equal, 0, 1)
+    select("Qq", v("QQ", 0, 256, p=(32, 48)), v("QI", p=(32, 48)), [[-1, 16], [0, 16]], Op.is_equal, 0, 1)
     for m in range(3):
         act("Qc%d" % m, col(5 + m), v("ID", 26, 27), scale=-float(W0 + B * m), bias=v("ID", 25, 26))
         act("Qn%d" % m, v("QQ", 256 + 128 * m, 384 + 128 * m, p=(0, 48)), v("QQ", 0, 128, p=(0, 48)), bias=col(5 + m, (0, 48)))
-    gp("W3", "affine_select", v("W3", p=(0, 32)), v("CONE", p=(0, 32)), [[128, 3], [1, 144]], Op.is_equal, 0.0, -15, -16)
+    select("W3", v("W3", p=(0, 32)), v("CONE", p=(0, 32)), [[128, 3], [1, 144]], Op.is_equal, -15, -16)
     mm("pH", pick(P(2, 144, 216), "W3", "R", 0, 6 * B, p=(0, 24), w0=288))
     act("HL", v("HL"), P(2, 144, 216), scale=-2.0)
+    dma("lh", "s", v("RH", p=(0, 8)), ext("hv", 0, B))
+    dma("lnn", "s", v("NN"), ext("nx"))
+    ts("Rh", v("RG", p=(0, 8)), v("RH", p=(0, 8)), -1.0, Op.mult)
+    select("G8", v("G8", p=(0, 8)), v("CONE", 0, 128, p=(0, 8)), [[-1, 8], [0, 16]], Op.is_equal, 0, 1)
+    ts("L8", v("L8"), v("PI"), 7, Op.bitwise_and)
+    act("C8", C8, v("L8", 0, 1), scale=128.0, bias=63.5)
+    act("PM", PM, LANE, Fn.Sign, bias=-7.5)
+    act("PH", PH, PM, scale=0.5)
+    ts("lo", v("LO"), v("ADI", 0, 12), 127, Op.bitwise_and)
+    act("lu", v("LU"), v("LO"))
+    act("G0", v("G0"), ind(v("NN"), v("LU")))
     mm("pK", *[pick(P(2, 72 * q, 72 * q + 72), "W3", "R", 0, 6 * B, p=(0, 24), w0=144 * q) for q in range(2)])
     tt("LKJ", v("LKJ"), P(2, 0, 144), v("IW17"), Op.add)
-    gp("IT", "affine_select", v("IT", 0, A), v("UI"), [[0, A]], Op.is_ge, 0.0, 0, 0)
-    gp("OT", "affine_select", v("OT", 0, A), v("VO"), [[0, A]], Op.is_ge, 0.0, 0, 0)
-    dma("c0", "g", v("CL", 0, B), ext("cs"), 96 * KB)
+    select("IT", v("IT", 0, A), v("UI"), [[0, A]], Op.is_ge, 0, 0)
+    select("OT", v("OT", 0, A), v("VO"), [[0, A]], Op.is_ge, 0, 0)
+    act("c0", v("CL", 0, B), v("UB", W0, W0 + B))
     mm("tg", [(P(1, 0, B), v("IB"), v("TG"))])
-    act("z.0", v("ZC", 0, B), v("ZS"), scale=0.0625)
+    ts("z.0", v("ZC", 0, B), v("ZS"), 0.0625, Op.mult)
     tt("D0", v("D0"), ind(v("ADI", 0, 12), v("ML")), v("DG"), Op.mult)
     mm("pD", [(P(5, 0, B), v("BO"), v("D0"))])
     act("AD0", v("AD", 0, B), P(5, 0, B))
+    act("ab", v("AB"), P(5, 0, B), Fn.Abs, scale=-1.0, bias=C8)
+    act("ar", v("AB"), v("AB"), Fn.Relu, bias=-63.5)
     for n in range(4):
-        gp("RS%d" % n, "affine_select", v("RS2", 256 * n, 256 * n + 256), v("CONE", 0, 256), [[0, 16], [1, 16]],
-           Op.not_equal, 0.0, 0, 0)
+        select("RS%d" % n, v("RS2", 256 * n, 256 * n + 256), v("CONE", 0, 256), [[0, 16], [1, 16]], Op.not_equal, 0, 0)
 
-    def first(E, t, rep, key, bank, sg, ms):
+    def first(E, t, rep, key, bank, sg, ms, span):
         e0 = NE * (t % 2)
         f0 = NE * (bank - 6)
-        for m in range(12):
-            kc = v("WF", key + m, key + m + 1)
-            if m < ms:
-                ts("%s%d.%d" % (E, m, t), v(E, e0 + EOFF[m], e0 + EOFF[m + 1]), sub(rep, 16 * m, B), kc,
-                   Op.is_equal, v("WCOL", m, m + 1), Op.mult)
+        nq = span // 16
+        end = lambda m: span * (m // nq + 1)
+        wt = lambda m: 12 - nq + m % nq
+        blocks = sorted(range(12), key=lambda m: (16 * m - end(m), m))
+        off = [sum(end(m) - 16 * m for m in blocks[:n]) for n in range(13)]
+        lst = [[(P(bank, c, c + span), v("IB"), v("THR", B - span, B))] for c in range(0, B, span)]
+        for n, m in enumerate(blocks):
+            kc, cols, e = v("WF", key + m, key + m + 1), sub(rep, 16 * m, end(m)), v(E, e0 + off[n], e0 + off[n + 1])
+            if n < ms:
+                ts("%s%d.%d" % (E, n, t), e, cols, kc, Op.is_equal, v("WCOL", wt(m), wt(m) + 1), Op.mult)
             else:
-                act("%s%d.%d" % (E, m, t), v("EF", f0 + EOFF[m], f0 + EOFF[m + 1]), sub(rep, 16 * m, B), Fn.Abs,
-                    scale=-1.0, bias=kc)
+                act("%s%d.%d" % (E, n, t), v("EF", f0 + off[n], f0 + off[n + 1]), cols, Fn.Abs, scale=-1.0, bias=kc)
+            lst[m // nq].append((P(bank, 16 * m, end(m)), v("BO") if n < ms else v("BOW", 128 * wt(m), 128 * wt(m) + 128), e))
         if ms < 12:
-            act("%sr.%d" % (E, t), v(E, e0 + EOFF[ms], e0 + NE), v("EF", f0 + EOFF[ms], f0 + NE), Fn.Relu, scale=-1.0, bias=1.0)
-        mm("%sm.%d" % (E, t), [(P(bank, 0, B), v("IB"), v("THR"))]
-           + [(P(bank, 16 * m, B), v("BO") if m < ms else v("BOW", 128 * m, 128 * m + 128),
-               v(E, e0 + EOFF[m], e0 + EOFF[m + 1])) for m in range(12)])
+            act("%sr.%d" % (E, t), v(E, e0 + off[ms], e0 + off[12]), v("EF", f0 + off[ms], f0 + off[12]), Fn.Relu,
+                scale=-1.0, bias=1.0)
+        mm("%sm.%d" % (E, t), *lst)
         act("%ss.%d" % (E, t), v(sg, 0, B), P(bank, 0, B), Fn.Sign)
         o = B + B * (t % 2)
         scan("%sc.%d" % (E, t), v(sg, o, o + B), v("RST"), v(sg, 0, B), 0.0, Op.mult, Op.max)
         return v(sg, o + 15, o + B, 16)
 
     def ints(t):
-        last = t == STEPS
         N = lambda s: "%s.%d" % (s, t)
         ls, wf, nc, of = 48 * t, 24 * t, 2 * B * (t % 2), 2 * B * t
         al, rep = v("LST", ls, ls + 12), v("AD", B * t, B * t + B)
@@ -327,7 +313,7 @@ def build(opt):
             src = P(5, 448, 460)
             mm(N("pa"), pick(src, "WW", "AD", B * t, B * t + B, w0=144))
         act(N("al"), al, src)
-        if not last:
+        if t < STEPS:
             act(N("ka"), v("WF", wf, wf + 12), src)
         PT, QT = ("IT", "OT") if t % 2 == 0 else ("OT", "IT")
         pw = v({0: "UI", 1: "VO"}.get(t, PT), 0, A)
@@ -335,51 +321,50 @@ def build(opt):
         pc, qc = v("OFFS", of, of + B), v("OFFS", of + B, of + 2 * B)
         act(N("qc"), qc, ind(qw, al), bias=0.3)
         act(N("pc"), pc, ind(pw, al), bias=0.3)
-        if last:
+        if t == STEPS:
             return
         mx, sg = 4 * B * (t % 2), 24 * t
-        if opt["CONV"] == "v":
-            ts(N("nc"), v("NC", nc, nc + 2 * B), v("OFFS", of, of + 2 * B), -float(CEN), Op.add)
-        else:
-            act(N("nc"), v("NC", nc, nc + 2 * B), v("OFFS", of, of + 2 * B), bias=-float(CEN))
+        ts(N("nc"), v("NC", nc, nc + 2 * B), v("OFFS", of, of + 2 * B), -float(CEN), Op.add)
         ph, qh = v("NC", nc, nc + B), v("NC", nc + B, nc + 2 * B)
         rt = v("R", B * t, B * t + B, p=(0, 48))
         Q = lambda n: v("QQ", 128 * n, 128 * n + 128, p=(0, 48))
-        mm(N("pd"), [(P(5, 0, B), v("IB"), ph), (P(5, 0, B), v("IN"), qh)])
-        act(N("sd"), v("MX", mx + 3 * B, mx + 4 * B), P(5, 0, B), Fn.Sign, scale=1.0 if t % 2 == 0 else -1.0, bias=-0.5)
-        if opt["SEL"] == "m":
-            SUM0 = CEN
-            mm(N("pw"), [(PW(0, B), Q(0), rt)], [(PW(B, 2 * B), Q(1), rt)])
-            act(N("mk"), PW(0, 2 * B), PW(0, 2 * B), Fn.Relu, scale=2.0 ** -12, bias=1.0)
-            mm(N("pk"), [(PW(704, 896), Q(2 + t // 2), rt)])
-            tt(N("mx"), v("MX", mx, mx + 2 * B), v("NC", nc, nc + 2 * B), PW(0, 2 * B), Op.mult)
-            tt(N("my"), v("MX", mx + 2 * B, mx + 3 * B), ph, PW(B, 2 * B), Op.mult)
+        votes = v("MX", mx + 3 * B, mx + 4 * B)
+        if t == 0:
+            tt(N("sd"), votes, pc, qc, Op.is_gt)
         else:
-            SUM0 = 16 * CEN
-            mm(N("pw"), *[[(PW(128 + B * n, 320 + B * n), v("IB"), x), (PW(128 + B * n, 320 + B * n), Q(q), rt)]
-                          for n, (x, q) in enumerate(((ph, 0), (qh, 1), (ph, 1)))])
-            mm(N("pk"), [(PW(704, 896), Q(2 + t // 2), rt)])
-            ts(N("mx"), v("MX", mx, mx + 3 * B), PW(128, 704), -float(CEN), Op.max)
+            mm(N("pd"), [(P(5, 0, B), v("IB"), ph), (P(5, 0, B), v("IN"), qh)])
+            act(N("sd"), votes, P(5, 0, B), Fn.Sign, scale=1.0 if t % 2 == 0 else -1.0, bias=-0.5)
+        mm(N("pw"), [(PW(0, B), Q(0), rt)], [(PW(B, 2 * B), Q(1), rt)])
+        act(N("mk"), PW(0, 2 * B), PW(0, 2 * B), Fn.Relu, scale=2.0 ** -12, bias=1.0)
+        mm(N("pk"), [(PW(704, 896), Q(2 + t // 2), rt)])
+        tt(N("mx"), v("MX", mx, mx + 2 * B), v("NC", nc, nc + 2 * B), PW(0, 2 * B), Op.mult)
+        tt(N("my"), v("MX", mx + 2 * B, mx + 3 * B), ph, PW(B, 2 * B), Op.mult)
         tt(N("nm"), v("NM"), PW(704, 896), pc, Op.max)
-        mm(N("pp"), pick(P(5, B, B + 48), "WW", "MX", mx, mx + 4 * B)
-           + [(P(5, B + 36, B + 48), v("IB"), v("HL", 12 * t, 12 * t + 12))])
-        ix = v("IX", 12 * t, 12 * t + 12)
-        if opt["IDX"] == "s":
-            act(N("vs"), v("SG", sg, sg + 12), P(5, B + 36, B + 48), Fn.Sign, bias=16.5)
+        ag = v("AG", B * t, B * t + B)
+        if t == 0:
+            mm(N("pp"), pick(P(5, B, B + 36), "WW", "MX", mx, mx + 3 * B))
+            a, b = P(7, 256, 256 + B), P(6, 256, 256 + B)
+            mm(N("pu"), [(a, v("BO"), votes), (a, v("G8", p=(0, 8)), v("RG", p=(0, 8)))])
+            act(N("vs"), v("SV"), a, Fn.Sign, scale=PM, bias=PH)
+            mm(N("pv"), [(b, v("IB"), v("G0")), (b, v("JN"), v("AB")), (b, v("JP"), v("SV"))])
+            act(N("ix"), v("G0"), b, Fn.Relu, bias=-BIG)
+            mm(N("px"), [(a, v("BO"), v("G0"))])
+            act(N("ag"), ag, a)
+        else:
+            vote, ix = P(5, B + 36, B + 48), v("IX", 12 * t, 12 * t + 12)
+            mm(N("pp"), pick(P(5, B, B + 48), "WW", "MX", mx, mx + 4 * B) + [(vote, v("IB"), v("HL", 12 * t, 12 * t + 12))])
+            act(N("vs"), v("SG", sg, sg + 12), vote, Fn.Sign, bias=16.5)
             mm(N("pv"), [(P(5, 460, 472), v("ID"), v("WF", wf, wf + 12)), (P(5, 460, 472), v("J5"), v("SG", sg, sg + 12))])
             act(N("ix"), ix, P(5, 460, 472), bias=512.0)
-        else:
-            ts(N("vs"), v("VT"), P(5, B + 36, B + 48), -16.5, Op.is_gt, float(A), Op.mult)
-            tt(N("ix"), ix, v("VT"), al, Op.add)
-        act(N("ag"), v("AG", B * t, B * t + B), ind(v("NX"), ix))
-        send("a", t + 1, [v("AG", B * t, B * t + B)], v("AD", B * t + B, B * t + 2 * B))
-        act(N("ls"), v("LST", ls + 12, ls + 48), P(5, B, B + 36), bias=float(SUM0))
+            act(N("ag"), ag, ind(v("NX"), ix))
+        send("a", t, [ag], v("AD", B * t + B, B * t + 2 * B))
+        act(N("ls"), v("LST", ls + 12, ls + 48), P(5, B, B + 36), bias=float(CEN))
         if t >= 2:
-            act(N("rs"), v("SG", sg + 12, sg + 24), P(5, B + 24, B + 36), Fn.Relu, bias=float(SUM0 + 1 - W0 - B * (t // 2 - 1)))
+            act(N("rs"), v("SG", sg + 12, sg + 24), P(5, B + 24, B + 36), Fn.Relu, bias=float(CEN + 1 - W0 - B * (t // 2 - 1)))
         rq = v("RQ", B * (t % 2), B * (t % 2) + B)
         mm(N("pq"), [(P(5, 240, 240 + B), v("BO"), v("MX", mx + B, mx + 2 * B))])
-        act(N("rq"), rq, P(5, 240, 240 + B), bias=float(SUM0 + B))
-        nb = first("EA", t, rep, wf, 6, "SA", MA if t else 12)
+        act(N("rq"), rq, P(5, 240, 240 + B), bias=float(CEN + B))
+        nb = first("EA", t, rep, wf, 6, "SA", opt["MA"] if t else 12, B)
         dc = 36 * (t // 2)
         mm(N("pl"), [(P(6, B, B + 36), v("IB"), v("DC", dc, dc + 36)), (P(6, B, B + 12), v("JP"), nb),
                      (P(6, B + 12, B + 24), v("JP"), nb), (P(6, B + 24, B + 36), v("JN"), nb)]
@@ -387,9 +372,11 @@ def build(opt):
         tt(N("l2"), v("L2", 24 * t, 24 * t + 24), P(6, B, B + 24), v("LST", ls, ls + 24), Op.max)
         tt(N("kq"), v("WF", wf + 12, wf + 24), P(6, B + 24, B + 36), v("LST", ls + 24, ls + 36), Op.add)
         act(N("sn"), ind(v(PT), v("L2", 24 * t, 24 * t + 12)), v("NM"), Fn.Silu)
-        ng = first("EG", t, rq, wf + 12, 7, "SO", MG if t < STEPS - 1 else opt["ML"])
+        ng = first("EG", t, rq, wf + 12, 7, "SO", opt["MG"] if t < STEPS - 1 else opt["ML"], RUN)
         mm(N("pt"), [(P(7, B, B + 12), v("ID"), v("WF", wf + 12, wf + 24)), (P(7, B, B + 12), v("JN"), ng)])
         tt(N("tl"), v("TL", 12 * t, 12 * t + 12), P(7, B, B + 12), v("IW"), Op.max)
+
+    sums = []
 
     def floats(t):
         last = t == STEPS
@@ -402,73 +389,68 @@ def build(opt):
         yw = {0: v("VB"), 1: v("UB")}.get(t, v(Y, B, ey))
         of, py, h2 = 2 * B * t, 16 * B * (t % 2), B * (t % 2)
         al = v("LST", 48 * t, 48 * t + 12)
-        w = B // opt["NA"]
-        for n, c in enumerate(range(0, B, w)):
-            act(N("PY%d" % n), v("PY", py + 16 * c, py + 16 * (c + w)), ind(yw, v("OFFS", of + B + c, of + B + c + w)),
+        runs = [(c, c + RUN) for c in range(B - RUN, -1, -RUN)]
+        halves = [c + d for c, _ in runs for d in (0, RUN // 2)]
+        for n, c in enumerate(halves):
+            d = c + RUN // 2
+            act(N("PY%d" % n), v("PY", py + 16 * c, py + 16 * d), ind(yw, v("OFFS", of + B + c, of + B + d)),
                 scale=1.0 if last else 0.0625)
-        split = opt["SPLIT"] or last
-        for n in range(3):
-            d = 64 * n
-            a, b = 16 * d, 16 * (d + 64)
-            w = 32 if N("PR%d" % n) in opt["HALF"].split() else 64
-            for c in range(d, d + 64, w):
-                tt(N(("PR%d" if c == d else "PQ%d") % n), v("PR", 16 * c, 16 * (c + w)), ind(xw, v("OFFS", of + c, of + c + w)),
-                   v("PY", py + 16 * c, py + 16 * (c + w)), Op.mult)
-            if t >= opt["SCAN"] and n == 2:
-                scan(N("S2"), v("SS"), v("RS2"), v("PR", a, b), 0.0, Op.mult, Op.add)
+        scanned = t in opt["SCAN"]
+        for n, (c, d) in enumerate(runs):
+            a, b = 16 * c, 16 * d
+            tt(N("PR%d" % n), v("PR", a, b), ind(xw, v("OFFS", of + c, of + d)), v("PY", py + a, py + b), Op.mult)
+            if scanned and c == 0:
+                scan(N("S%d" % n), v("SS"), v("RS2"), v("PR", a, b), 0.0, Op.mult, Op.add)
             else:
-                o = P(2, 0, 64) if split and n == 2 else P(0, d, d + 64)
-                lst = [(o, v("ID" if last else "ID16"), v("PR", a + k, b, 16)) for k in range(16)]
+                lst = [(P(0 if c else 2, c, d), v("ID" if last else "ID16"), v("PR", a + k, b, 16)) for k in range(16)]
                 j = mm(N("S%d" % n), lst[:8], stop=False, after=sums[-1:])
                 sums[:] = [mm(N("Z%d" % n), lst[8:], start=False, after=[j])]
         bg = v("BG", h2, h2 + B)
         act(N("bg"), bg, ind(v("BSB") if t == 0 else v("BS", 0, A), al))
         z = v("ZC", h2, h2 + B)
         if t > 0:
-            zl = v("ZL", B * (t - 1), B * t)
-            if opt["CLIP"] == "s":
-                act(N("zt"), v("ZT"), zl, Fn.Relu, scale=0.0625, bias=0.0625)
-                act(N("z"), z, v("ZT"), bias=-0.0625)
-            else:
-                ts(N("z"), z, zl, -1.0, Op.max, 0.0625, Op.mult)
+            act(N("zt"), v("ZT"), v("ZL", B * (t - 1), B * t), Fn.Relu, scale=0.0625, bias=0.0625)
+            act(N("z"), z, v("ZT"), bias=-0.0625)
         y, tmp = v("YS", B * t, B * t + B), P(1, B, 2 * B)
         if not last:
             wj, yj, dd, c = v("WJ", h2, h2 + B), v("YJ", h2, h2 + B), v("DD", B * t, B * t + B), v("CL", B * t, B * t + B)
             pw = v("PY", py, py + 16 * B)
-            dma(N("cx"), "y", v(X, ex, ex + B), c, 96 * KB)
+            dma(N("cx"), "y", v(X, ex, ex + B), c)
             tt(N("dd"), dd, ind(xc, v("L2", 24 * t + 12, 24 * t + 24)), c, Op.subtract)
-            send("c", t + 1, [dd, c], v("CL", B * t + B, B * t + 2 * B), 1)
+            send("c", t, [dd, c], v("CL", B * t + B, B * t + 2 * B), 1)
             tt(N("wj"), wj, ind(xw, v("LST", 48 * t + 36, 48 * t + 48)), z, Op.mult)
             act(N("yj"), yj, ind(pw, v("LKJ", 72 + 12 * t, 84 + 12 * t)), scale=16.0)
             tt(N("m2"), v("M2"), ind(pw, v("LKJ", 12 * t, 12 * t + 12)), dd, Op.mult)
-        for n, (a, b) in enumerate(((0, 128), (128, B)) if split else ((0, B),)):
-            s = P(0, a, b) if n == 0 else v("SS", 15, 1024, 16) if t >= opt["SCAN"] else P(2, 0, 64)
-            zz = sub(z, a, b)
-            if n == 1 and opt["SCAN"] <= t < STEPS:
-                act(N("zu"), v("ZU"), zz, scale=16.0)
-                zz = v("ZU")
+        for n, (a, b) in enumerate(((RUN, B), (0, RUN))):
+            s, zz = P(2 * n, a, b), sub(z, a, b)
+            if n == 1 and scanned:
+                s = v("SS", 15, 16 * RUN, 16)
+                if not last:
+                    act(N("zu"), v("ZU"), zz, scale=16.0)
+                    zz = v("ZU")
             tt(N("t%d" % n), sub(tmp, a, b), s, zz, Op.mult)
             tt(N("y%d" % n), sub(y, a, b), sub(tmp, a, b), sub(bg, a, b), Op.add)
-            if n == 1 and opt["ST"] and not last:
-                tt(N("bt"), v("BT"), sub(bg, a, b), P(1, a, b), Op.subtract)
-                tt(N("e1"), P(1, 2 * B, 2 * B + 64), sub(tmp, a, b), v("BT"), Op.add)
-                tt(N("m1"), v("M1", a, b), P(1, 2 * B, 2 * B + 64), sub(wj, a, b), Op.mult)
-                continue
             if last:
-                dma(N("oy%d" % n), "y", ext("ys", B * t + a, B * t + b), sub(y, a, b), 64 * KB, out=True)
-                continue
-            tt(N("e%d" % n), sub(tmp, a, b), sub(y, a, b), P(1, a, b), Op.subtract)
-            tt(N("m%d" % n), v("M1", a, b), sub(tmp, a, b), sub(wj, a, b), Op.mult)
+                dma(N("oy%d" % n), "y", ext("ys", B * t + a, B * t + b), sub(y, a, b), out=True)
+            elif n == 0:
+                tt(N("e0"), sub(tmp, a, b), sub(y, a, b), P(1, a, b), Op.subtract)
+                tt(N("m0"), v("M1", a, b), sub(tmp, a, b), sub(wj, a, b), Op.mult)
+            else:
+                e1 = P(1, 2 * B, 2 * B + RUN)
+                tt(N("bt"), v("BT"), sub(bg, a, b), P(1, a, b), Op.subtract)
+                tt(N("e1"), e1, sub(tmp, a, b), v("BT"), Op.add)
+                tt(N("m1"), v("M1", a, b), e1, sub(wj, a, b), Op.mult)
         if last:
             return
-        dma(N("oy"), "y", ext("ys", B * t, B * t + B), y, 96 * KB, out=True)
-        send("z", t + 1, [y], v("ZL", B * t, B * t + B), 3, [v("ONE")])
-        for n, (a, b) in enumerate(((0, 128), (128, B)) if split else ((0, B),)):
-            tt(N("sy%d" % n), ind(v(Y, 0, ey), v("TL", 12 * t + a // 16, 12 * t + b // 16)), sub(yj, a, b), v("M1", a, b), Op.subtract)
+        dma(N("oy"), "y", ext("ys", B * t, B * t + B), y, out=True)
+        send("z", t, [y], v("ZL", B * t, B * t + B), 3, [v("ONE")])
+        for n, (a, b) in enumerate(runs):
+            tt(N("sy%d" % n), ind(v(Y, 0, ey), v("TL", 12 * t + a // 16, 12 * t + b // 16)), sub(yj, a, b), v("M1", a, b),
+               Op.subtract)
         tt(N("sb"), ind(v("BS"), v("L2", 24 * t, 24 * t + 12)), bg, v("M2"), Op.add)
         if t == STEPS - 1:
-            dma("ob", "y", ext("fb"), v("BS", 0, A), 512 * KB, out=True)
-            dma("oc", "y", ext("fc"), v("CL", 6 * B, 7 * B), 96 * KB, out=True)
+            dma("ob", "y", ext("fb"), v("BS", 0, A), out=True)
+            dma("oc", "y", ext("fc"), v("CL", 6 * B, 7 * B), out=True)
 
     ints(0)
     for t in range(STEPS + 1):
@@ -528,12 +510,10 @@ def schedule(opt=OPT, pro=PRO, loop=LOOP, post=POST):
     ops = build(opt)
     depend(ops)
     order = expand(ops, pro, loop, post)
-    assert sorted(order) == list(range(len(ops)))
     pos = {j: i for i, j in enumerate(order)}
     bank, lastg, cnt, nd = {}, [], {}, 0
     for j in order:
         o = ops[j]
-        assert all(pos[i] < pos[j] for i in o["d"]), o["nm"]
         for b in o["banks"]:
             o["d"].update(i for e, i in bank.get(b, {}).items() if e != o["e"])
             bank.setdefault(b, {})[o["e"]] = j
@@ -551,8 +531,6 @@ def schedule(opt=OPT, pro=PRO, loop=LOOP, post=POST):
             o["sig"] = (o["tag"], -1)
         elif o["k"] == "r":
             o["sig"] = ("l" + o["i"][0][2]["sem"], -2)
-        else:
-            o["sig"] = None
     known = {}
     for j in order:
         o = ops[j]

from concourse.bass import DstId, RemoteDMATransfer
from concourse.mybir import AluOpType as Op, ActivationFunctionType as Fn, AxisListType as Ax

A, W0, B, STEPS = 1024, 2048, 192, 6
H = B // 2
RUN = 64
CEN = 1408
BIG = 3072.0
TW = B + W0 + 3 * B
NE = sum(B - 16 * m for m in range(12))
F32, BF, I32, U16, F16 = "float32", "bfloat16", "int32", "uint16", "float16"


def _s(n, d):
    return ("sbuf", [128, n], d)


SCRATCH = {
    "U": _s(TW, F32), "V": _s(TW, F32), "BS": _s(A + B, F32), "IT": _s(A + B, F32), "OT": _s(A + B, F32),
    "UB": _s(W0 + B, BF), "VB": _s(W0, BF), "BSB": _s(A, BF), "UI": _s(A, I32), "VO": _s(A, I32), "NX": _s(2 * A, I32),
    "ADI": _s(16, I32), "RI": _s(216, I32), "RB": _s(360, BF), "NEG": _s(72, BF), "R": _s(6 * B, BF),
    "ZS": _s(B, BF), "TG": _s(B, BF), "D0": _s(B, F16), "RH": _s(B, I32), "RG": _s(B, BF),
    "NN": _s(128, I32), "G8": _s(128, BF), "L8": _s(2, I32), "LO": _s(12, I32), "LU": _s(12, U16), "G0": _s(B, F16),
    "AB": _s(B, BF), "SV": _s(B, BF),
    "PI": _s(2, I32), "LI": _s(2, I32), "COL": _s(16, F32), "IJ": _s(B, BF), "JL": _s(256, BF), "JH": _s(128, BF),
    "DG": _s(B, BF), "BO": _s(128, BF), "WW": _s(288, BF), "ID": _s(128, F32), "ID16": _s(128, F32), "IB": _s(128, BF),
    "JP": _s(128, BF), "JN": _s(128, BF), "IN": _s(128, BF), "J5": _s(128, BF), "BOW": _s(12 * 128, BF),
    "RST": _s(B, BF), "RS2": _s(16 * RUN, BF), "SS": _s(16 * RUN, F32), "ONE": _s(H, F32),
    "IW": _s(12, F32), "ML": _s(12, U16), "DC": _s(108, F16), "IW16": _s(144, F32), "IW17": _s(144, F32),
    "W3": _s(432, BF), "CONE": _s(432, BF), "QQ": _s(640, BF), "QI": _s(256, BF), "L2P": _s(256, BF),
    "WROW": _s(B, BF), "OFFL": _s(B, BF), "THR": _s(B, BF), "CHALF": _s(B, BF), "WT": _s(16, F32), "WCOL": _s(12, F32),
    "LKJ": _s(144, U16), "HL": _s(72, BF),
    "AD": _s(7 * B, F16), "AG": _s(6 * B, F16), "LST": _s(7 * 48, U16), "WF": _s(6 * 24, F32), "OFFS": _s(7 * 2 * B, U16),
    "NC": _s(2 * 2 * B, F16), "MX": _s(2 * 4 * B, F16), "RQ": _s(2 * B, U16), "SG": _s(6 * 24, BF),
    "IX": _s(6 * 12, U16), "NM": _s(B, F32),
    "EA": _s(2 * NE, BF), "EG": _s(2 * NE, BF), "EF": _s(2 * NE, BF), "SA": _s(3 * B, BF), "SO": _s(3 * B, BF),
    "L2": _s(6 * 24, U16), "TL": _s(6 * 12, U16),
    "PY": _s(2 * 16 * B, F32), "PR": _s(16 * B, F32), "YS": _s(7 * B, F32), "ZL": _s(6 * B, F32), "ZC": _s(2 * B, F32),
    "ZT": _s(B, F32), "ZU": _s(RUN, F32), "DD": _s(6 * B, F32), "CL": _s(7 * B, F32), "BG": _s(2 * B, F32),
    "WJ": _s(2 * B, F32), "YJ": _s(2 * B, F32), "M1": _s(B, F32), "M2": _s(B, F32), "BT": _s(RUN, F32),
    "PW": ("psum", [128, 1024], F32),
}
for _b in (0, 1, 2, 5, 6, 7):
    SCRATCH["P%d" % _b] = ("psum", [128, 512], F32)
NDMA = 54
SEMAPHORES = (["ev", "es", "et", "eg", "outs"] + ["d%d" % i for i in range(NDMA)]
              + ["%s%s%d" % (w, k, t) for w in ("m", "lm") for k in "acz" for t in range(1, STEPS + 1)])

OPT = {
    "MA": 8,
    "MG": 5,
    "ML": 0,
    "SCAN": (5, 6),
}
PRO = """
fWW JL lnn lad fQI lr1 lr0 lr2 PI lvo fQQ LI fONE lh LANE PF DG fR GRP IJ JH QI L2P L8 lui lvt IW ML lo fH D0 BO OFFL Rk
PM C8 Rq Rd3 Rn1 lut al.0 PH Rd0 lu Ql ka.0 Rd4 Rd1 pD Rn0 IW16 RST Qq Ri lnx5 Rd2 lzs W3 G8 lnx14 ltg lnx10 lnx7 Qk fDC
lnx12 lnx3 lnx15 lnx4 cV lbs lnx9 lnx8 WROW lcs lnx11 lnx13 qc.0 WR2 AD0 ab WT L16 IB W96 WCOL WH THR pc.0 ar G0 Rh EA7.0
sd.0 lnx2 lnx6 EA1.0 lnx0 lnx1 EA11.0 EA6.0 BOW10 EA9.0 ID16 JN JP EA2.0 EA8.0 EA4.0 W0 EA3.0 IN EA5.0 PY0.0 pu.0 vs.0
pv.0 BOW8 EA0.0 EA10.0 pw.0 PY1.0 ID ix.0 tg px.0 nc.0 mk.0 Qc0 EAm.0 pK ag.0 PY3.0 DCa0 PR0.0 EAs.0 PY2.0 mx.0 pq.0 rq.0
BOW9 my.0 IW17 z.0 EAc.0 RS0 senda.0 PY5.0 S0.0 BOW11 Qn0 DCn0 IT pw.1 pp.0 pl.0 mk.1 ls.0 Qc1 PR1.0 PY4.0 pk.0 l2.0 c0
DCa2 kq.0 EG4.0 Z0.0 S1.0 Z1.0 LKJ EG0.0 EG7.0 EG5.0 J5 EG8.0 EG6.0 EG10.0 nm.0 EG2.0 DCn1 EG1.0 dd.0 EG11.0 EG9.0 EG3.0
PR2.0 t0.0 bg.0 wj.0 y0.0 e0.0 m0.0 yj.0 EGr.0 EGm.0 sn.0 EGs.0 pa.1 Qn1 DCn2 al.1 S2.0 Z2.0 ka.1 EA5.1 OT m2.0 EA2.1
DCa1 qc.1 EA11.1 f1 pc.1 PY1.1 EA10.1 EA8.1 PY0.1 EGc.0 bt.0 EA7.1 nc.1 pt.0 EA1.1 EA6.1 mx.1 t1.0 pd.1 EA4.1 tl.0 pH RS1
my.1 cB sy0.0 e1.0 y1.0 sendc.0 RS3 sy1.0 sd.1 EA9.1 m1.0 Qc2 HL pw.2 pq.1 EA0.1 pk.1 pp.1 sendz.0 EAr.1 PY2.1 Qn2 cx.0
oy.0 RS2 sy2.0 EA3.1 cx.1 vs.1 EAm.1 cU"""
LOOP = """
PR0 vs PY3 nm EAm EAs pv ix ls rs ag mk:1 PY4 rq S0 PY5 EAc pl Z0 PR1 S1 sendc:-1 cx kq EG9 EG8 EG7 Z1 sb:-1 sendz:-1 zt
EG0 EG1 EG3 l2 EG5 oy:-1 EG6 EG11 EG10 EG4 bg EGr EG2 z yj sn PR2 dd t0 EGm EGs wj y0 m2 senda pa:1 al:1 ka:1 EGc e0 S2
qc:1 EA0:1 EA1:1 EA6:1 bt pc:1 PY0:1 EA11:1 PY1:1 m0 pt tl EA8:1 nc:1 Z2 sy0 mx:1 sy1 t1 my:1 e1 pd:1 EA9:1 pq:1 EA10:1
sd:1 EAr:1 PY2:1 EA2:1 y1 m1 pw:2 pk:1 EA4:1 EA3:1 pp:1 sy2 EA7:1 EA5:1"""
POST = """
PR0.5 EAc.5 PR1.5 S0.5 pl.5 kq.5 l2.5 sb.4 Z0.5 EG7.5 EG8.5 zt.5 S1.5 Z1.5 EG6.5 PR2.5 nm.5 EG4.5 EG3.5 EG2.5 EG11.5 EG0.5
EG1.5 EG5.5 EG10.5 S2.5 EG9.5 yj.5 EGr.5 bg.5 z.5 t0.5 bt.5 wj.5 sn.5 y0.5 EGm.5 EGs.5 EGc.5 pa.6 e0.5 al.6 pt.5 zu.5 t1.5
m0.5 tl.5 y1.5 e1.5 sy0.5 m1.5 sy1.5 dd.5 sendz.5 sendc.5 qc.6 pc.6 PY1.6 PY0.6 PY3.6 PY2.6 PY5.6 PY4.6 sy2.5 m2.5 PR0.6
S0.6 Z0.6 PR1.6 S1.6 Z1.6 PR2.6 sb.5 ob zt.6 oc oy.5 S2.6 bg.6 z.6 t0.6 t1.6 y0.6 oy0.6 y1.6 oy1.6"""


def v(name, a=0, b=None, st=1, p=(0, 128, 1)):
    if b is None:
        b = SCRATCH[name][1][1]
    return ("v", name, a, b, st, p if len(p) == 3 else p + (1,))


def ind(win, off):
    return ("i", win, off)


def ext(name, *ix):
    return ("x", name, ix)


def isview(x):
    return isinstance(x, tuple) and len(x) > 0 and x[0] in ("v", "i", "x")


def inps(x):
    return x[0] == "v" and SCRATCH[x[1]][0] == "psum"


def build(opt):
    ops = []

    def add(nm, eng, instrs, kind="c", extra_w=(), tag=None, after=()):
        rd, wr = [], list(extra_w)
        for (m, a, k) in instrs:
            vs = [x for x in list(a) + list(k.values()) if isview(x)]
            for n, x in enumerate(vs):
                if x[0] == "x":
                    continue
                if x[0] == "i":
                    (wr if n == 0 else rd).append(x[1])
                    rd.append(x[2])
                else:
                    (wr if n == 0 else rd).append(x)
        ops.append({"nm": nm, "e": eng, "i": instrs, "k": kind, "r": rd, "w": wr, "tag": tag, "after": list(after),
                    "n": len(ops)})
        return len(ops) - 1

    def vec(nm, m, *a):
        return add(nm, "v", [(m, a, {})])

    def tt(nm, o, x, y, op):
        return vec(nm, "tensor_tensor", o, x, y, op)

    def ts(nm, o, x, s1, op0, s2=None, op1=None):
        if op1 is None:
            return vec(nm, "tensor_scalar", o, x, s1, None, op0)
        return vec(nm, "tensor_scalar", o, x, s1, s2, op0, op1)

    def cp(nm, o, x):
        return vec(nm, "tensor_copy", o, x)

    def fill(nm, o, c):
        return vec(nm, "memset", o, c)

    def scan(nm, o, x, y, init, op0, op1):
        return vec(nm, "tensor_tensor_scan", o, x, y, init, op0, op1)

    def act(nm, o, x, f=Fn.Identity, **k):
        return add(nm, "s", [("activation", (o, x, f), k)])

    def mm(nm, *groups, start=True, stop=True, after=()):
        ins = [("matmul", (o, l, r, start and n == 0, stop and n == len(lst) - 1), {})
               for lst in groups for n, (o, l, r) in enumerate(lst)]
        j = add(nm, "t", ins, after=after)
        ops[j]["soft"] = set(after)
        return j

    def pick(o, w, src, a, b, p=(0, 128), w0=0):
        return [(o, v(w, w0 + 15 - l, w0 + 143 - l, p=p), v(src, a + l, b, 16, p=p)) for l in range(16)]

    def dma(nm, q, o, x, out=False, after=()):
        return add(nm, q, [("dma_start", (o, x), {})], kind="o" if out else "d", after=after)

    def gp(nm, m, *a, **k):
        return add(nm, "g", [(m, a, k)])

    def iota(nm, o, pat, base=0, cm=0):
        if SCRATCH[o[1]][2] == I32:
            return gp(nm, "iota", o, pat, base, cm)
        return gp(nm, "iota", o, pat, base, cm, allow_small_or_imprecise_dtypes=True)

    def select(nm, o, x, pat, op, base, cm):
        return gp(nm, "affine_select", o, x, pat, op, 0.0, base, cm)

    def send(kind, t, srcs, dst, alu=0, whole=()):
        sem = "m%s%d" % (kind, t + 1)
        kw = {"s": list(srcs), "w": list(whole), "d": [dst], "alu": alu, "sem": sem}
        s = add("send%s.%d" % (kind, t), "g", [("send", (), kw)], kind="r")
        ops[s]["r"] = list(srcs) + list(whole)
        add("land%s.%d" % (kind, t), "x", [], kind="a", extra_w=[dst], after=[s], tag=sem)

    col = lambda j, p=(0, 128): v("COL", j, j + 1, p=p)
    LANE, PF, GRP, L16, W96, C8, PM, PH = col(0), col(1), col(2), col(3), col(4), col(8), col(9), col(10)
    P = lambda b, a, c: v("P%d" % b, a, c)
    PW = lambda a, c: v("PW", a, c)
    sub = lambda x, a, b: v(x[1], x[2] + a, x[2] + b)

    dma("lad", "y", v("ADI", 0, 12), ext("ad"))
    for n, nm in enumerate(("sl", "tr", "hv")):
        dma("lr%d" % n, "s", v("RI", 72 * n, 72 * n + 72), ext(nm))
    dma("lvo", "y", v("VO"), ext("vo"))
    dma("lvt", "y", v("VB"), ext("vt"))
    lui = dma("lui", "y", v("UI"), ext("ui"))
    lut = dma("lut", "y", v("UB", 0, W0), ext("ut"))
    dma("lcs", "y", v("UB", W0, W0 + B), ext("cs"))
    dma("lzs", "y", v("ZS"), ext("zs"))
    dma("ltg", "y", v("TG"), ext("tg"))
    for l in range(16):
        dma("lnx%d" % l, "y", v("NX", p=(l, 128, 16)), ext("nx"))
    dma("lbs", "y", v("BSB"), ext("bs"))
    dma("cV", "g", v("V", B, B + W0), ext("vt"), after=[lui])
    dma("cB", "g", v("BS", 0, A), ext("bs"), after=[lut])
    dma("cU", "g", v("U", B, B + W0), ext("ut"), after=[lut])
    iota("PI", v("PI"), [[0, 2]], 0, 1)
    iota("JL", v("JL"), [[0, 16], [1, 16]])
    iota("IJ", v("IJ"), [[1, B]])
    iota("JH", v("JH"), [[16, 8], [0, 16]])
    iota("IW16", v("IW16"), [[0, 12], [256, 12]])
    fill("fR", v("NEG"), -1.0)
    fill("fQQ", v("QQ", 0, 256, p=(0, 32)), 0.0)
    fill("fQI", v("QI", p=(32, 48)), -4096.0)
    fill("fONE", v("CONE"), 1.0)
    fill("fWW", v("WW"), 0.0)
    iota("fDC", v("DC"), [[0, 108]], B)
    fill("fH", v("CHALF"), 0.5)
    iota("f1", v("ONE"), [[0, H]], 1)
    ts("LI", v("LI"), v("PI"), 15, Op.bitwise_and)
    cp("LANE", LANE, v("LI", 0, 1))
    cp("PF", PF, v("PI", 0, 1))
    tt("GRP", GRP, PF, LANE, Op.subtract)
    ts("BO", v("BO"), v("JH"), GRP, Op.is_equal)
    cp("WH", v("WW", 15, 128, 16), v("BO", 0, 128, 16))
    ts("DG", v("DG"), v("JL", 0, B), LANE, Op.is_equal)
    select("RST", v("RST", 0, B), v("CONE", 0, B), [[0, 12], [1, 16]], Op.not_equal, 0, 0)
    ts("IB", v("IB"), v("IJ", 0, 128), PF, Op.is_equal)
    cp("W0", v("WW", 144 + 15, 144 + 128, 16), v("IB", 0, 128, 16))
    for nm, c in (("ID", 1.0), ("ID16", 16.0), ("JP", BIG), ("JN", -BIG), ("IN", -1.0), ("J5", 512.0)):
        ts(nm, v(nm), v("IB"), c, Op.mult)
    ts("OFFL", v("OFFL"), v("DG"), 2.0 ** 99, Op.mult, -2.0 ** 99, Op.add)
    scan("WROW", v("WROW"), v("CHALF"), v("OFFL"), 2.0 ** 97, Op.mult, Op.max)
    act("WR2", P(1, B, 2 * B), v("WROW"), scale=-2.5)
    tt("THR", v("THR"), P(1, B, 2 * B), v("OFFL"), Op.add)
    tt("WT", v("WT"), v("WROW", 96, 112), v("DG", 0, 16), Op.mult)
    vec("W96", "tensor_reduce", W96, v("WT"), Ax.X, Op.add)
    ts("WCOL", v("WCOL"), v("WROW", 0, B, 16), W96, Op.mult)
    for m in range(min(opt["MA"], 8), 12):
        ts("BOW%d" % m, v("BOW", 128 * m, 128 * m + 128), v("BO"), v("WCOL", m, m + 1), Op.mult)
    cp("ML", v("ML"), v("IJ", 0, 12))
    ts("IW", v("IW"), v("IJ", 0, B, 16), LANE, Op.add)
    for m in range(3):
        act("DCa%d" % m, v("DC", 36 * m, 36 * m + 12), v("IW"), bias=A - BIG)
        act("DCn%d" % m, v("DC", 36 * m + 12, 36 * m + 24), v("IW"), bias=W0 + B * m - BIG)
    ts("L16", L16, LANE, 16.0, Op.mult)
    ts("IW17", v("IW17"), v("IW16"), L16, Op.add)
    dma("Ri", "y", v("R", p=(25, 26)), v("IJ", p=(0, 6)))
    dma("Rn0", "y", v("R", p=(24, 25)), v("NEG", p=(0, 16)))
    dma("Rn1", "y", v("R", p=(26, 32)), v("NEG", p=(0, 96)))
    cp("Rk", v("RB", 0, 216), v("RI"))
    act("Rq", v("RB", 216, 360), v("RI", 0, 144), Fn.Square)
    for n, p0 in enumerate((0, 8, 16, 32, 40)):
        dma("Rd%d" % n, "y", v("R", p=(p0, p0 + 8)), v("RB", 72 * n, 72 * n + 72))
    act("L2P", v("L2P", p=(0, 1)), v("JL", p=(0, 1)), Fn.Square, scale=64.0)
    dma("Ql", "s", v("QQ", 0, 256, p=(24, 25)), v("L2P", p=(0, 1)))
    act("QI", v("QI", p=(0, 16)), v("JL", p=(0, 16)), Fn.Silu, scale=8192.0)
    select("Qk", v("QQ", 0, 256, p=(0, 16)), v("QI", p=(0, 16)), [[-1, 16], [0, 16]], Op.is_equal, 0, 1)
    select("Qq", v("QQ", 0, 256, p=(32, 48)), v("QI", p=(32, 48)), [[-1, 16], [0, 16]], Op.is_equal, 0, 1)
    for m in range(3):
        act("Qc%d" % m, col(5 + m), v("ID", 26, 27), scale=-float(W0 + B * m), bias=v("ID", 25, 26))
        act("Qn%d" % m, v("QQ", 256 + 128 * m, 384 + 128 * m, p=(0, 48)), v("QQ", 0, 128, p=(0, 48)), bias=col(5 + m, (0, 48)))
    select("W3", v("W3", p=(0, 32)), v("CONE", p=(0, 32)), [[128, 3], [1, 144]], Op.is_equal, -15, -16)
    mm("pH", pick(P(2, 144, 216), "W3", "R", 0, 6 * B, p=(0, 24), w0=288))
    act("HL", v("HL"), P(2, 144, 216), scale=-2.0)
    dma("lh", "s", v("RH", p=(0, 8)), ext("hv", 0, B))
    dma("lnn", "s", v("NN"), ext("nx"))
    ts("Rh", v("RG", p=(0, 8)), v("RH", p=(0, 8)), -1.0, Op.mult)
    select("G8", v("G8", p=(0, 8)), v("CONE", 0, 128, p=(0, 8)), [[-1, 8], [0, 16]], Op.is_equal, 0, 1)
    ts("L8", v("L8"), v("PI"), 7, Op.bitwise_and)
    act("C8", C8, v("L8", 0, 1), scale=128.0, bias=63.5)
    act("PM", PM, LANE, Fn.Sign, bias=-7.5)
    act("PH", PH, PM, scale=0.5)
    ts("lo", v("LO"), v("ADI", 0, 12), 127, Op.bitwise_and)
    act("lu", v("LU"), v("LO"))
    act("G0", v("G0"), ind(v("NN"), v("LU")))
    mm("pK", *[pick(P(2, 72 * q, 72 * q + 72), "W3", "R", 0, 6 * B, p=(0, 24), w0=144 * q) for q in range(2)])
    tt("LKJ", v("LKJ"), P(2, 0, 144), v("IW17"), Op.add)
    select("IT", v("IT", 0, A), v("UI"), [[0, A]], Op.is_ge, 0, 0)
    select("OT", v("OT", 0, A), v("VO"), [[0, A]], Op.is_ge, 0, 0)
    act("c0", v("CL", 0, B), v("UB", W0, W0 + B))
    mm("tg", [(P(1, 0, B), v("IB"), v("TG"))])
    ts("z.0", v("ZC", 0, B), v("ZS"), 0.0625, Op.mult)
    tt("D0", v("D0"), ind(v("ADI", 0, 12), v("ML")), v("DG"), Op.mult)
    mm("pD", [(P(5, 0, B), v("BO"), v("D0"))])
    act("AD0", v("AD", 0, B), P(5, 0, B))
    act("ab", v("AB"), P(5, 0, B), Fn.Abs, scale=-1.0, bias=C8)
    act("ar", v("AB"), v("AB"), Fn.Relu, bias=-63.5)
    for n in range(4):
        select("RS%d" % n, v("RS2", 256 * n, 256 * n + 256), v("CONE", 0, 256), [[0, 16], [1, 16]], Op.not_equal, 0, 0)

    def first(E, t, rep, key, bank, sg, ms, span):
        e0 = NE * (t % 2)
        f0 = NE * (bank - 6)
        nq = span // 16
        end = lambda m: span * (m // nq + 1)
        wt = lambda m: 12 - nq + m % nq
        blocks = sorted(range(12), key=lambda m: (16 * m - end(m), m))
        off = [sum(end(m) - 16 * m for m in blocks[:n]) for n in range(13)]
        lst = [[(P(bank, c, c + span), v("IB"), v("THR", B - span, B))] for c in range(0, B, span)]
        for n, m in enumerate(blocks):
            kc, cols, e = v("WF", key + m, key + m + 1), sub(rep, 16 * m, end(m)), v(E, e0 + off[n], e0 + off[n + 1])
            if n < ms:
                ts("%s%d.%d" % (E, n, t), e, cols, kc, Op.is_equal, v("WCOL", wt(m), wt(m) + 1), Op.mult)
            else:
                act("%s%d.%d" % (E, n, t), v("EF", f0 + off[n], f0 + off[n + 1]), cols, Fn.Abs, scale=-1.0, bias=kc)
            lst[m // nq].append((P(bank, 16 * m, end(m)), v("BO") if n < ms else v("BOW", 128 * wt(m), 128 * wt(m) + 128), e))
        if ms < 12:
            act("%sr.%d" % (E, t), v(E, e0 + off[ms], e0 + off[12]), v("EF", f0 + off[ms], f0 + off[12]), Fn.Relu,
                scale=-1.0, bias=1.0)
        mm("%sm.%d" % (E, t), *lst)
        act("%ss.%d" % (E, t), v(sg, 0, B), P(bank, 0, B), Fn.Sign)
        o = B + B * (t % 2)
        scan("%sc.%d" % (E, t), v(sg, o, o + B), v("RST"), v(sg, 0, B), 0.0, Op.mult, Op.max)
        return v(sg, o + 15, o + B, 16)

    def ints(t):
        N = lambda s: "%s.%d" % (s, t)
        ls, wf, nc, of = 48 * t, 24 * t, 2 * B * (t % 2), 2 * B * t
        al, rep = v("LST", ls, ls + 12), v("AD", B * t, B * t + B)
        if t == 0:
            src = v("ADI", 0, 12)
        else:
            src = P(5, 448, 460)
            mm(N("pa"), pick(src, "WW", "AD", B * t, B * t + B, w0=144))
        act(N("al"), al, src)
        if t < STEPS:
            act(N("ka"), v("WF", wf, wf + 12), src)
        PT, QT = ("IT", "OT") if t % 2 == 0 else ("OT", "IT")
        pw = v({0: "UI", 1: "VO"}.get(t, PT), 0, A)
        qw = v({0: "VO"}.get(t, QT), 0, A)
        pc, qc = v("OFFS", of, of + B), v("OFFS", of + B, of + 2 * B)
        act(N("qc"), qc, ind(qw, al), bias=0.3)
        act(N("pc"), pc, ind(pw, al), bias=0.3)
        if t == STEPS:
            return
        mx, sg = 4 * B * (t % 2), 24 * t
        ts(N("nc"), v("NC", nc, nc + 2 * B), v("OFFS", of, of + 2 * B), -float(CEN), Op.add)
        ph, qh = v("NC", nc, nc + B), v("NC", nc + B, nc + 2 * B)
        rt = v("R", B * t, B * t + B, p=(0, 48))
        Q = lambda n: v("QQ", 128 * n, 128 * n + 128, p=(0, 48))
        votes = v("MX", mx + 3 * B, mx + 4 * B)
        if t == 0:
            tt(N("sd"), votes, pc, qc, Op.is_gt)
        else:
            mm(N("pd"), [(P(5, 0, B), v("IB"), ph), (P(5, 0, B), v("IN"), qh)])
            act(N("sd"), votes, P(5, 0, B), Fn.Sign, scale=1.0 if t % 2 == 0 else -1.0, bias=-0.5)
        mm(N("pw"), [(PW(0, B), Q(0), rt)], [(PW(B, 2 * B), Q(1), rt)])
        act(N("mk"), PW(0, 2 * B), PW(0, 2 * B), Fn.Relu, scale=2.0 ** -12, bias=1.0)
        mm(N("pk"), [(PW(704, 896), Q(2 + t // 2), rt)])
        tt(N("mx"), v("MX", mx, mx + 2 * B), v("NC", nc, nc + 2 * B), PW(0, 2 * B), Op.mult)
        tt(N("my"), v("MX", mx + 2 * B, mx + 3 * B), ph, PW(B, 2 * B), Op.mult)
        tt(N("nm"), v("NM"), PW(704, 896), pc, Op.max)
        ag = v("AG", B * t, B * t + B)
        if t == 0:
            mm(N("pp"), pick(P(5, B, B + 36), "WW", "MX", mx, mx + 3 * B))
            a, b = P(7, 256, 256 + B), P(6, 256, 256 + B)
            mm(N("pu"), [(a, v("BO"), votes), (a, v("G8", p=(0, 8)), v("RG", p=(0, 8)))])
            act(N("vs"), v("SV"), a, Fn.Sign, scale=PM, bias=PH)
            mm(N("pv"), [(b, v("IB"), v("G0")), (b, v("JN"), v("AB")), (b, v("JP"), v("SV"))])
            act(N("ix"), v("G0"), b, Fn.Relu, bias=-BIG)
            mm(N("px"), [(a, v("BO"), v("G0"))])
            act(N("ag"), ag, a)
        else:
            vote, ix = P(5, B + 36, B + 48), v("IX", 12 * t, 12 * t + 12)
            mm(N("pp"), pick(P(5, B, B + 48), "WW", "MX", mx, mx + 4 * B) + [(vote, v("IB"), v("HL", 12 * t, 12 * t + 12))])
            act(N("vs"), v("SG", sg, sg + 12), vote, Fn.Sign, bias=16.5)
            mm(N("pv"), [(P(5, 460, 472), v("ID"), v("WF", wf, wf + 12)), (P(5, 460, 472), v("J5"), v("SG", sg, sg + 12))])
            act(N("ix"), ix, P(5, 460, 472), bias=512.0)
            act(N("ag"), ag, ind(v("NX"), ix))
        send("a", t, [ag], v("AD", B * t + B, B * t + 2 * B))
        act(N("ls"), v("LST", ls + 12, ls + 48), P(5, B, B + 36), bias=float(CEN))
        if t >= 2:
            act(N("rs"), v("SG", sg + 12, sg + 24), P(5, B + 24, B + 36), Fn.Relu, bias=float(CEN + 1 - W0 - B * (t // 2 - 1)))
        rq = v("RQ", B * (t % 2), B * (t % 2) + B)
        mm(N("pq"), [(P(5, 240, 240 + B), v("BO"), v("MX", mx + B, mx + 2 * B))])
        act(N("rq"), rq, P(5, 240, 240 + B), bias=float(CEN + B))
        nb = first("EA", t, rep, wf, 6, "SA", opt["MA"] if t else 12, B)
        dc = 36 * (t // 2)
        mm(N("pl"), [(P(6, B, B + 36), v("IB"), v("DC", dc, dc + 36)), (P(6, B, B + 12), v("JP"), nb),
                     (P(6, B + 12, B + 24), v("JP"), nb), (P(6, B + 24, B + 36), v("JN"), nb)]
           + ([(P(6, B + 24, B + 36), v("JN"), v("SG", sg + 12, sg + 24))] if t >= 2 else []))
        tt(N("l2"), v("L2", 24 * t, 24 * t + 24), P(6, B, B + 24), v("LST", ls, ls + 24), Op.max)
        tt(N("kq"), v("WF", wf + 12, wf + 24), P(6, B + 24, B + 36), v("LST", ls + 24, ls + 36), Op.add)
        act(N("sn"), ind(v(PT), v("L2", 24 * t, 24 * t + 12)), v("NM"), Fn.Silu)
        ng = first("EG", t, rq, wf + 12, 7, "SO", opt["MG"] if t < STEPS - 1 else opt["ML"], RUN)
        mm(N("pt"), [(P(7, B, B + 12), v("ID"), v("WF", wf + 12, wf + 24)), (P(7, B, B + 12), v("JN"), ng)])
        tt(N("tl"), v("TL", 12 * t, 12 * t + 12), P(7, B, B + 12), v("IW"), Op.max)

    sums = []

    def floats(t):
        last = t == STEPS
        N = lambda s: "%s.%d" % (s, t)
        X, Y = ("U", "V") if t % 2 == 0 else ("V", "U")
        ex = B + W0 + B * (t // 2)
        ey = B + W0 + B * ((t + 1) // 2)
        xw = v("UB", 0, W0) if t == 0 else v(X, B, ex)
        xc = v("UB") if t == 0 else v(X, B, ex + B)
        yw = {0: v("VB"), 1: v("UB")}.get(t, v(Y, B, ey))
        of, py, h2 = 2 * B * t, 16 * B * (t % 2), B * (t % 2)
        al = v("LST", 48 * t, 48 * t + 12)
        runs = [(c, c + RUN) for c in range(B - RUN, -1, -RUN)]
        halves = [c + d for c, _ in runs for d in (0, RUN // 2)]
        for n, c in enumerate(halves):
            d = c + RUN // 2
            act(N("PY%d" % n), v("PY", py + 16 * c, py + 16 * d), ind(yw, v("OFFS", of + B + c, of + B + d)),
                scale=1.0 if last else 0.0625)
        scanned = t in opt["SCAN"]
        for n, (c, d) in enumerate(runs):
            a, b = 16 * c, 16 * d
            tt(N("PR%d" % n), v("PR", a, b), ind(xw, v("OFFS", of + c, of + d)), v("PY", py + a, py + b), Op.mult)
            if scanned and c == 0:
                scan(N("S%d" % n), v("SS"), v("RS2"), v("PR", a, b), 0.0, Op.mult, Op.add)
            else:
                lst = [(P(0 if c else 2, c, d), v("ID" if last else "ID16"), v("PR", a + k, b, 16)) for k in range(16)]
                j = mm(N("S%d" % n), lst[:8], stop=False, after=sums[-1:])
                sums[:] = [mm(N("Z%d" % n), lst[8:], start=False, after=[j])]
        bg = v("BG", h2, h2 + B)
        act(N("bg"), bg, ind(v("BSB") if t == 0 else v("BS", 0, A), al))
        z = v("ZC", h2, h2 + B)
        if t > 0:
            act(N("zt"), v("ZT"), v("ZL", B * (t - 1), B * t), Fn.Relu, scale=0.0625, bias=0.0625)
            act(N("z"), z, v("ZT"), bias=-0.0625)
        y, tmp = v("YS", B * t, B * t + B), P(1, B, 2 * B)
        if not last:
            wj, yj, dd, c = v("WJ", h2, h2 + B), v("YJ", h2, h2 + B), v("DD", B * t, B * t + B), v("CL", B * t, B * t + B)
            pw = v("PY", py, py + 16 * B)
            dma(N("cx"), "y", v(X, ex, ex + B), c)
            tt(N("dd"), dd, ind(xc, v("L2", 24 * t + 12, 24 * t + 24)), c, Op.subtract)
            send("c", t, [dd, c], v("CL", B * t + B, B * t + 2 * B), 1)
            tt(N("wj"), wj, ind(xw, v("LST", 48 * t + 36, 48 * t + 48)), z, Op.mult)
            act(N("yj"), yj, ind(pw, v("LKJ", 72 + 12 * t, 84 + 12 * t)), scale=16.0)
            tt(N("m2"), v("M2"), ind(pw, v("LKJ", 12 * t, 12 * t + 12)), dd, Op.mult)
        for n, (a, b) in enumerate(((RUN, B), (0, RUN))):
            s, zz = P(2 * n, a, b), sub(z, a, b)
            if n == 1 and scanned:
                s = v("SS", 15, 16 * RUN, 16)
                if not last:
                    act(N("zu"), v("ZU"), zz, scale=16.0)
                    zz = v("ZU")
            tt(N("t%d" % n), sub(tmp, a, b), s, zz, Op.mult)
            tt(N("y%d" % n), sub(y, a, b), sub(tmp, a, b), sub(bg, a, b), Op.add)
            if last:
                dma(N("oy%d" % n), "y", ext("ys", B * t + a, B * t + b), sub(y, a, b), out=True)
            elif n == 0:
                tt(N("e0"), sub(tmp, a, b), sub(y, a, b), P(1, a, b), Op.subtract)
                tt(N("m0"), v("M1", a, b), sub(tmp, a, b), sub(wj, a, b), Op.mult)
            else:
                e1 = P(1, 2 * B, 2 * B + RUN)
                tt(N("bt"), v("BT"), sub(bg, a, b), P(1, a, b), Op.subtract)
                tt(N("e1"), e1, sub(tmp, a, b), v("BT"), Op.add)
                tt(N("m1"), v("M1", a, b), e1, sub(wj, a, b), Op.mult)
        if last:
            return
        dma(N("oy"), "y", ext("ys", B * t, B * t + B), y, out=True)
        send("z", t, [y], v("ZL", B * t, B * t + B), 3, [v("ONE")])
        for n, (a, b) in enumerate(runs):
            tt(N("sy%d" % n), ind(v(Y, 0, ey), v("TL", 12 * t + a // 16, 12 * t + b // 16)), sub(yj, a, b), v("M1", a, b),
               Op.subtract)
        tt(N("sb"), ind(v("BS"), v("L2", 24 * t, 24 * t + 12)), bg, v("M2"), Op.add)
        if t == STEPS - 1:
            dma("ob", "y", ext("fb"), v("BS", 0, A), out=True)
            dma("oc", "y", ext("fc"), v("CL", 6 * B, 7 * B), out=True)

    ints(0)
    for t in range(STEPS + 1):
        if t < STEPS:
            ints(t + 1)
        floats(t)
    return ops


def overlap(x, y):
    if not (x[1] == y[1] and x[2] < y[3] and y[2] < x[3] and x[5][0] < y[5][1] and y[5][0] < x[5][1]):
        return False
    return x[5][2] == 1 or x[5][2] != y[5][2] or (x[5][0] - y[5][0]) % x[5][2] == 0


def depend(ops):
    hist = {}
    for o in ops:
        d = set(o["after"])
        for x in o["r"]:
            d.update(j for (j, y, w) in hist.get(x[1], ()) if w and overlap(x, y))
        for x in o["w"]:
            d.update(j for (j, y, w) in hist.get(x[1], ()) if overlap(x, y))
        d.discard(o["n"])
        o["d"] = d
        o["banks"] = sorted(set((x[1], b) for x in o["r"] + o["w"] if inps(x) for b in range(x[2] // 512, (x[3] - 1) // 512 + 1)))
        for x in o["r"]:
            hist.setdefault(x[1], []).append((o["n"], x, False))
        for x in o["w"]:
            hist.setdefault(x[1], []).append((o["n"], x, True))


def expand(ops, pro, loop, post):
    at = {o["nm"]: o["n"] for o in ops}
    names = pro.split()
    for p in range(STEPS + 3):
        for x in loop.split():
            nm, dt = x.split(":") if ":" in x else (x, "0")
            if "%s.%d" % (nm, p + int(dt)) not in post.split():
                names.append("%s.%d" % (nm, p + int(dt)))
    order, seen = [], set()

    def emit(j):
        if j not in seen:
            seen.add(j)
            for i in sorted(ops[j]["d"]):
                emit(i)
            order.append(j)

    for x in names + post.split() + [o["nm"] for o in ops]:
        if x in at:
            emit(at[x])
    return order


def schedule(opt=OPT, pro=PRO, loop=LOOP, post=POST):
    ops = build(opt)
    depend(ops)
    order = expand(ops, pro, loop, post)
    pos = {j: i for i, j in enumerate(order)}
    bank, lastg, cnt, nd = {}, [], {}, 0
    for j in order:
        o = ops[j]
        for b in o["banks"]:
            o["d"].update(i for e, i in bank.get(b, {}).items() if e != o["e"])
            bank.setdefault(b, {})[o["e"]] = j
        if o["e"] == "g" and o["k"] == "c":
            o["d"].update(lastg)
            lastg[:] = [j]
        if o["k"] == "c":
            s = "e" + o["e"]
            cnt[s] = cnt.get(s, 0) + 1
            o["sig"] = (s, cnt[s])
        elif o["k"] == "d":
            o["sig"] = ("d%d" % nd, 16)
            nd += 1
        elif o["k"] == "a":
            o["sig"] = (o["tag"], -1)
        elif o["k"] == "r":
            o["sig"] = ("l" + o["i"][0][2]["sem"], -2)
    known = {}
    for j in order:
        o = ops[j]
        if o["k"] == "a":
            o["clock"] = {}
            continue
        kn = known.setdefault(o["e"], {})
        o["waits"] = []
        for i in sorted(o["d"], key=lambda i: -pos[i]):
            s, c = ops[i]["sig"]
            if i in o.get("soft", ()) or (s in kn and kn[s] >= c):
                continue
            o["waits"].append((s, c))
            kn[s] = c
            for s2, c2 in ops[i]["clock"].items():
                if kn.get(s2, -3) < c2:
                    kn[s2] = c2
        o["clock"] = dict(kn)
    need = {}
    for j in order:
        for (s, c) in ops[j].get("waits", ()):
            if s[0] == "e":
                need.setdefault(s, set()).add(c)
    renum = {s: {c: i + 1 for i, c in enumerate(sorted(cs))} for s, cs in need.items()}
    for j in order:
        o = ops[j]
        if o["k"] == "a":
            continue
        o["waits"] = [(s, renum[s][c]) if s[0] == "e" else (s, c) for (s, c) in o["waits"]]
        if o["k"] == "c":
            s, c = o["sig"]
            o["inc"] = s if c in renum.get(s, {}) else None
    return ops, order


PLAN = []


def masks(topo, core, nxt, prv):
    a, b = topo.engines(core, nxt), topo.engines(core, prv)
    k = min(len(a), len(b), len(set(a) | set(b)) // 2)
    if len(a) <= len(b):
        ea = a[:k]
        eb = [e for e in reversed(b) if e not in ea][:k]
    else:
        eb = b[:k]
        ea = [e for e in reversed(a) if e not in eb][:k]
    return sum(1 << e for e in ea), sum(1 << e for e in eb), k


def rank_program(g, core, T, topo):
    rank = T.rank_of(core)
    if rank is None:
        return
    if not PLAN:
        PLAN.append(schedule())
    ops, order = PLAN[0]
    cores = list(T.cores)
    N = len(cores)
    nxt, prv = cores[(rank + 1) % N], cores[(rank - 1) % N]
    mn, mp, k = masks(topo, core, nxt, prv)
    arrive = masks(topo, prv, core, cores[(rank - 2) % N])[2] + masks(topo, nxt, cores[(rank + 2) % N], core)[2]
    idn, idp = [DstId(rid=topo.addr(c)[0], pnc=topo.addr(c)[1]) for c in (nxt, prv)]
    Q = {"v": g.vector, "s": g.scalar, "t": g.tensor, "g": g, "y": g.sync}

    def ap(x):
        if not isview(x):
            return x
        if x[0] == "i":
            return ap(x[1]).indirect(ap(x[2]))
        if x[0] == "x":
            return T[x[1]][:, x[2][0]:x[2][1]] if x[2] else T[x[1]][:]
        p = x[5]
        ps = slice(p[0], p[1]) if p[2] == 1 else slice(p[0], p[1], p[2])
        return T[x[1]][ps, x[2]:x[3]] if x[4] == 1 else T[x[1]][ps, x[2]:x[3]:x[4]]

    def half(x, h):
        return ap(v(x[1], x[2] + h * H, x[2] + h * H + H))

    def transfer(kw, h, to, mask):
        srcs = [half(x, h) for x in kw["s"]] + [ap(x) for x in kw["w"]]
        sem, dst = T.sem[kw["sem"]], half(kw["d"][0], h)
        if kw["alu"]:
            return RemoteDMATransfer(dst_ids=[to], dma_engine_mask=mask, remote_sem=sem, srcs=srcs, dsts=[dst], alu_op=kw["alu"])
        return RemoteDMATransfer(dst_ids=[to], dma_engine_mask=mask, remote_sem=sem, src=srcs[0], dst=dst)

    calls = {
        "matmul": lambda q: q.matmul, "activation": lambda q: q.activation, "dma_start": lambda q: q.dma_start,
        "tensor_tensor": lambda q: q.tensor_tensor, "tensor_scalar": lambda q: q.tensor_scalar,
        "tensor_copy": lambda q: q.tensor_copy, "memset": lambda q: q.memset, "iota": lambda q: q.iota,
        "tensor_tensor_scan": lambda q: q.tensor_tensor_scan, "affine_select": lambda q: q.affine_select,
        "tensor_reduce": lambda q: q.tensor_reduce,
    }
    sent, outs = [], 0
    for j in order:
        o = ops[j]
        if o["k"] == "a":
            continue
        q = Q[o["e"]]
        for (s, c) in o["waits"]:
            q.wait_ge(T.sem[s], {-1: arrive, -2: 2 * k}.get(c, c))
        if o["k"] == "r":
            kw = o["i"][0][2]
            g.remote_dma_fused([transfer(kw, 0, idn, mn), transfer(kw, 1, idp, mp)], local_sem=T.sem[o["sig"][0]])
            sent.append(o["sig"][0])
            continue
        for (m, a, kw) in o["i"]:
            ins = calls[m](q)(*[ap(x) for x in a], **{n: ap(x) for n, x in kw.items()})
        if o["k"] == "c":
            if o["inc"]:
                ins.then_inc(T.sem[o["inc"]], 1)
        elif o["k"] == "d":
            ins.then_inc(T.sem[o["sig"][0]], 16)
        else:
            ins.then_inc(T.sem.outs, 16)
            outs += 16
    for s in sent:
        g.wait_ge(T.sem[s], 2 * k)
    g.sync.wait_ge(T.sem.outs, outs)
